import numpy as np
import ml_dtypes


def mxq(x, axis, fmt="e4m3"):
    dtype, down = {"e4m3": (ml_dtypes.float8_e4m3fn, 7), "e5m2": (ml_dtypes.float8_e5m2, 14)}[fmt]
    v = np.moveaxis(np.asarray(x, np.float32).astype(ml_dtypes.bfloat16).astype(np.float64), axis, -1)
    blocks = v.reshape(v.shape[:-1] + (-1, 32))
    amax = np.abs(blocks).max(-1, keepdims=True)
    byte = np.maximum(np.where(amax > 0, np.frexp(amax)[1] - 1 + 127, 0) - down, 1)
    scale = np.exp2(byte - 127.0)
    codes = (blocks / scale).astype(np.float32).astype(dtype).astype(np.float64)
    return np.moveaxis((codes * scale).reshape(v.shape), -1, axis)


WIDE = False


def mx_kscale(k):
    if not WIDE:
        return np.ones(k)
    levels = np.array([10, -10, 5, -5, 0])
    if k % 512:
        return np.exp2(np.random.permutation(np.resize(levels, k // 32))).repeat(32)
    a = np.empty((k // 512, 16))
    for p in range(k // 512):
        a[p, :8] = np.random.permutation(np.resize(levels, 8))
        for g in range(8):
            far = levels[np.abs(levels - a[p, g]) >= 10]
            a[p, g + 8] = far[np.random.randint(len(far))]
    return np.exp2(a.ravel()).repeat(32)


BF16 = ml_dtypes.bfloat16


def bf(x):
    return np.asarray(x, np.float32).astype(BF16)


def f64(x):
    return np.asarray(x).astype(np.float64)


E2M1 = np.array([0.0, 0.5, 1.0, 1.5, 2.0, 3.0, 4.0, 6.0, -0.0, -0.5, -1.0, -1.5, -2.0, -3.0, -4.0, -6.0])


def pack_weight(w, fmt):
    k, n = w.shape
    w = f64(bf(w)).reshape(k // 32, 32, n)
    amax = np.abs(w).max(1)
    if fmt == "e4m3":
        byte = np.frexp(amax)[1] - 1 + 127 - 7
    else:
        mant, ex = np.frexp(amax / 6.0)
        byte = np.where(mant > 0.5, ex, ex - 1) + 127
    byte = np.clip(np.where(amax > 0, byte, 1), 1, 254)
    scaled = (w * np.exp2(127.0 - byte)[:, None, :]).reshape(k, n).astype(np.float32)
    by_word = np.ascontiguousarray(scaled.reshape(k // 512, 128, 4, n).transpose(0, 1, 3, 2))
    if fmt == "e4m3":
        words = by_word.astype(ml_dtypes.float8_e4m3fn).view(np.uint8)
    else:
        c = by_word.astype(ml_dtypes.float4_e2m1fn).view(np.uint8) & 0xF
        words = c[..., 0::2] | (c[..., 1::2] << 4)
    return np.ascontiguousarray(words), np.ascontiguousarray(byte.astype(np.uint8).reshape(k // 512, 16, n))


def unpack_weight(words, scales, fmt):
    g, p, n, _ = words.shape
    if fmt == "e4m3":
        vals = np.ascontiguousarray(words).view(ml_dtypes.float8_e4m3fn).astype(np.float64)
    else:
        nib = np.empty((g, p, n, 4), np.uint8)
        nib[..., 0::2] = words & 0xF
        nib[..., 1::2] = words >> 4
        vals = E2M1[nib]
    vals = vals * np.repeat(np.exp2(scales.astype(np.float64) - 127.0), 8, axis=1)[..., None]
    return vals.transpose(0, 1, 3, 2).reshape(g * 512, n)
def pack4(w):
    words, scales = pack_weight(w, "e2m1")
    return words.reshape(words.shape[0], 128, -1), scales


def unpack4(words, scales):
    return unpack_weight(words.reshape(words.shape[0], 128, -1, 2), scales, "e2m1")


T, D, A = 3072, 1024, 512
CLIP_LO, CLIP_HI = 0.8, 1.2


def draw0():
    s = mx_kscale(D)
    t = mx_kscale(T)
    h = np.random.standard_normal((T, D))
    h_words, h_scales = pack4(h / np.sqrt(T) / t[:, None])
    advantage = np.random.standard_normal(T)
    ratio = np.exp(0.3 * np.random.standard_normal(T))
    return {"x": bf(h * s),
            "w": bf(np.random.standard_normal((D, A)) / np.sqrt(D) / s[:, None]),
            "action": bf(np.random.random((T, A)) < 0.5),
            "weight": bf(advantage * np.clip(ratio, CLIP_LO, CLIP_HI) * t),
            "h_words": h_words,
            "h_scales": h_scales}


def core(x, w, action, weight, h_words, h_scales):
    z = mxq(f64(x), 1, "e4m3") @ mxq(f64(w), 0, "e4m3")
    prob = 1.0 / (1.0 + np.exp(-z))
    g = f64(weight)[:, None] * (prob - f64(action))
    hid = unpack4(h_words, h_scales)
    return hid.T @ mxq(g, 0, "e4m3")


def e4m3fn_bytes(y):
    return np.clip(np.asarray(y, np.float64), -448.0, 448.0).astype(np.float32).astype(ml_dtypes.float8_e4m3fn).view(np.uint8)


def e4m3fn_values(b):
    return np.asarray(b, np.uint8).view(ml_dtypes.float8_e4m3fn).astype(np.float64)


def setup_inputs():
    d = draw0()
    x0 = np.asarray(d['x']).astype(np.float64)
    s = (np.max(np.abs(x0), axis=(0,), keepdims=True) / 448.0).astype(np.float32)
    out = {}
    for k, v in d.items():
        if k == 'x':
            out['x_bytes'] = e4m3fn_bytes(x0 / s.astype(np.float64))
            out['x_scale'] = s
        else:
            out[k] = v
    return out


def reference(x_bytes, x_scale, w, action, weight, h_words, h_scales):
    return core(e4m3fn_values(x_bytes) * x_scale.astype(np.float64), w, action, weight, h_words, h_scales)

@@ -1,0 +1,346 @@
+from contextlib import ExitStack
+
+import concourse.mybir as mybir
+from concourse.masks import make_identity
+
+T, D, A = 3072, 1024, 512
+FLOPS = 2 * T * D * A * 2
+
+F32 = mybir.dt.float32
+BF16 = mybir.dt.bfloat16
+I32 = mybir.dt.int32
+U32 = mybir.dt.uint32
+U8 = mybir.dt.uint8
+FP8 = mybir.dt.float8_e4m3fn
+FP8X4 = mybir.dt.float8_e4m3fn_x4
+FP4X4 = mybir.dt.float4_e2m1fn_x4
+MULT = mybir.AluOpType.mult
+ADD = mybir.AluOpType.add
+SUB = mybir.AluOpType.subtract
+SIGMOID = mybir.ActivationFunctionType.Sigmoid
+
+P = 128
+K_PASS = 512
+GROUPS = T // K_PASS
+HALVES = 2 * GROUPS
+X_PASSES = D // K_PASS
+M_TILES = D // P
+EARLY = 4
+POOL_TILES = tuple((h, 0) for h in range(0, 12, 2))
+
+
+def tile_clipped_policy_head_grad_s13_kernel(
+    tc, x_bytes, x_scale, w, action, weight, h_words, h_scales, out
+):
+    nc = tc.nc
+    with ExitStack() as ctx:
+        keep = ctx.enter_context(tc.tile_pool(name="keep", bufs=1))
+        three = ctx.enter_context(tc.tile_pool(name="three", bufs=3))
+        four = ctx.enter_context(tc.tile_pool(name="four", bufs=4))
+        two = ctx.enter_context(tc.tile_pool(name="two", bufs=2))
+        psum_t = ctx.enter_context(tc.psum_pool(name="psum_t", bufs=2))
+        psum_z = ctx.enter_context(tc.psum_pool(name="psum_z", bufs=2))
+        psum_o = ctx.enter_context(tc.psum_pool(name="psum_o", bufs=1))
+        ctx.enter_context(tc.manual_schedule())
+
+        x_raw = [keep.tile([P, 4 * D], U8, align_bytes=64, name=f"x_raw{g}") for g in range(GROUPS)]
+        act = [keep.tile([P, 4, A], BF16, align_bytes=64, name=f"act{g}") for g in range(GROUPS)]
+        hw = [keep.tile([P, 2 * D], U8, align_bytes=64, name=f"hw{g}") for g in range(GROUPS)]
+        w_raw = [keep.tile([P, 4, A], BF16, align_bytes=64, name=f"w_raw{c}") for c in range(X_PASSES)]
+        w_int = [keep.tile([P, A, 4], BF16, align_bytes=64, name=f"w_int{c}") for c in range(X_PASSES)]
+        w_codes = [keep.tile([P, A], U32, align_bytes=64, name=f"w_codes{c}") for c in range(X_PASSES)]
+        w_scales = [keep.tile([P, A], U8, align_bytes=64, name=f"w_scales{c}") for c in range(X_PASSES)]
+        g_codes = [keep.tile([P, A], U32, align_bytes=64, name=f"g_codes{g}") for g in range(GROUPS)]
+        g_scales = [keep.tile([P, A], U8, align_bytes=64, name=f"g_scales{g}") for g in range(GROUPS)]
+        hs = keep.tile([P, GROUPS, D // 4], I32, align_bytes=64, name="hs")
+        xs = keep.tile([P, X_PASSES, 2, 2], F32, align_bytes=64, name="xs")
+        wt_raw = keep.tile([P, GROUPS, 4], BF16, align_bytes=64, name="wt_raw")
+        wt = keep.tile([P, GROUPS, 4], F32, align_bytes=64, name="wt")
+        ident = keep.tile([P, P], F32, align_bytes=64, name="ident")
+        warm = keep.tile([P, 1], F32, align_bytes=64, name="warm")
+
+        def load_x(g, lo, hi):
+            src = x_bytes[g * K_PASS : (g + 1) * K_PASS, :].rearrange("(p t) k -> p (t k)", t=4)
+            nc.sync.dma_start(out=x_raw[g][:, lo * D : hi * D], in_=src[:, lo * D : hi * D])
+
+        def load_w(c):
+            nc.sync.dma_start(
+                out=w_raw[c][:], in_=w[c * K_PASS : (c + 1) * K_PASS, :].rearrange("(p j) n -> p j n", j=4)
+            )
+
+        def load_act(g):
+            nc.sync.dma_start(
+                out=act[g][:], in_=action[g * K_PASS : (g + 1) * K_PASS, :].rearrange("(p t) a -> p t a", t=4)
+            )
+
+        def load_h(g):
+            nc.sync.dma_start(out=hw[g][:], in_=h_words[g])
+
+        nc.vector.memset(warm[:], 0.0)
+        nc.scalar.activation(out=warm[:], in_=warm[:], func=SIGMOID)
+        make_identity(nc, ident[:])
+        nc.gpsimd.memset(hs[:], 0)
+
+        load_x(0, 0, 2)
+        load_w(0)
+        nc.sync.dma_start(
+            out=xs[:].rearrange("p c u e -> p c (u e)"),
+            in_=x_scale.rearrange("o (c p t) -> p (o c) t", p=P, t=4),
+        )
+        load_w(1)
+        load_x(0, 2, 4)
+        nc.sync.dma_start(out=wt_raw[:], in_=weight.rearrange("(g p t) -> p g t", p=P, t=4))
+        load_x(1, 0, 4)
+        load_act(0)
+        load_x(2, 0, 4)
+        load_act(1)
+        scales_src = h_scales.bitcast(I32).rearrange("g (q r) n -> r q g n", r=4)
+        for r in range(4):
+            nc.sync.dma_start(out=hs[r:P:32, :, :], in_=scales_src[r])
+        load_h(0)
+        load_x(3, 0, 4)
+        load_act(2)
+        load_h(1)
+        for g in range(3, GROUPS):
+            if g + 1 < GROUPS:
+                load_x(g + 1, 0, 4)
+            load_act(g)
+            load_h(g - 1)
+        load_h(GROUPS - 1)
+
+        cast = {}
+        banks = {}
+        xg = {}
+        x_codes = {}
+        x_scales = {}
+        z = {}
+        sig = {}
+        aw = {}
+        gp = {}
+        gi = {}
+
+        def do_cast(h, split):
+            if h >= HALVES:
+                return
+            g, lo = h // 2, 2 * (h % 2)
+            cast[h] = three.tile([P, 2 * D], BF16, align_bytes=64, name="cast")
+            step = 2 // split
+            for i in range(split):
+                cols = slice(i * step * D, (i + 1) * step * D)
+                raw = slice((lo + i * step) * D, (lo + (i + 1) * step) * D)
+                nc.scalar.copy(out=cast[h][:, cols], in_=x_raw[g][:, raw].bitcast(FP8))
+
+        def do_transposes(h, c):
+            if h >= HALVES:
+                return
+            bank = psum_t.tile([P, 2, 2 * P], F32, name="bank")
+            banks[h, c] = bank
+            for i in range(2):
+                words = cast[h][:, i * D : (i + 1) * D].bitcast(F32)
+                for u in range(2):
+                    nc.tensor.transpose(
+                        bank[:, u, i * P : (i + 1) * P], words[:, 256 * c + u : 256 * (c + 1) : 2], ident[:]
+                    )
+
+        def do_scale(h, c):
+            if c == 0:
+                xg[h] = three.tile([P, X_PASSES, 2 * P, 2, 2], BF16, align_bytes=64, name="xg")
+            nc.vector.tensor_tensor(
+                out=xg[h][:, c],
+                in0=banks[h, c][:].bitcast(BF16).rearrange("p u (r e) -> p r u e", e=2),
+                in1=xs[:, c].unsqueeze(1).to_broadcast([P, 2 * P, 2, 2]),
+                op=MULT,
+            )
+
+        def do_quant_x(h):
+            x_codes[h] = four.tile([P, X_PASSES, 2 * P], U32, align_bytes=64, name="x_codes")
+            x_scales[h] = four.tile([P, X_PASSES, 2 * P], U8, align_bytes=64, name="x_scales")
+            nc.vector.quantize_mx(
+                out=x_codes[h][:].rearrange("p c r -> p (c r)").bitcast(FP8X4),
+                scales=x_scales[h][:].rearrange("p c r -> p (c r)"),
+                in_=xg[h][:].rearrange("p c r u e -> p (c r u e)"),
+            )
+
+        def do_z(h, i):
+            zt = psum_z.tile([P, A], F32, name="zt")
+            z[h, i] = zt
+            for c in range(X_PASSES):
+                nc.tensor.matmul_mx(
+                    out=zt[:],
+                    lhsT=x_codes[h][:, c, i * P : (i + 1) * P].bitcast(FP8X4),
+                    lhsT_scale=x_scales[h][:, c, i * P : (i + 1) * P],
+                    rhs=w_codes[c][:].bitcast(FP8X4),
+                    rhs_scale=w_scales[c][:],
+                    start=(c == 0),
+                    stop=(c == X_PASSES - 1),
+                )
+
+        def do_sigmoid(h, i):
+            if i == 0:
+                sig[h] = four.tile([P, 2, A], F32, align_bytes=64, name="sig")
+            nc.scalar.activation(out=sig[h][:, i, :], in_=z[h, i][:], func=SIGMOID)
+
+        def do_aw(h):
+            if h >= HALVES:
+                return
+            g = h // 2
+            aw[h] = three.tile([P, 2, A], F32, align_bytes=64, name="aw")
+            for i in range(2):
+                t = 2 * (h % 2) + i
+                if (h, i) in POOL_TILES:
+                    continue
+                nc.gpsimd.tensor_scalar(
+                    out=aw[h][:, i, :], in0=act[g][:, t, :], scalar1=wt[:, g, t : t + 1], scalar2=0.0,
+                    op0=MULT, op1=ADD,
+                )
+
+        def do_residual_pool(h):
+            for i in range(2):
+                if (h, i) in POOL_TILES:
+                    g, t = h // 2, 2 * (h % 2) + i
+                    if t == 0:
+                        gp[g] = two.tile([P, 4, A], BF16, align_bytes=64, name="gp")
+                    nc.gpsimd.tensor_tensor(out=aw[h][:, i, :], in0=sig[h][:, i, :], in1=act[g][:, t, :], op=SUB)
+                    nc.gpsimd.tensor_scalar(
+                        out=gp[g][:, t, :], in0=aw[h][:, i, :], scalar1=wt[:, g, t : t + 1], scalar2=1.0,
+                        op0=MULT, op1=MULT,
+                    )
+
+        def do_residual(h, i):
+            g, t = h // 2, 2 * (h % 2) + i
+            if (h, i) in POOL_TILES:
+                return
+            if t == 0:
+                gp[g] = two.tile([P, 4, A], BF16, align_bytes=64, name="gp")
+            nc.vector.scalar_tensor_tensor(
+                out=gp[g][:, t, :], in0=sig[h][:, i, :], scalar=wt[:, g, t : t + 1], in1=aw[h][:, i, :],
+                op0=MULT, op1=SUB,
+            )
+
+        def do_interleave(g, lo, hi, vector):
+            if lo == 0:
+                gi[g] = two.tile([P, A, 4], BF16, align_bytes=64, name="gi")
+            dst = gi[g][:, lo:hi, :]
+            src = gp[g][:, :, lo:hi].rearrange("p t a -> p a t")
+            if vector:
+                nc.vector.tensor_copy(out=dst, in_=src)
+            else:
+                nc.scalar.copy(out=dst, in_=src)
+
+        def do_quant_g(g, lo, hi):
+            nc.vector.quantize_mx(
+                out=g_codes[g][:, lo:hi].bitcast(FP8X4),
+                scales=g_scales[g][:, lo:hi],
+                in_=gi[g][:, lo:hi, :].rearrange("p a t -> p (a t)"),
+            )
+
+        def do_out(acc, m, g):
+            nc.tensor.matmul_mx(
+                out=acc[:],
+                lhsT=hw[g][:, 2 * P * m : 2 * P * (m + 1)].bitcast(FP4X4),
+                lhsT_scale=hs[:, g, 32 * m : 32 * (m + 1)].bitcast(U8),
+                rhs=g_codes[g][:].bitcast(FP8X4),
+                rhs_scale=g_scales[g][:],
+                start=(g == 0),
+                stop=(g == GROUPS - 1),
+            )
+
+        def do_w_interleave(c, vector):
+            if vector:
+                nc.vector.tensor_copy(out=w_int[c][:], in_=w_raw[c][:].rearrange("p j n -> p n j"))
+            else:
+                nc.scalar.copy(out=w_int[c][:], in_=w_raw[c][:].rearrange("p j n -> p n j"))
+
+        def do_quant_w(c):
+            nc.vector.quantize_mx(
+                out=w_codes[c][:].bitcast(FP8X4), scales=w_scales[c][:],
+                in_=w_int[c][:].rearrange("p n j -> p (n j)"),
+            )
+
+        accs = [psum_o.tile([P, A], F32, name=f"acc{m}") for m in range(EARLY)]
+
+        do_cast(0, 2)
+        do_cast(1, 1)
+        do_w_interleave(0, True)
+        do_transposes(0, 0)
+        do_transposes(0, 1)
+        do_w_interleave(1, False)
+
+        for h in range(HALVES):
+            if h >= 1:
+                for i in range(2):
+                    do_z(h - 1, i)
+                    do_sigmoid(h - 1, i)
+            if h % 2 == 0 and h >= 4:
+                do_interleave((h - 4) // 2, 0, A, False)
+            do_cast(h + 2, 1)
+            do_scale(h, 0)
+            if h == 0:
+                do_quant_w(0)
+            do_transposes(h + 1, 0)
+            if h >= 1:
+                do_aw(h - 1)
+            if h >= 2:
+                do_residual_pool(h - 2)
+            do_scale(h, 1)
+            if h == 0:
+                nc.vector.tensor_copy(out=wt[:], in_=wt_raw[:])
+            do_transposes(h + 1, 1)
+            if h % 2 == 1 and h >= 5:
+                do_quant_g((h - 5) // 2, 0, A)
+            if h >= 5:
+                g = (h - 5) // 2
+                for m in (range(2) if h % 2 == 1 else range(2, EARLY)):
+                    do_out(accs[m], m, g)
+            if h >= 2 and h < HALVES - 1:
+                for i in range(2):
+                    do_residual(h - 2, i)
+            if h == HALVES - 1:
+                do_residual(h - 2, 0)
+            do_quant_x(h)
+            if h == 0:
+                do_quant_w(1)
+
+        last = GROUPS - 1
+        for m in range(2, EARLY):
+            do_out(accs[m], m, last - 2)
+        accs.append(psum_t.tile([P, A], F32, name="bank"))
+        accs.append(psum_t.tile([P, A], F32, name="bank"))
+        do_aw(HALVES - 1)
+        for g in range(last - 1):
+            do_out(accs[EARLY], EARLY, g)
+        do_residual(HALVES - 3, 1)
+        do_residual_pool(HALVES - 2)
+        for i in range(2):
+            do_z(HALVES - 1, i)
+            do_sigmoid(HALVES - 1, i)
+        for i in range(2):
+            do_residual(HALVES - 2, i)
+        for g in range(last - 1):
+            do_out(accs[EARLY + 1], EARLY + 1, g)
+        accs.append(psum_z.tile([P, A], F32, name="zt"))
+        accs.append(psum_z.tile([P, A], F32, name="zt"))
+        for g in range(last - 1):
+            do_out(accs[EARLY + 2], EARLY + 2, g)
+        do_interleave(last - 1, 0, 256, False)
+        do_residual(HALVES - 1, 0)
+        do_interleave(last - 1, 256, A, True)
+        do_residual(HALVES - 1, 1)
+        do_quant_g(last - 1, 0, A)
+        do_interleave(last, 0, 256, True)
+        do_interleave(last, 256, A, False)
+        for m in range(EARLY + 3):
+            do_out(accs[m], m, last - 1)
+        do_quant_g(last, 0, 256)
+        do_quant_g(last, 256, A)
+        for m in range(M_TILES):
+            if m == EARLY + 3:
+                for g in range(last):
+                    do_out(accs[m], m, g)
+            do_out(accs[m], m, last)
+            res = keep.tile([P, A], F32, align_bytes=64, name=f"res{m}")
+            if m % 2 == 0:
+                nc.vector.tensor_copy(out=res[:], in_=accs[m][:])
+            else:
+                nc.scalar.copy(out=res[:], in_=accs[m][:])
+            nc.sync.dma_start(out=out[m * P : (m + 1) * P, :], in_=res[:])

@@ -25,8 +25,8 @@ GROUPS = T // K_PASS
 HALVES = 2 * GROUPS
 X_PASSES = D // K_PASS
 M_TILES = D // P
-EARLY = 4
-POOL_TILES = tuple((h, 0) for h in range(0, 12, 2))
+EARLY = 3
+A_HALF = A // 2
 
 
 def tile_clipped_policy_head_grad_s13_kernel(
@@ -35,15 +35,14 @@ def tile_clipped_policy_head_grad_s13_kernel(
     nc = tc.nc
     with ExitStack() as ctx:
         keep = ctx.enter_context(tc.tile_pool(name="keep", bufs=1))
-        three = ctx.enter_context(tc.tile_pool(name="three", bufs=3))
-        four = ctx.enter_context(tc.tile_pool(name="four", bufs=4))
         two = ctx.enter_context(tc.tile_pool(name="two", bufs=2))
+        three = ctx.enter_context(tc.tile_pool(name="three", bufs=3))
         psum_t = ctx.enter_context(tc.psum_pool(name="psum_t", bufs=2))
-        psum_z = ctx.enter_context(tc.psum_pool(name="psum_z", bufs=2))
+        psum_z = ctx.enter_context(tc.psum_pool(name="psum_z", bufs=3))
         psum_o = ctx.enter_context(tc.psum_pool(name="psum_o", bufs=1))
         ctx.enter_context(tc.manual_schedule())
 
-        x_raw = [keep.tile([P, 4 * D], U8, align_bytes=64, name=f"x_raw{g}") for g in range(GROUPS)]
+        x_raw = [keep.tile([P, 2 * D], U8, align_bytes=64, name=f"x_raw{h}") for h in range(HALVES)]
         act = [keep.tile([P, 4, A], BF16, align_bytes=64, name=f"act{g}") for g in range(GROUPS)]
         hw = [keep.tile([P, 2 * D], U8, align_bytes=64, name=f"hw{g}") for g in range(GROUPS)]
         w_raw = [keep.tile([P, 4, A], BF16, align_bytes=64, name=f"w_raw{c}") for c in range(X_PASSES)]
@@ -54,14 +53,14 @@ def tile_clipped_policy_head_grad_s13_kernel(
         g_scales = [keep.tile([P, A], U8, align_bytes=64, name=f"g_scales{g}") for g in range(GROUPS)]
         hs = keep.tile([P, GROUPS, D // 4], I32, align_bytes=64, name="hs")
         xs = keep.tile([P, X_PASSES, 2, 2], F32, align_bytes=64, name="xs")
-        wt_raw = keep.tile([P, GROUPS, 4], BF16, align_bytes=64, name="wt_raw")
-        wt = keep.tile([P, GROUPS, 4], F32, align_bytes=64, name="wt")
+        wt = keep.tile([P, GROUPS, 4], BF16, align_bytes=64, name="wt")
         ident = keep.tile([P, P], F32, align_bytes=64, name="ident")
-        warm = keep.tile([P, 1], F32, align_bytes=64, name="warm")
+        ident_bf = keep.tile([P, P], BF16, align_bytes=64, name="ident_bf")
 
-        def load_x(g, lo, hi):
+        def load_x(h):
+            g, lo = h // 2, 2 * (h % 2)
             src = x_bytes[g * K_PASS : (g + 1) * K_PASS, :].rearrange("(p t) k -> p (t k)", t=4)
-            nc.sync.dma_start(out=x_raw[g][:, lo * D : hi * D], in_=src[:, lo * D : hi * D])
+            nc.sync.dma_start(out=x_raw[h][:], in_=src[:, lo * D : (lo + 2) * D])
 
         def load_w(c):
             nc.sync.dma_start(
@@ -76,37 +75,36 @@ def tile_clipped_policy_head_grad_s13_kernel(
         def load_h(g):
             nc.sync.dma_start(out=hw[g][:], in_=h_words[g])
 
-        nc.vector.memset(warm[:], 0.0)
-        nc.scalar.activation(out=warm[:], in_=warm[:], func=SIGMOID)
         make_identity(nc, ident[:])
-        nc.gpsimd.memset(hs[:], 0)
+        make_identity(nc, ident_bf[:])
+        nc.vector.memset(hs[:], 0)
 
-        load_x(0, 0, 2)
+        load_x(0)
         load_w(0)
         nc.sync.dma_start(
             out=xs[:].rearrange("p c u e -> p c (u e)"),
             in_=x_scale.rearrange("o (c p t) -> p (o c) t", p=P, t=4),
         )
+        load_x(1)
         load_w(1)
-        load_x(0, 2, 4)
-        nc.sync.dma_start(out=wt_raw[:], in_=weight.rearrange("(g p t) -> p g t", p=P, t=4))
-        load_x(1, 0, 4)
+        nc.sync.dma_start(out=wt[:], in_=weight.rearrange("(g p t) -> p g t", p=P, t=4))
+        load_x(2)
         load_act(0)
-        load_x(2, 0, 4)
+        load_x(3)
+        load_x(4)
         load_act(1)
+        load_x(5)
         scales_src = h_scales.bitcast(I32).rearrange("g (q r) n -> r q g n", r=4)
         for r in range(4):
             nc.sync.dma_start(out=hs[r:P:32, :, :], in_=scales_src[r])
-        load_h(0)
-        load_x(3, 0, 4)
-        load_act(2)
-        load_h(1)
-        for g in range(3, GROUPS):
-            if g + 1 < GROUPS:
-                load_x(g + 1, 0, 4)
-            load_act(g)
-            load_h(g - 1)
-        load_h(GROUPS - 1)
+        for g in range(GROUPS):
+            if g + 3 < GROUPS:
+                load_x(2 * g + 6)
+            load_h(g)
+            if g + 2 < GROUPS:
+                load_act(g + 2)
+            if g + 3 < GROUPS:
+                load_x(2 * g + 7)
 
         cast = {}
         banks = {}
@@ -115,6 +113,7 @@ def tile_clipped_policy_head_grad_s13_kernel(
         x_scales = {}
         z = {}
         sig = {}
+        diag = {}
         aw = {}
         gp = {}
         gi = {}
@@ -122,13 +121,11 @@ def tile_clipped_policy_head_grad_s13_kernel(
         def do_cast(h, split):
             if h >= HALVES:
                 return
-            g, lo = h // 2, 2 * (h % 2)
             cast[h] = three.tile([P, 2 * D], BF16, align_bytes=64, name="cast")
-            step = 2 // split
+            step = 2 * D // split
             for i in range(split):
-                cols = slice(i * step * D, (i + 1) * step * D)
-                raw = slice((lo + i * step) * D, (lo + (i + 1) * step) * D)
-                nc.scalar.copy(out=cast[h][:, cols], in_=x_raw[g][:, raw].bitcast(FP8))
+                cols = slice(i * step, (i + 1) * step)
+                nc.scalar.copy(out=cast[h][:, cols], in_=x_raw[h][:, cols].bitcast(FP8))
 
         def do_transposes(h, c):
             if h >= HALVES:
@@ -144,7 +141,7 @@ def tile_clipped_policy_head_grad_s13_kernel(
 
         def do_scale(h, c):
             if c == 0:
-                xg[h] = three.tile([P, X_PASSES, 2 * P, 2, 2], BF16, align_bytes=64, name="xg")
+                xg[h] = two.tile([P, X_PASSES, 2 * P, 2, 2], BF16, align_bytes=64, name="xg")
             nc.vector.tensor_tensor(
                 out=xg[h][:, c],
                 in0=banks[h, c][:].bitcast(BF16).rearrange("p u (r e) -> p r u e", e=2),
@@ -153,8 +150,8 @@ def tile_clipped_policy_head_grad_s13_kernel(
             )
 
         def do_quant_x(h):
-            x_codes[h] = four.tile([P, X_PASSES, 2 * P], U32, align_bytes=64, name="x_codes")
-            x_scales[h] = four.tile([P, X_PASSES, 2 * P], U8, align_bytes=64, name="x_scales")
+            x_codes[h] = two.tile([P, X_PASSES, 2 * P], U32, align_bytes=64, name="x_codes")
+            x_scales[h] = two.tile([P, X_PASSES, 2 * P], U8, align_bytes=64, name="x_scales")
             nc.vector.quantize_mx(
                 out=x_codes[h][:].rearrange("p c r -> p (c r)").bitcast(FP8X4),
                 scales=x_scales[h][:].rearrange("p c r -> p (c r)"),
@@ -176,62 +173,47 @@ def tile_clipped_policy_head_grad_s13_kernel(
                 )
 
         def do_sigmoid(h, i):
-            if i == 0:
-                sig[h] = four.tile([P, 2, A], F32, align_bytes=64, name="sig")
-            nc.scalar.activation(out=sig[h][:, i, :], in_=z[h, i][:], func=SIGMOID)
+            sig[h, i] = three.tile([P, A], F32, align_bytes=64, name="sig")
+            nc.scalar.activation(out=sig[h, i][:], in_=z[h, i][:], func=SIGMOID)
 
-        def do_aw(h):
-            if h >= HALVES:
+        def do_diag(g):
+            if g >= GROUPS:
                 return
-            g = h // 2
-            aw[h] = three.tile([P, 2, A], F32, align_bytes=64, name="aw")
-            for i in range(2):
-                t = 2 * (h % 2) + i
-                if (h, i) in POOL_TILES:
-                    continue
+            diag[g] = two.tile([P, 4, P], BF16, align_bytes=64, name="diag")
+            for t in range(4):
                 nc.gpsimd.tensor_scalar(
-                    out=aw[h][:, i, :], in0=act[g][:, t, :], scalar1=wt[:, g, t : t + 1], scalar2=0.0,
+                    out=diag[g][:, t, :], in0=ident_bf[:], scalar1=wt[:, g, t : t + 1], scalar2=0.0,
                     op0=MULT, op1=ADD,
                 )
 
-        def do_residual_pool(h):
-            for i in range(2):
-                if (h, i) in POOL_TILES:
-                    g, t = h // 2, 2 * (h % 2) + i
-                    if t == 0:
-                        gp[g] = two.tile([P, 4, A], BF16, align_bytes=64, name="gp")
-                    nc.gpsimd.tensor_tensor(out=aw[h][:, i, :], in0=sig[h][:, i, :], in1=act[g][:, t, :], op=SUB)
-                    nc.gpsimd.tensor_scalar(
-                        out=gp[g][:, t, :], in0=aw[h][:, i, :], scalar1=wt[:, g, t : t + 1], scalar2=1.0,
-                        op0=MULT, op1=MULT,
-                    )
+        def do_aw(h, i):
+            g, t = h // 2, 2 * (h % 2) + i
+            aw[h, i] = psum_z.tile([P, A], F32, name="zt")
+            nc.tensor.matmul(aw[h, i][:], lhsT=diag[g][:, t, :], rhs=act[g][:, t, :], start=True, stop=True)
 
         def do_residual(h, i):
             g, t = h // 2, 2 * (h % 2) + i
-            if (h, i) in POOL_TILES:
-                return
             if t == 0:
                 gp[g] = two.tile([P, 4, A], BF16, align_bytes=64, name="gp")
             nc.vector.scalar_tensor_tensor(
-                out=gp[g][:, t, :], in0=sig[h][:, i, :], scalar=wt[:, g, t : t + 1], in1=aw[h][:, i, :],
+                out=gp[g][:, t, :], in0=sig[h, i][:], scalar=wt[:, g, t : t + 1], in1=aw[h, i][:],
                 op0=MULT, op1=SUB,
             )
 
-        def do_interleave(g, lo, hi, vector):
-            if lo == 0:
-                gi[g] = two.tile([P, A, 4], BF16, align_bytes=64, name="gi")
-            dst = gi[g][:, lo:hi, :]
-            src = gp[g][:, :, lo:hi].rearrange("p t a -> p a t")
+        def do_interleave(g, half, vector):
+            gi[g, half] = three.tile([P, A_HALF, 4], BF16, align_bytes=64, name="gi")
+            src = gp[g][:, :, half * A_HALF : (half + 1) * A_HALF].rearrange("p t a -> p a t")
             if vector:
-                nc.vector.tensor_copy(out=dst, in_=src)
+                nc.vector.tensor_copy(out=gi[g, half][:], in_=src)
             else:
-                nc.scalar.copy(out=dst, in_=src)
+                nc.scalar.copy(out=gi[g, half][:], in_=src)
 
-        def do_quant_g(g, lo, hi):
+        def do_quant_g(g, half):
+            cols = slice(half * A_HALF, (half + 1) * A_HALF)
             nc.vector.quantize_mx(
-                out=g_codes[g][:, lo:hi].bitcast(FP8X4),
-                scales=g_scales[g][:, lo:hi],
-                in_=gi[g][:, lo:hi, :].rearrange("p a t -> p (a t)"),
+                out=g_codes[g][:, cols].bitcast(FP8X4),
+                scales=g_scales[g][:, cols],
+                in_=gi[g, half][:].rearrange("p a t -> p (a t)"),
             )
 
         def do_out(acc, m, g):
@@ -265,76 +247,67 @@ def tile_clipped_policy_head_grad_s13_kernel(
         do_transposes(0, 0)
         do_transposes(0, 1)
         do_w_interleave(1, False)
+        do_diag(0)
 
         for h in range(HALVES):
             if h >= 1:
                 for i in range(2):
                     do_z(h - 1, i)
                     do_sigmoid(h - 1, i)
-            if h % 2 == 0 and h >= 4:
-                do_interleave((h - 4) // 2, 0, A, False)
-            do_cast(h + 2, 1)
-            do_scale(h, 0)
-            if h == 0:
-                do_quant_w(0)
-            do_transposes(h + 1, 0)
-            if h >= 1:
-                do_aw(h - 1)
-            if h >= 2:
-                do_residual_pool(h - 2)
-            do_scale(h, 1)
-            if h == 0:
-                nc.vector.tensor_copy(out=wt[:], in_=wt_raw[:])
-            do_transposes(h + 1, 1)
-            if h % 2 == 1 and h >= 5:
-                do_quant_g((h - 5) // 2, 0, A)
+                for i in range(2):
+                    do_aw(h - 1, i)
             if h >= 5:
                 g = (h - 5) // 2
                 for m in (range(2) if h % 2 == 1 else range(2, EARLY)):
                     do_out(accs[m], m, g)
-            if h >= 2 and h < HALVES - 1:
-                for i in range(2):
-                    do_residual(h - 2, i)
-            if h == HALVES - 1:
-                do_residual(h - 2, 0)
+            do_cast(h + 2, 1)
+            if h >= 3:
+                do_interleave((h - 3) // 2, (h - 3) % 2, False)
+            if h % 2 == 1:
+                do_diag((h + 1) // 2)
+            for c in range(X_PASSES):
+                do_scale(h, c)
+                do_transposes(h + 1, c)
+            if h == 0:
+                do_quant_w(0)
+            else:
+                do_residual(h - 1, 0)
             do_quant_x(h)
             if h == 0:
                 do_quant_w(1)
+            else:
+                do_residual(h - 1, 1)
+            if h >= 3:
+                do_quant_g((h - 3) // 2, (h - 3) % 2)
 
         last = GROUPS - 1
-        for m in range(2, EARLY):
-            do_out(accs[m], m, last - 2)
-        accs.append(psum_t.tile([P, A], F32, name="bank"))
-        accs.append(psum_t.tile([P, A], F32, name="bank"))
-        do_aw(HALVES - 1)
-        for g in range(last - 1):
-            do_out(accs[EARLY], EARLY, g)
-        do_residual(HALVES - 3, 1)
-        do_residual_pool(HALVES - 2)
+        do_interleave(last - 1, 1, False)
         for i in range(2):
             do_z(HALVES - 1, i)
             do_sigmoid(HALVES - 1, i)
         for i in range(2):
-            do_residual(HALVES - 2, i)
-        for g in range(last - 1):
-            do_out(accs[EARLY + 1], EARLY + 1, g)
-        accs.append(psum_z.tile([P, A], F32, name="zt"))
-        accs.append(psum_z.tile([P, A], F32, name="zt"))
-        for g in range(last - 1):
-            do_out(accs[EARLY + 2], EARLY + 2, g)
-        do_interleave(last - 1, 0, 256, False)
-        do_residual(HALVES - 1, 0)
-        do_interleave(last - 1, 256, A, True)
-        do_residual(HALVES - 1, 1)
-        do_quant_g(last - 1, 0, A)
-        do_interleave(last, 0, 256, True)
-        do_interleave(last, 256, A, False)
-        for m in range(EARLY + 3):
+            do_aw(HALVES - 1, i)
+        do_quant_g(last - 1, 1)
+        for m in range(2, EARLY):
+            do_out(accs[m], m, last - 2)
+        for m in range(EARLY, EARLY + 2):
+            accs.append(psum_t.tile([P, A], F32, name="bank"))
+            for g in range(last - 1):
+                do_out(accs[m], m, g)
+        for i in range(2):
+            do_residual(HALVES - 1, i)
+        for m in range(EARLY + 2):
             do_out(accs[m], m, last - 1)
-        do_quant_g(last, 0, 256)
-        do_quant_g(last, 256, A)
+        do_interleave(last, 0, False)
+        do_interleave(last, 1, True)
+        do_quant_g(last, 1)
+        do_quant_g(last, 0)
+        for m in range(EARLY + 2, M_TILES):
+            accs.append(psum_z.tile([P, A], F32, name="zt"))
+        for g in range(last):
+            do_out(accs[EARLY + 2], EARLY + 2, g)
         for m in range(M_TILES):
-            if m == EARLY + 3:
+            if m > EARLY + 2:
                 for g in range(last):
                     do_out(accs[m], m, g)
             do_out(accs[m], m, last)

@@ -18,6 +18,7 @@ MULT = mybir.AluOpType.mult
 ADD = mybir.AluOpType.add
 SUB = mybir.AluOpType.subtract
 SIGMOID = mybir.ActivationFunctionType.Sigmoid
+COPY = mybir.ActivationFunctionType.Copy
 
 P = 128
 K_PASS = 512
@@ -25,8 +26,11 @@ GROUPS = T // K_PASS
 HALVES = 2 * GROUPS
 X_PASSES = D // K_PASS
 M_TILES = D // P
-EARLY = 3
+EARLY = 4
 A_HALF = A // 2
+W_POOL = 384
+VECTOR_CASTS = 3
+TAIL_SCALAR = 176
 
 
 def tile_clipped_policy_head_grad_s13_kernel(
@@ -35,10 +39,12 @@ def tile_clipped_policy_head_grad_s13_kernel(
     nc = tc.nc
     with ExitStack() as ctx:
         keep = ctx.enter_context(tc.tile_pool(name="keep", bufs=1))
+        one = ctx.enter_context(tc.tile_pool(name="one", bufs=1))
         two = ctx.enter_context(tc.tile_pool(name="two", bufs=2))
         three = ctx.enter_context(tc.tile_pool(name="three", bufs=3))
+        four = ctx.enter_context(tc.tile_pool(name="four", bufs=4))
         psum_t = ctx.enter_context(tc.psum_pool(name="psum_t", bufs=2))
-        psum_z = ctx.enter_context(tc.psum_pool(name="psum_z", bufs=3))
+        psum_z = ctx.enter_context(tc.psum_pool(name="psum_z", bufs=2))
         psum_o = ctx.enter_context(tc.psum_pool(name="psum_o", bufs=1))
         ctx.enter_context(tc.manual_schedule())
 
@@ -53,7 +59,8 @@ def tile_clipped_policy_head_grad_s13_kernel(
         g_scales = [keep.tile([P, A], U8, align_bytes=64, name=f"g_scales{g}") for g in range(GROUPS)]
         hs = keep.tile([P, GROUPS, D // 4], I32, align_bytes=64, name="hs")
         xs = keep.tile([P, X_PASSES, 2, 2], F32, align_bytes=64, name="xs")
-        wt = keep.tile([P, GROUPS, 4], BF16, align_bytes=64, name="wt")
+        wt_raw = keep.tile([P, GROUPS, 4], BF16, align_bytes=64, name="wt_raw")
+        wt = keep.tile([P, GROUPS, 4], F32, align_bytes=64, name="wt")
         ident = keep.tile([P, P], F32, align_bytes=64, name="ident")
         ident_bf = keep.tile([P, P], BF16, align_bytes=64, name="ident_bf")
 
@@ -80,20 +87,20 @@ def tile_clipped_policy_head_grad_s13_kernel(
         nc.vector.memset(hs[:], 0)
 
         load_x(0)
-        load_w(0)
+        load_x(1)
         nc.sync.dma_start(
             out=xs[:].rearrange("p c u e -> p c (u e)"),
             in_=x_scale.rearrange("o (c p t) -> p (o c) t", p=P, t=4),
         )
-        load_x(1)
         load_w(1)
-        nc.sync.dma_start(out=wt[:], in_=weight.rearrange("(g p t) -> p g t", p=P, t=4))
+        load_w(0)
         load_x(2)
-        load_act(0)
+        nc.sync.dma_start(out=wt_raw[:], in_=weight.rearrange("(g p t) -> p g t", p=P, t=4))
         load_x(3)
+        load_act(0)
         load_x(4)
-        load_act(1)
         load_x(5)
+        load_act(1)
         scales_src = h_scales.bitcast(I32).rearrange("g (q r) n -> r q g n", r=4)
         for r in range(4):
             nc.sync.dma_start(out=hs[r:P:32, :, :], in_=scales_src[r])
@@ -117,15 +124,22 @@ def tile_clipped_policy_head_grad_s13_kernel(
         aw = {}
         gp = {}
         gi = {}
+        diff = {}
 
-        def do_cast(h, split):
+        def do_cast(h):
             if h >= HALVES:
                 return
             cast[h] = three.tile([P, 2 * D], BF16, align_bytes=64, name="cast")
-            step = 2 * D // split
-            for i in range(split):
-                cols = slice(i * step, (i + 1) * step)
-                nc.scalar.copy(out=cast[h][:, cols], in_=x_raw[h][:, cols].bitcast(FP8))
+            if h == 0:
+                for c in range(X_PASSES):
+                    lo = slice(c * K_PASS, (c + 1) * K_PASS)
+                    hi = slice(D + c * K_PASS, D + (c + 1) * K_PASS)
+                    nc.vector.tensor_copy(out=cast[h][:, lo], in_=x_raw[h][:, lo].bitcast(FP8))
+                    nc.scalar.copy(out=cast[h][:, hi], in_=x_raw[h][:, hi].bitcast(FP8))
+            elif h < VECTOR_CASTS:
+                nc.vector.tensor_copy(out=cast[h][:], in_=x_raw[h][:].bitcast(FP8))
+            else:
+                nc.scalar.copy(out=cast[h][:], in_=x_raw[h][:].bitcast(FP8))
 
         def do_transposes(h, c):
             if h >= HALVES:
@@ -150,8 +164,8 @@ def tile_clipped_policy_head_grad_s13_kernel(
             )
 
         def do_quant_x(h):
-            x_codes[h] = two.tile([P, X_PASSES, 2 * P], U32, align_bytes=64, name="x_codes")
-            x_scales[h] = two.tile([P, X_PASSES, 2 * P], U8, align_bytes=64, name="x_scales")
+            x_codes[h] = three.tile([P, X_PASSES, 2 * P], U32, align_bytes=64, name="x_codes")
+            x_scales[h] = three.tile([P, X_PASSES, 2 * P], U8, align_bytes=64, name="x_scales")
             nc.vector.quantize_mx(
                 out=x_codes[h][:].rearrange("p c r -> p (c r)").bitcast(FP8X4),
                 scales=x_scales[h][:].rearrange("p c r -> p (c r)"),
@@ -173,21 +187,25 @@ def tile_clipped_policy_head_grad_s13_kernel(
                 )
 
         def do_sigmoid(h, i):
-            sig[h, i] = three.tile([P, A], F32, align_bytes=64, name="sig")
+            sig[h, i] = four.tile([P, A], F32, align_bytes=64, name="sig")
             nc.scalar.activation(out=sig[h, i][:], in_=z[h, i][:], func=SIGMOID)
+
+        def do_logits(h, tiles):
+            for i in tiles:
+                do_z(h, i)
+                do_sigmoid(h, i)
 
         def do_diag(g):
             if g >= GROUPS:
                 return
             diag[g] = two.tile([P, 4, P], BF16, align_bytes=64, name="diag")
-            for t in range(4):
-                nc.gpsimd.tensor_scalar(
-                    out=diag[g][:, t, :], in0=ident_bf[:], scalar1=wt[:, g, t : t + 1], scalar2=0.0,
-                    op0=MULT, op1=ADD,
-                )
+            for t in range(1, 4):
+                nc.scalar.activation(out=diag[g][:, t, :], in_=ident_bf[:], func=COPY, scale=wt[:, g, t : t + 1])
 
         def do_aw(h, i):
             g, t = h // 2, 2 * (h % 2) + i
+            if t == 0:
+                return
             aw[h, i] = psum_z.tile([P, A], F32, name="zt")
             nc.tensor.matmul(aw[h, i][:], lhsT=diag[g][:, t, :], rhs=act[g][:, t, :], start=True, stop=True)
 
@@ -195,18 +213,50 @@ def tile_clipped_policy_head_grad_s13_kernel(
             g, t = h // 2, 2 * (h % 2) + i
             if t == 0:
                 gp[g] = two.tile([P, 4, A], BF16, align_bytes=64, name="gp")
+                return
             nc.vector.scalar_tensor_tensor(
                 out=gp[g][:, t, :], in0=sig[h, i][:], scalar=wt[:, g, t : t + 1], in1=aw[h, i][:],
                 op0=MULT, op1=SUB,
             )
 
-        def do_interleave(g, half, vector):
-            gi[g, half] = three.tile([P, A_HALF, 4], BF16, align_bytes=64, name="gi")
-            src = gp[g][:, :, half * A_HALF : (half + 1) * A_HALF].rearrange("p t a -> p a t")
-            if vector:
-                nc.vector.tensor_copy(out=gi[g, half][:], in_=src)
+        def do_pool_sub(g, half):
+            if half == 0:
+                diff[g] = one.tile([P, A], F32, align_bytes=64, name="diff")
+            cols = slice(half * A_HALF, (half + 1) * A_HALF)
+            nc.gpsimd.tensor_tensor(out=diff[g][:, cols], in0=sig[2 * g, 0][:, cols], in1=act[g][:, 0, cols], op=SUB)
+
+        def do_vector_sub(h, i):
+            g, t = h // 2, 2 * (h % 2) + i
+            diff[h, i] = four.tile([P, A], F32, align_bytes=64, name="vdiff")
+            nc.vector.tensor_tensor(out=diff[h, i][:], in0=sig[h, i][:], in1=act[g][:, t, :], op=SUB)
+
+        def do_scalar_mul(h, i):
+            g, t = h // 2, 2 * (h % 2) + i
+            nc.scalar.activation(out=gp[g][:, t, :], in_=diff[h, i][:], func=COPY, scale=wt[:, g, t : t + 1])
+
+        def do_vector_mul(h, i):
+            g, t = h // 2, 2 * (h % 2) + i
+            nc.vector.tensor_scalar(
+                out=gp[g][:, t, :], in0=diff[h, i][:], scalar1=wt[:, g, t : t + 1], scalar2=None, op0=MULT
+            )
+
+        def do_pool_mul(g):
+            nc.gpsimd.tensor_scalar(
+                out=gp[g][:, 0, :], in0=diff[g][:], scalar1=wt[:, g, 0:1], scalar2=0.0, op0=MULT, op1=ADD
+            )
+
+        def interleave(engine, dst, src):
+            if engine == "vector":
+                nc.vector.tensor_copy(out=dst, in_=src)
+            elif engine == "scalar":
+                nc.scalar.copy(out=dst, in_=src)
             else:
-                nc.scalar.copy(out=gi[g, half][:], in_=src)
+                nc.gpsimd.tensor_scalar(out=dst, in0=src, scalar1=1.0, scalar2=0.0, op0=MULT, op1=ADD)
+
+        def do_interleave(g, half, engine, name="gi"):
+            gi[g, half] = one.tile([P, A_HALF, 4], BF16, align_bytes=64, name=name)
+            src = gp[g][:, :, half * A_HALF : (half + 1) * A_HALF].rearrange("p t a -> p a t")
+            interleave(engine, gi[g, half][:], src)
 
         def do_quant_g(g, half):
             cols = slice(half * A_HALF, (half + 1) * A_HALF)
@@ -227,11 +277,8 @@ def tile_clipped_policy_head_grad_s13_kernel(
                 stop=(g == GROUPS - 1),
             )
 
-        def do_w_interleave(c, vector):
-            if vector:
-                nc.vector.tensor_copy(out=w_int[c][:], in_=w_raw[c][:].rearrange("p j n -> p n j"))
-            else:
-                nc.scalar.copy(out=w_int[c][:], in_=w_raw[c][:].rearrange("p j n -> p n j"))
+        def do_w_interleave(c, engine, lo, hi):
+            interleave(engine, w_int[c][:, lo:hi, :], w_raw[c][:, :, lo:hi].rearrange("p j n -> p n j"))
 
         def do_quant_w(c):
             nc.vector.quantize_mx(
@@ -241,75 +288,92 @@ def tile_clipped_policy_head_grad_s13_kernel(
 
         accs = [psum_o.tile([P, A], F32, name=f"acc{m}") for m in range(EARLY)]
 
-        do_cast(0, 2)
-        do_cast(1, 1)
-        do_w_interleave(0, True)
+        do_cast(0)
+        do_cast(1)
         do_transposes(0, 0)
         do_transposes(0, 1)
-        do_w_interleave(1, False)
-        do_diag(0)
+        do_w_interleave(1, "gpsimd", 0, W_POOL)
+        do_w_interleave(1, "scalar", W_POOL, A)
+        do_w_interleave(0, "scalar", 0, A)
 
         for h in range(HALVES):
+            if h >= 6:
+                for m in range(2 * (h % 2), 2 * (h % 2) + 2):
+                    do_out(accs[m], m, (h - 6) // 2)
+            if h >= 2:
+                for i in range(2):
+                    do_aw(h - 2, i)
             if h >= 1:
-                for i in range(2):
-                    do_z(h - 1, i)
-                    do_sigmoid(h - 1, i)
-                for i in range(2):
-                    do_aw(h - 1, i)
-            if h >= 5:
-                g = (h - 5) // 2
-                for m in (range(2) if h % 2 == 1 else range(2, EARLY)):
-                    do_out(accs[m], m, g)
-            do_cast(h + 2, 1)
-            if h >= 3:
-                do_interleave((h - 3) // 2, (h - 3) % 2, False)
-            if h % 2 == 1:
-                do_diag((h + 1) // 2)
+                do_cast(h + 2)
+            if h % 2 == 1 and h < HALVES - 1:
+                do_diag(h // 2)
+            if h == 1:
+                do_logits(0, (0, 1))
+            if h == 2:
+                do_logits(1, (0,))
+            if h >= 4:
+                do_interleave((h - 4) // 2, h % 2, "gpsimd")
+            if h >= 2:
+                do_pool_sub(h // 2 - 1, h % 2)
             for c in range(X_PASSES):
                 do_scale(h, c)
                 do_transposes(h + 1, c)
+            if h >= 2:
+                for i in range(2):
+                    do_residual(h - 2, i)
+            if h % 2 == 1 and h >= 3:
+                do_pool_mul(h // 2 - 1)
             if h == 0:
-                do_quant_w(0)
-            else:
-                do_residual(h - 1, 0)
+                nc.vector.tensor_copy(out=wt[:], in_=wt_raw[:])
+            if h == HALVES - 1:
+                accs.append(psum_t.tile([P, A], F32, name="bank"))
+                for g in range(GROUPS - 3):
+                    do_out(accs[EARLY], EARLY, g)
+            if h == 2:
+                do_logits(1, (1,))
+            if h >= 3:
+                do_logits(h - 1, (0, 1))
             do_quant_x(h)
             if h == 0:
                 do_quant_w(1)
-            else:
-                do_residual(h - 1, 1)
-            if h >= 3:
-                do_quant_g((h - 3) // 2, (h - 3) % 2)
+                do_quant_w(0)
+                do_cast(2)
+            if h >= 4:
+                do_quant_g((h - 4) // 2, h % 2)
 
         last = GROUPS - 1
-        do_interleave(last - 1, 1, False)
-        for i in range(2):
-            do_z(HALVES - 1, i)
-            do_sigmoid(HALVES - 1, i)
-        for i in range(2):
-            do_aw(HALVES - 1, i)
+        gp[last] = two.tile([P, 4, A], BF16, align_bytes=64, name="gp")
+        accs.append(psum_t.tile([P, A], F32, name="bank"))
+        for g in range(last - 2):
+            do_out(accs[EARLY + 1], EARLY + 1, g)
+        do_interleave(last - 1, 0, "vector", "gi_a")
+        do_interleave(last - 1, 1, "scalar", "gi_b")
+        do_logits(HALVES - 1, (0, 1))
+        do_vector_sub(HALVES - 2, 0)
+        do_quant_g(last - 1, 0)
+        do_vector_sub(HALVES - 2, 1)
         do_quant_g(last - 1, 1)
-        for m in range(2, EARLY):
-            do_out(accs[m], m, last - 2)
-        for m in range(EARLY, EARLY + 2):
-            accs.append(psum_t.tile([P, A], F32, name="bank"))
-            for g in range(last - 1):
-                do_out(accs[m], m, g)
         for i in range(2):
-            do_residual(HALVES - 1, i)
+            do_scalar_mul(HALVES - 2, i)
+        for i in range(2):
+            do_vector_sub(HALVES - 1, i)
+        for i in range(2):
+            do_vector_mul(HALVES - 1, i)
         for m in range(EARLY + 2):
-            do_out(accs[m], m, last - 1)
-        do_interleave(last, 0, False)
-        do_interleave(last, 1, True)
-        do_quant_g(last, 1)
-        do_quant_g(last, 0)
+            do_out(accs[m], m, last - 2)
         for m in range(EARLY + 2, M_TILES):
             accs.append(psum_z.tile([P, A], F32, name="zt"))
-        for g in range(last):
-            do_out(accs[EARLY + 2], EARLY + 2, g)
+            for g in range(last - 1):
+                do_out(accs[m], m, g)
+        gi[last] = one.tile([P, A, 4], BF16, align_bytes=64, name="gi_last")
+        for engine, lo, hi in (("scalar", 0, TAIL_SCALAR), ("vector", TAIL_SCALAR, A)):
+            interleave(engine, gi[last][:, lo:hi, :], gp[last][:, :, lo:hi].rearrange("p t a -> p a t"))
+        nc.vector.quantize_mx(
+            out=g_codes[last][:].bitcast(FP8X4), scales=g_scales[last][:],
+            in_=gi[last][:].rearrange("p a t -> p (a t)"),
+        )
         for m in range(M_TILES):
-            if m > EARLY + 2:
-                for g in range(last):
-                    do_out(accs[m], m, g)
+            do_out(accs[m], m, last - 1)
             do_out(accs[m], m, last)
             res = keep.tile([P, A], F32, align_bytes=64, name=f"res{m}")
             if m % 2 == 0:

@@ -59,6 +59,7 @@ def tile_clipped_policy_head_grad_s13_kernel(
         g_scales = [keep.tile([P, A], U8, align_bytes=64, name=f"g_scales{g}") for g in range(GROUPS)]
         hs = keep.tile([P, GROUPS, D // 4], I32, align_bytes=64, name="hs")
         xs = keep.tile([P, X_PASSES, 2, 2], F32, align_bytes=64, name="xs")
+        xs_full = [keep.tile([P, 2 * P, 4], F32, align_bytes=64, name=f"xs_full{c}") for c in range(X_PASSES)]
         wt_raw = keep.tile([P, GROUPS, 4], BF16, align_bytes=64, name="wt_raw")
         wt = keep.tile([P, GROUPS, 4], F32, align_bytes=64, name="wt")
         ident = keep.tile([P, P], F32, align_bytes=64, name="ident")
@@ -144,22 +145,22 @@ def tile_clipped_policy_head_grad_s13_kernel(
         def do_transposes(h, c):
             if h >= HALVES:
                 return
-            bank = psum_t.tile([P, 2, 2 * P], F32, name="bank")
+            bank = psum_t.tile([P, 2 * P, 2], F32, name="bank")
             banks[h, c] = bank
             for i in range(2):
                 words = cast[h][:, i * D : (i + 1) * D].bitcast(F32)
                 for u in range(2):
                     nc.tensor.transpose(
-                        bank[:, u, i * P : (i + 1) * P], words[:, 256 * c + u : 256 * (c + 1) : 2], ident[:]
+                        bank[:, i * P : (i + 1) * P, u], words[:, 256 * c + u : 256 * (c + 1) : 2], ident[:]
                     )
 
         def do_scale(h, c):
             if c == 0:
                 xg[h] = two.tile([P, X_PASSES, 2 * P, 2, 2], BF16, align_bytes=64, name="xg")
             nc.vector.tensor_tensor(
-                out=xg[h][:, c],
-                in0=banks[h, c][:].bitcast(BF16).rearrange("p u (r e) -> p r u e", e=2),
-                in1=xs[:, c].unsqueeze(1).to_broadcast([P, 2 * P, 2, 2]),
+                out=xg[h][:, c].rearrange("p r u e -> p (r u e)"),
+                in0=banks[h, c][:].rearrange("p r u -> p (r u)").bitcast(BF16),
+                in1=xs_full[c][:].rearrange("p r t -> p (r t)"),
                 op=MULT,
             )
 
@@ -290,6 +291,11 @@ def tile_clipped_policy_head_grad_s13_kernel(
 
         do_cast(0)
         do_cast(1)
+        for c in range(X_PASSES):
+            nc.vector.tensor_copy(
+                out=xs_full[c][:],
+                in_=xs[:, c].rearrange("p u e -> p (u e)").unsqueeze(1).to_broadcast([P, 2 * P, 4]),
+            )
         do_transposes(0, 0)
         do_transposes(0, 1)
         do_w_interleave(1, "gpsimd", 0, W_POOL)

@@ -28,8 +28,8 @@ X_PASSES = D // K_PASS
 M_TILES = D // P
 EARLY = 4
 A_HALF = A // 2
-W_POOL = 384
-VECTOR_CASTS = 3
+W_VECTOR = 256
+REPEAT = 32
 TAIL_SCALAR = 176
 
 
@@ -59,7 +59,7 @@ def tile_clipped_policy_head_grad_s13_kernel(
         g_scales = [keep.tile([P, A], U8, align_bytes=64, name=f"g_scales{g}") for g in range(GROUPS)]
         hs = keep.tile([P, GROUPS, D // 4], I32, align_bytes=64, name="hs")
         xs = keep.tile([P, X_PASSES, 2, 2], F32, align_bytes=64, name="xs")
-        xs_full = [keep.tile([P, 2 * P, 4], F32, align_bytes=64, name=f"xs_full{c}") for c in range(X_PASSES)]
+        xs_rep = keep.tile([P, X_PASSES, REPEAT, 4], F32, align_bytes=64, name="xs_rep")
         wt_raw = keep.tile([P, GROUPS, 4], BF16, align_bytes=64, name="wt_raw")
         wt = keep.tile([P, GROUPS, 4], F32, align_bytes=64, name="wt")
         ident = keep.tile([P, P], F32, align_bytes=64, name="ident")
@@ -88,12 +88,12 @@ def tile_clipped_policy_head_grad_s13_kernel(
         nc.vector.memset(hs[:], 0)
 
         load_x(0)
-        load_x(1)
         nc.sync.dma_start(
             out=xs[:].rearrange("p c u e -> p c (u e)"),
             in_=x_scale.rearrange("o (c p t) -> p (o c) t", p=P, t=4),
         )
         load_w(1)
+        load_x(1)
         load_w(0)
         load_x(2)
         nc.sync.dma_start(out=wt_raw[:], in_=weight.rearrange("(g p t) -> p g t", p=P, t=4))
@@ -137,8 +137,6 @@ def tile_clipped_policy_head_grad_s13_kernel(
                     hi = slice(D + c * K_PASS, D + (c + 1) * K_PASS)
                     nc.vector.tensor_copy(out=cast[h][:, lo], in_=x_raw[h][:, lo].bitcast(FP8))
                     nc.scalar.copy(out=cast[h][:, hi], in_=x_raw[h][:, hi].bitcast(FP8))
-            elif h < VECTOR_CASTS:
-                nc.vector.tensor_copy(out=cast[h][:], in_=x_raw[h][:].bitcast(FP8))
             else:
                 nc.scalar.copy(out=cast[h][:], in_=x_raw[h][:].bitcast(FP8))
 
@@ -158,9 +156,11 @@ def tile_clipped_policy_head_grad_s13_kernel(
             if c == 0:
                 xg[h] = two.tile([P, X_PASSES, 2 * P, 2, 2], BF16, align_bytes=64, name="xg")
             nc.vector.tensor_tensor(
-                out=xg[h][:, c].rearrange("p r u e -> p (r u e)"),
-                in0=banks[h, c][:].rearrange("p r u -> p (r u)").bitcast(BF16),
-                in1=xs_full[c][:].rearrange("p r t -> p (r t)"),
+                out=xg[h][:, c].rearrange("p (o r) u e -> p o (r u e)", r=REPEAT),
+                in0=banks[h, c][:].rearrange("p (o r) u -> p o (r u)", r=REPEAT).bitcast(BF16),
+                in1=xs_rep[:, c].rearrange("p r t -> p (r t)").unsqueeze(1).to_broadcast(
+                    [P, 2 * P // REPEAT, 4 * REPEAT]
+                ),
                 op=MULT,
             )
 
@@ -213,18 +213,19 @@ def tile_clipped_policy_head_grad_s13_kernel(
         def do_residual(h, i):
             g, t = h // 2, 2 * (h % 2) + i
             if t == 0:
-                gp[g] = two.tile([P, 4, A], BF16, align_bytes=64, name="gp")
                 return
             nc.vector.scalar_tensor_tensor(
                 out=gp[g][:, t, :], in0=sig[h, i][:], scalar=wt[:, g, t : t + 1], in1=aw[h, i][:],
                 op0=MULT, op1=SUB,
             )
 
-        def do_pool_sub(g, half):
-            if half == 0:
-                diff[g] = one.tile([P, A], F32, align_bytes=64, name="diff")
+        def do_pool_residual(g, half):
             cols = slice(half * A_HALF, (half + 1) * A_HALF)
-            nc.gpsimd.tensor_tensor(out=diff[g][:, cols], in0=sig[2 * g, 0][:, cols], in1=act[g][:, 0, cols], op=SUB)
+            part = three.tile([P, A_HALF], F32, align_bytes=64, name="part", tag="gi")
+            nc.gpsimd.tensor_tensor(out=part[:], in0=sig[2 * g, 0][:, cols], in1=act[g][:, 0, cols], op=SUB)
+            nc.gpsimd.tensor_scalar(
+                out=gp[g][:, 0, cols], in0=part[:], scalar1=wt[:, g, 0:1], scalar2=0.0, op0=MULT, op1=ADD
+            )
 
         def do_vector_sub(h, i):
             g, t = h // 2, 2 * (h % 2) + i
@@ -241,11 +242,6 @@ def tile_clipped_policy_head_grad_s13_kernel(
                 out=gp[g][:, t, :], in0=diff[h, i][:], scalar1=wt[:, g, t : t + 1], scalar2=None, op0=MULT
             )
 
-        def do_pool_mul(g):
-            nc.gpsimd.tensor_scalar(
-                out=gp[g][:, 0, :], in0=diff[g][:], scalar1=wt[:, g, 0:1], scalar2=0.0, op0=MULT, op1=ADD
-            )
-
         def interleave(engine, dst, src):
             if engine == "vector":
                 nc.vector.tensor_copy(out=dst, in_=src)
@@ -255,7 +251,7 @@ def tile_clipped_policy_head_grad_s13_kernel(
                 nc.gpsimd.tensor_scalar(out=dst, in0=src, scalar1=1.0, scalar2=0.0, op0=MULT, op1=ADD)
 
         def do_interleave(g, half, engine, name="gi"):
-            gi[g, half] = one.tile([P, A_HALF, 4], BF16, align_bytes=64, name=name)
+            gi[g, half] = three.tile([P, A_HALF, 4], BF16, align_bytes=64, name=name, tag=name)
             src = gp[g][:, :, half * A_HALF : (half + 1) * A_HALF].rearrange("p t a -> p a t")
             interleave(engine, gi[g, half][:], src)
 
@@ -290,16 +286,15 @@ def tile_clipped_policy_head_grad_s13_kernel(
         accs = [psum_o.tile([P, A], F32, name=f"acc{m}") for m in range(EARLY)]
 
         do_cast(0)
-        do_cast(1)
-        for c in range(X_PASSES):
-            nc.vector.tensor_copy(
-                out=xs_full[c][:],
-                in_=xs[:, c].rearrange("p u e -> p (u e)").unsqueeze(1).to_broadcast([P, 2 * P, 4]),
-            )
+        nc.vector.tensor_copy(
+            out=xs_rep[:],
+            in_=xs[:].rearrange("p c u e -> p c (u e)").unsqueeze(2).to_broadcast([P, X_PASSES, REPEAT, 4]),
+        )
         do_transposes(0, 0)
         do_transposes(0, 1)
-        do_w_interleave(1, "gpsimd", 0, W_POOL)
-        do_w_interleave(1, "scalar", W_POOL, A)
+        do_w_interleave(1, "vector", 0, W_VECTOR)
+        do_w_interleave(1, "scalar", W_VECTOR, A)
+        do_cast(1)
         do_w_interleave(0, "scalar", 0, A)
 
         for h in range(HALVES):
@@ -309,26 +304,26 @@ def tile_clipped_policy_head_grad_s13_kernel(
             if h >= 2:
                 for i in range(2):
                     do_aw(h - 2, i)
-            if h >= 1:
-                do_cast(h + 2)
+            if h >= 4:
+                do_interleave((h - 4) // 2, h % 2, "scalar")
+            do_cast(h + 2)
             if h % 2 == 1 and h < HALVES - 1:
                 do_diag(h // 2)
-            if h == 1:
-                do_logits(0, (0, 1))
             if h == 2:
                 do_logits(1, (0,))
-            if h >= 4:
-                do_interleave((h - 4) // 2, h % 2, "gpsimd")
             if h >= 2:
-                do_pool_sub(h // 2 - 1, h % 2)
+                if h % 2 == 0:
+                    gp[h // 2 - 1] = two.tile([P, 4, A], BF16, align_bytes=64, name="gp")
+                do_pool_residual(h // 2 - 1, h % 2)
             for c in range(X_PASSES):
                 do_scale(h, c)
+                if (h, c) == (1, 0):
+                    do_quant_w(0)
+                    do_logits(0, (0, 1))
                 do_transposes(h + 1, c)
             if h >= 2:
                 for i in range(2):
                     do_residual(h - 2, i)
-            if h % 2 == 1 and h >= 3:
-                do_pool_mul(h // 2 - 1)
             if h == 0:
                 nc.vector.tensor_copy(out=wt[:], in_=wt_raw[:])
             if h == HALVES - 1:
@@ -342,8 +337,6 @@ def tile_clipped_policy_head_grad_s13_kernel(
             do_quant_x(h)
             if h == 0:
                 do_quant_w(1)
-                do_quant_w(0)
-                do_cast(2)
             if h >= 4:
                 do_quant_g((h - 4) // 2, h % 2)
 

@@ -29,7 +29,6 @@ M_TILES = D // P
 EARLY = 4
 A_HALF = A // 2
 W_VECTOR = 256
-REPEAT = 32
 TAIL_SCALAR = 176
 
 
@@ -59,7 +58,7 @@ def tile_clipped_policy_head_grad_s13_kernel(
         g_scales = [keep.tile([P, A], U8, align_bytes=64, name=f"g_scales{g}") for g in range(GROUPS)]
         hs = keep.tile([P, GROUPS, D // 4], I32, align_bytes=64, name="hs")
         xs = keep.tile([P, X_PASSES, 2, 2], F32, align_bytes=64, name="xs")
-        xs_rep = keep.tile([P, X_PASSES, REPEAT, 4], F32, align_bytes=64, name="xs_rep")
+        xs_full = [keep.tile([P, 2 * P, 4], F32, align_bytes=64, name=f"xs_full{c}") for c in range(X_PASSES)]
         wt_raw = keep.tile([P, GROUPS, 4], BF16, align_bytes=64, name="wt_raw")
         wt = keep.tile([P, GROUPS, 4], F32, align_bytes=64, name="wt")
         ident = keep.tile([P, P], F32, align_bytes=64, name="ident")
@@ -143,24 +142,22 @@ def tile_clipped_policy_head_grad_s13_kernel(
         def do_transposes(h, c):
             if h >= HALVES:
                 return
-            bank = psum_t.tile([P, 2 * P, 2], F32, name="bank")
+            bank = psum_t.tile([P, 2, 2 * P], F32, name="bank")
             banks[h, c] = bank
             for i in range(2):
                 words = cast[h][:, i * D : (i + 1) * D].bitcast(F32)
                 for u in range(2):
                     nc.tensor.transpose(
-                        bank[:, i * P : (i + 1) * P, u], words[:, 256 * c + u : 256 * (c + 1) : 2], ident[:]
+                        bank[:, u, i * P : (i + 1) * P], words[:, 256 * c + u : 256 * (c + 1) : 2], ident[:]
                     )
 
         def do_scale(h, c):
             if c == 0:
                 xg[h] = two.tile([P, X_PASSES, 2 * P, 2, 2], BF16, align_bytes=64, name="xg")
             nc.vector.tensor_tensor(
-                out=xg[h][:, c].rearrange("p (o r) u e -> p o (r u e)", r=REPEAT),
-                in0=banks[h, c][:].rearrange("p (o r) u -> p o (r u)", r=REPEAT).bitcast(BF16),
-                in1=xs_rep[:, c].rearrange("p r t -> p (r t)").unsqueeze(1).to_broadcast(
-                    [P, 2 * P // REPEAT, 4 * REPEAT]
-                ),
+                out=xg[h][:, c],
+                in0=banks[h, c][:].bitcast(BF16).rearrange("p u (r e) -> p r u e", e=2),
+                in1=xs_full[c][:].rearrange("p r (u e) -> p r u e", e=2),
                 op=MULT,
             )
 
@@ -173,8 +170,8 @@ def tile_clipped_policy_head_grad_s13_kernel(
                 in_=xg[h][:].rearrange("p c r u e -> p (c r u e)"),
             )
 
-        def do_z(h, i):
-            zt = psum_z.tile([P, A], F32, name="zt")
+        def do_z(h, i, pool, name):
+            zt = pool.tile([P, A], F32, name=name)
             z[h, i] = zt
             for c in range(X_PASSES):
                 nc.tensor.matmul_mx(
@@ -193,38 +190,35 @@ def tile_clipped_policy_head_grad_s13_kernel(
 
         def do_logits(h, tiles):
             for i in tiles:
-                do_z(h, i)
-                do_sigmoid(h, i)
+                do_z(h, i, psum_z, "zt")
+                if (h, i) != (HALVES - 2, 1):
+                    do_sigmoid(h, i)
 
         def do_diag(g):
             if g >= GROUPS:
                 return
             diag[g] = two.tile([P, 4, P], BF16, align_bytes=64, name="diag")
-            for t in range(1, 4):
+            for t in (1, 3):
                 nc.scalar.activation(out=diag[g][:, t, :], in_=ident_bf[:], func=COPY, scale=wt[:, g, t : t + 1])
 
         def do_aw(h, i):
             g, t = h // 2, 2 * (h % 2) + i
-            if t == 0:
-                return
             aw[h, i] = psum_z.tile([P, A], F32, name="zt")
             nc.tensor.matmul(aw[h, i][:], lhsT=diag[g][:, t, :], rhs=act[g][:, t, :], start=True, stop=True)
 
         def do_residual(h, i):
             g, t = h // 2, 2 * (h % 2) + i
-            if t == 0:
-                return
             nc.vector.scalar_tensor_tensor(
                 out=gp[g][:, t, :], in0=sig[h, i][:], scalar=wt[:, g, t : t + 1], in1=aw[h, i][:],
                 op0=MULT, op1=SUB,
             )
 
-        def do_pool_residual(g, half):
-            cols = slice(half * A_HALF, (half + 1) * A_HALF)
-            part = three.tile([P, A_HALF], F32, align_bytes=64, name="part", tag="gi")
-            nc.gpsimd.tensor_tensor(out=part[:], in0=sig[2 * g, 0][:, cols], in1=act[g][:, 0, cols], op=SUB)
+        def do_pool_residual(h):
+            g, t = h // 2, 2 * (h % 2)
+            part = three.tile([P, A], F32, align_bytes=64, name="part", tag="gi")
+            nc.gpsimd.tensor_tensor(out=part[:], in0=sig[h, 0][:], in1=act[g][:, t, :], op=SUB)
             nc.gpsimd.tensor_scalar(
-                out=gp[g][:, 0, cols], in0=part[:], scalar1=wt[:, g, 0:1], scalar2=0.0, op0=MULT, op1=ADD
+                out=gp[g][:, t, :], in0=part[:], scalar1=wt[:, g, t : t + 1], scalar2=0.0, op0=MULT, op1=ADD
             )
 
         def do_vector_sub(h, i):
@@ -286,10 +280,11 @@ def tile_clipped_policy_head_grad_s13_kernel(
         accs = [psum_o.tile([P, A], F32, name=f"acc{m}") for m in range(EARLY)]
 
         do_cast(0)
-        nc.vector.tensor_copy(
-            out=xs_rep[:],
-            in_=xs[:].rearrange("p c u e -> p c (u e)").unsqueeze(2).to_broadcast([P, X_PASSES, REPEAT, 4]),
-        )
+        spread = [
+            xs[:, c].rearrange("p u e -> p (u e)").unsqueeze(1).to_broadcast([P, 2 * P, 4]) for c in range(X_PASSES)
+        ]
+        nc.vector.tensor_copy(out=xs_full[0][:], in_=spread[0])
+        nc.scalar.copy(out=xs_full[1][:], in_=spread[1])
         do_transposes(0, 0)
         do_transposes(0, 1)
         do_w_interleave(1, "vector", 0, W_VECTOR)
@@ -302,19 +297,19 @@ def tile_clipped_policy_head_grad_s13_kernel(
                 for m in range(2 * (h % 2), 2 * (h % 2) + 2):
                     do_out(accs[m], m, (h - 6) // 2)
             if h >= 2:
-                for i in range(2):
-                    do_aw(h - 2, i)
-            if h >= 4:
+                do_aw(h - 2, 1)
+            if 4 <= h < HALVES - 1:
                 do_interleave((h - 4) // 2, h % 2, "scalar")
-            do_cast(h + 2)
-            if h % 2 == 1 and h < HALVES - 1:
-                do_diag(h // 2)
-            if h == 2:
-                do_logits(1, (0,))
             if h >= 2:
                 if h % 2 == 0:
                     gp[h // 2 - 1] = two.tile([P, 4, A], BF16, align_bytes=64, name="gp")
-                do_pool_residual(h // 2 - 1, h % 2)
+                do_pool_residual(h - 2)
+                do_logits(h - 1, (0,))
+            do_cast(h + 2)
+            if h == HALVES - 2:
+                do_interleave(GROUPS - 3, 1, "scalar", "gi_a")
+            if h % 2 == 1 and h < HALVES - 1:
+                do_diag(h // 2)
             for c in range(X_PASSES):
                 do_scale(h, c)
                 if (h, c) == (1, 0):
@@ -322,46 +317,46 @@ def tile_clipped_policy_head_grad_s13_kernel(
                     do_logits(0, (0, 1))
                 do_transposes(h + 1, c)
             if h >= 2:
-                for i in range(2):
-                    do_residual(h - 2, i)
+                do_residual(h - 2, 1)
             if h == 0:
                 nc.vector.tensor_copy(out=wt[:], in_=wt_raw[:])
             if h == HALVES - 1:
                 accs.append(psum_t.tile([P, A], F32, name="bank"))
                 for g in range(GROUPS - 3):
                     do_out(accs[EARLY], EARLY, g)
-            if h == 2:
-                do_logits(1, (1,))
-            if h >= 3:
-                do_logits(h - 1, (0, 1))
+            if h >= 2:
+                do_logits(h - 1, (1,))
             do_quant_x(h)
             if h == 0:
                 do_quant_w(1)
-            if h >= 4:
+            if 4 <= h < HALVES - 1:
                 do_quant_g((h - 4) // 2, h % 2)
+            if h == HALVES - 1:
+                do_quant_g(GROUPS - 3, 1)
 
         last = GROUPS - 1
         gp[last] = two.tile([P, 4, A], BF16, align_bytes=64, name="gp")
-        accs.append(psum_t.tile([P, A], F32, name="bank"))
-        for g in range(last - 2):
-            do_out(accs[EARLY + 1], EARLY + 1, g)
-        do_interleave(last - 1, 0, "vector", "gi_a")
-        do_interleave(last - 1, 1, "scalar", "gi_b")
-        do_logits(HALVES - 1, (0, 1))
+        do_interleave(last - 1, 0, "scalar", "gi_b")
+        do_z(HALVES - 1, 0, psum_z, "zt")
+        do_z(HALVES - 1, 1, psum_t, "bank")
+        do_sigmoid(HALVES - 2, 1)
+        for i in range(2):
+            do_sigmoid(HALVES - 1, i)
         do_vector_sub(HALVES - 2, 0)
-        do_quant_g(last - 1, 0)
+        do_vector_mul(HALVES - 2, 0)
+        do_interleave(last - 1, 1, "vector", "gi_c")
         do_vector_sub(HALVES - 2, 1)
+        do_quant_g(last - 1, 0)
         do_quant_g(last - 1, 1)
         for i in range(2):
-            do_scalar_mul(HALVES - 2, i)
-        for i in range(2):
             do_vector_sub(HALVES - 1, i)
-        for i in range(2):
-            do_vector_mul(HALVES - 1, i)
-        for m in range(EARLY + 2):
+        do_scalar_mul(HALVES - 2, 1)
+        do_scalar_mul(HALVES - 1, 0)
+        do_vector_mul(HALVES - 1, 1)
+        for m in range(EARLY + 1):
             do_out(accs[m], m, last - 2)
-        for m in range(EARLY + 2, M_TILES):
-            accs.append(psum_z.tile([P, A], F32, name="zt"))
+        for m, pool, name in ((5, psum_z, "zt"), (6, psum_z, "zt"), (7, psum_t, "bank")):
+            accs.append(pool.tile([P, A], F32, name=name))
             for g in range(last - 1):
                 do_out(accs[m], m, g)
         gi[last] = one.tile([P, A, 4], BF16, align_bytes=64, name="gi_last")

@@ -29,6 +29,7 @@ M_TILES = D // P
 EARLY = 4
 A_HALF = A // 2
 W_VECTOR = 256
+HEAD_DIAGS = 5
 TAIL_SCALAR = 176
 
 
@@ -93,9 +94,9 @@ def tile_clipped_policy_head_grad_s13_kernel(
         )
         load_w(1)
         load_x(1)
+        nc.sync.dma_start(out=wt_raw[:], in_=weight.rearrange("(g p t) -> p g t", p=P, t=4))
         load_w(0)
         load_x(2)
-        nc.sync.dma_start(out=wt_raw[:], in_=weight.rearrange("(g p t) -> p g t", p=P, t=4))
         load_x(3)
         load_act(0)
         load_x(4)
@@ -124,7 +125,6 @@ def tile_clipped_policy_head_grad_s13_kernel(
         aw = {}
         gp = {}
         gi = {}
-        diff = {}
 
         def do_cast(h):
             if h >= HALVES:
@@ -153,7 +153,7 @@ def tile_clipped_policy_head_grad_s13_kernel(
 
         def do_scale(h, c):
             if c == 0:
-                xg[h] = two.tile([P, X_PASSES, 2 * P, 2, 2], BF16, align_bytes=64, name="xg")
+                xg[h] = one.tile([P, X_PASSES, 2 * P, 2, 2], BF16, align_bytes=64, name="xg", tag=f"xg{h % 2}")
             nc.vector.tensor_tensor(
                 out=xg[h][:, c],
                 in0=banks[h, c][:].bitcast(BF16).rearrange("p u (r e) -> p r u e", e=2),
@@ -194,17 +194,18 @@ def tile_clipped_policy_head_grad_s13_kernel(
                 if (h, i) != (HALVES - 2, 1):
                     do_sigmoid(h, i)
 
-        def do_diag(g):
-            if g >= GROUPS:
-                return
-            diag[g] = two.tile([P, 4, P], BF16, align_bytes=64, name="diag")
-            for t in (1, 3):
-                nc.scalar.activation(out=diag[g][:, t, :], in_=ident_bf[:], func=COPY, scale=wt[:, g, t : t + 1])
-
-        def do_aw(h, i):
+        def do_diag(h, i=1):
             g, t = h // 2, 2 * (h % 2) + i
-            aw[h, i] = psum_z.tile([P, A], F32, name="zt")
-            nc.tensor.matmul(aw[h, i][:], lhsT=diag[g][:, t, :], rhs=act[g][:, t, :], start=True, stop=True)
+            h = (h, i)
+            diag[h] = keep.tile([P, P], BF16, align_bytes=64, name=f"diag{g}_{t}")
+            nc.gpsimd.tensor_scalar(
+                out=diag[h][:], in0=ident_bf[:], scalar1=wt_raw[:, g, t : t + 1], scalar2=0.0, op0=MULT, op1=ADD
+            )
+
+        def do_aw(h, i, pool, name):
+            g, t = h // 2, 2 * (h % 2) + i
+            aw[h, i] = pool.tile([P, A], F32, name=name)
+            nc.tensor.matmul(aw[h, i][:], lhsT=diag[h, i][:], rhs=act[g][:, t, :], start=True, stop=True)
 
         def do_residual(h, i):
             g, t = h // 2, 2 * (h % 2) + i
@@ -213,28 +214,24 @@ def tile_clipped_policy_head_grad_s13_kernel(
                 op0=MULT, op1=SUB,
             )
 
-        def do_pool_residual(h):
+        def do_pool_residual(h, step):
             g, t = h // 2, 2 * (h % 2)
-            part = three.tile([P, A], F32, align_bytes=64, name="part", tag="gi")
+            part = one.tile([P, A], F32, align_bytes=64, name="part", tag=f"xg{(step - 1) % 2}")
             nc.gpsimd.tensor_tensor(out=part[:], in0=sig[h, 0][:], in1=act[g][:, t, :], op=SUB)
             nc.gpsimd.tensor_scalar(
                 out=gp[g][:, t, :], in0=part[:], scalar1=wt[:, g, t : t + 1], scalar2=0.0, op0=MULT, op1=ADD
             )
 
-        def do_vector_sub(h, i):
+        def do_aw_sbuf(h, i, engine):
             g, t = h // 2, 2 * (h % 2) + i
-            diff[h, i] = four.tile([P, A], F32, align_bytes=64, name="vdiff")
-            nc.vector.tensor_tensor(out=diff[h, i][:], in0=sig[h, i][:], in1=act[g][:, t, :], op=SUB)
-
-        def do_scalar_mul(h, i):
-            g, t = h // 2, 2 * (h % 2) + i
-            nc.scalar.activation(out=gp[g][:, t, :], in_=diff[h, i][:], func=COPY, scale=wt[:, g, t : t + 1])
-
-        def do_vector_mul(h, i):
-            g, t = h // 2, 2 * (h % 2) + i
-            nc.vector.tensor_scalar(
-                out=gp[g][:, t, :], in0=diff[h, i][:], scalar1=wt[:, g, t : t + 1], scalar2=None, op0=MULT
-            )
+            aw[h, i] = four.tile([P, A], F32, align_bytes=64, name="aw_sbuf")
+            if engine == "scalar":
+                nc.scalar.activation(out=aw[h, i][:], in_=act[g][:, t, :], func=COPY, scale=wt[:, g, t : t + 1])
+            else:
+                nc.gpsimd.tensor_scalar(
+                    out=aw[h, i][:], in0=act[g][:, t, :], scalar1=wt[:, g, t : t + 1], scalar2=0.0,
+                    op0=MULT, op1=ADD,
+                )
 
         def interleave(engine, dst, src):
             if engine == "vector":
@@ -245,7 +242,7 @@ def tile_clipped_policy_head_grad_s13_kernel(
                 nc.gpsimd.tensor_scalar(out=dst, in0=src, scalar1=1.0, scalar2=0.0, op0=MULT, op1=ADD)
 
         def do_interleave(g, half, engine, name="gi"):
-            gi[g, half] = three.tile([P, A_HALF, 4], BF16, align_bytes=64, name=name, tag=name)
+            gi[g, half] = two.tile([P, A_HALF, 4], BF16, align_bytes=64, name=name)
             src = gp[g][:, :, half * A_HALF : (half + 1) * A_HALF].rearrange("p t a -> p a t")
             interleave(engine, gi[g, half][:], src)
 
@@ -277,7 +274,7 @@ def tile_clipped_policy_head_grad_s13_kernel(
                 in_=w_int[c][:].rearrange("p n j -> p (n j)"),
             )
 
-        accs = [psum_o.tile([P, A], F32, name=f"acc{m}") for m in range(EARLY)]
+        accs = []
 
         do_cast(0)
         spread = [
@@ -291,32 +288,54 @@ def tile_clipped_policy_head_grad_s13_kernel(
         do_w_interleave(1, "scalar", W_VECTOR, A)
         do_cast(1)
         do_w_interleave(0, "scalar", 0, A)
+        do_diag(1, 0)
+        for h in range(HEAD_DIAGS):
+            do_diag(h)
 
         for h in range(HALVES):
+            if h == 6:
+                accs.extend(psum_o.tile([P, A], F32, name=f"acc{m}") for m in range(EARLY))
             if h >= 6:
                 for m in range(2 * (h % 2), 2 * (h % 2) + 2):
                     do_out(accs[m], m, (h - 6) // 2)
-            if h >= 2:
-                do_aw(h - 2, 1)
+            if h >= 4:
+                do_aw(h - 2, 1, psum_z, "zt")
+            if h == 1:
+                for early in range(2):
+                    do_aw(early, 1, psum_o, f"acc{early}")
+                do_aw(1, 0, psum_o, "acc2")
             if 4 <= h < HALVES - 1:
                 do_interleave((h - 4) // 2, h % 2, "scalar")
-            if h >= 2:
-                if h % 2 == 0:
-                    gp[h // 2 - 1] = two.tile([P, 4, A], BF16, align_bytes=64, name="gp")
-                do_pool_residual(h - 2)
+            if h == HALVES - 1:
+                for i in range(2):
+                    do_aw_sbuf(h - 1, i, "scalar")
+            if h >= 3:
                 do_logits(h - 1, (0,))
+            if h == HALVES - 1:
+                do_aw_sbuf(h, 0, "scalar")
             do_cast(h + 2)
             if h == HALVES - 2:
                 do_interleave(GROUPS - 3, 1, "scalar", "gi_a")
-            if h % 2 == 1 and h < HALVES - 1:
-                do_diag(h // 2)
             for c in range(X_PASSES):
                 do_scale(h, c)
+                if c == 0 and h >= 2:
+                    if h % 2 == 0:
+                        gp[h // 2 - 1] = two.tile([P, 4, A], BF16, align_bytes=64, name="gp")
+                    if h >= 3:
+                        do_pool_residual(h - 2 if h > 3 else 0, h)
+                    if h == HALVES - 1:
+                        do_aw_sbuf(h, 1, "gpsimd")
+                    if h + HEAD_DIAGS - 4 < HALVES - 2 and h >= 4:
+                        do_diag(h + HEAD_DIAGS - 4)
                 if (h, c) == (1, 0):
                     do_quant_w(0)
-                    do_logits(0, (0, 1))
                 do_transposes(h + 1, c)
-            if h >= 2:
+            if h == 1:
+                do_logits(0, (0, 1))
+            if h == 3:
+                do_residual(0, 1)
+                do_residual(1, 0)
+            if h >= 3:
                 do_residual(h - 2, 1)
             if h == 0:
                 nc.vector.tensor_copy(out=wt[:], in_=wt_raw[:])
@@ -324,7 +343,9 @@ def tile_clipped_policy_head_grad_s13_kernel(
                 accs.append(psum_t.tile([P, A], F32, name="bank"))
                 for g in range(GROUPS - 3):
                     do_out(accs[EARLY], EARLY, g)
-            if h >= 2:
+            if h == 2:
+                do_logits(1, (0, 1))
+            if h >= 3:
                 do_logits(h - 1, (1,))
             do_quant_x(h)
             if h == 0:
@@ -342,17 +363,13 @@ def tile_clipped_policy_head_grad_s13_kernel(
         do_sigmoid(HALVES - 2, 1)
         for i in range(2):
             do_sigmoid(HALVES - 1, i)
-        do_vector_sub(HALVES - 2, 0)
-        do_vector_mul(HALVES - 2, 0)
+        do_residual(HALVES - 2, 0)
         do_interleave(last - 1, 1, "vector", "gi_c")
-        do_vector_sub(HALVES - 2, 1)
         do_quant_g(last - 1, 0)
+        do_residual(HALVES - 2, 1)
         do_quant_g(last - 1, 1)
         for i in range(2):
-            do_vector_sub(HALVES - 1, i)
-        do_scalar_mul(HALVES - 2, 1)
-        do_scalar_mul(HALVES - 1, 0)
-        do_vector_mul(HALVES - 1, 1)
+            do_residual(HALVES - 1, i)
         for m in range(EARLY + 1):
             do_out(accs[m], m, last - 2)
         for m, pool, name in ((5, psum_z, "zt"), (6, psum_z, "zt"), (7, psum_t, "bank")):

@@ -29,7 +29,6 @@ M_TILES = D // P
 EARLY = 4
 A_HALF = A // 2
 W_VECTOR = 256
-HEAD_DIAGS = 5
 TAIL_SCALAR = 176
 
 
@@ -84,17 +83,17 @@ def tile_clipped_policy_head_grad_s13_kernel(
             nc.sync.dma_start(out=hw[g][:], in_=h_words[g])
 
         make_identity(nc, ident[:])
-        make_identity(nc, ident_bf[:])
         nc.vector.memset(hs[:], 0)
+        nc.vector.tensor_copy(out=ident_bf[:], in_=ident[:])
 
         load_x(0)
         nc.sync.dma_start(
             out=xs[:].rearrange("p c u e -> p c (u e)"),
             in_=x_scale.rearrange("o (c p t) -> p (o c) t", p=P, t=4),
         )
+        nc.sync.dma_start(out=wt_raw[:], in_=weight.rearrange("(g p t) -> p g t", p=P, t=4))
         load_w(1)
         load_x(1)
-        nc.sync.dma_start(out=wt_raw[:], in_=weight.rearrange("(g p t) -> p g t", p=P, t=4))
         load_w(0)
         load_x(2)
         load_x(3)
@@ -194,18 +193,24 @@ def tile_clipped_policy_head_grad_s13_kernel(
                 if (h, i) != (HALVES - 2, 1):
                     do_sigmoid(h, i)
 
-        def do_diag(h, i=1):
-            g, t = h // 2, 2 * (h % 2) + i
-            h = (h, i)
-            diag[h] = keep.tile([P, P], BF16, align_bytes=64, name=f"diag{g}_{t}")
-            nc.gpsimd.tensor_scalar(
-                out=diag[h][:], in0=ident_bf[:], scalar1=wt_raw[:, g, t : t + 1], scalar2=0.0, op0=MULT, op1=ADD
+        def do_diags(tag, groups, first, step):
+            ts = range(first, 4, step)
+            shape = [P, len(groups), len(ts), P]
+            tile = keep.tile(shape, BF16, align_bytes=64, name="diags", tag=tag)
+            nc.gpsimd.tensor_tensor(
+                out=tile[:],
+                in0=ident_bf[:].unsqueeze(1).unsqueeze(1).to_broadcast(shape),
+                in1=wt[:, groups.start : groups.stop, first:4:step].unsqueeze(3).to_broadcast(shape),
+                op=MULT,
             )
+            for a, g in enumerate(groups):
+                for b, t in enumerate(ts):
+                    diag[g, t] = tile[:, a, b, :]
 
         def do_aw(h, i, pool, name):
             g, t = h // 2, 2 * (h % 2) + i
             aw[h, i] = pool.tile([P, A], F32, name=name)
-            nc.tensor.matmul(aw[h, i][:], lhsT=diag[h, i][:], rhs=act[g][:, t, :], start=True, stop=True)
+            nc.tensor.matmul(aw[h, i][:], lhsT=diag[g, t], rhs=act[g][:, t, :], start=True, stop=True)
 
         def do_residual(h, i):
             g, t = h // 2, 2 * (h % 2) + i
@@ -214,9 +219,9 @@ def tile_clipped_policy_head_grad_s13_kernel(
                 op0=MULT, op1=SUB,
             )
 
-        def do_pool_residual(h, step):
+        def do_pool_residual(h, slot):
             g, t = h // 2, 2 * (h % 2)
-            part = one.tile([P, A], F32, align_bytes=64, name="part", tag=f"xg{(step - 1) % 2}")
+            part = one.tile([P, A], F32, align_bytes=64, name="part", tag=slot)
             nc.gpsimd.tensor_tensor(out=part[:], in0=sig[h, 0][:], in1=act[g][:, t, :], op=SUB)
             nc.gpsimd.tensor_scalar(
                 out=gp[g][:, t, :], in0=part[:], scalar1=wt[:, g, t : t + 1], scalar2=0.0, op0=MULT, op1=ADD
@@ -228,9 +233,8 @@ def tile_clipped_policy_head_grad_s13_kernel(
             if engine == "scalar":
                 nc.scalar.activation(out=aw[h, i][:], in_=act[g][:, t, :], func=COPY, scale=wt[:, g, t : t + 1])
             else:
-                nc.gpsimd.tensor_scalar(
-                    out=aw[h, i][:], in0=act[g][:, t, :], scalar1=wt[:, g, t : t + 1], scalar2=0.0,
-                    op0=MULT, op1=ADD,
+                nc.vector.tensor_scalar(
+                    out=aw[h, i][:], in0=act[g][:, t, :], scalar1=wt[:, g, t : t + 1], scalar2=None, op0=MULT
                 )
 
         def interleave(engine, dst, src):
@@ -241,8 +245,8 @@ def tile_clipped_policy_head_grad_s13_kernel(
             else:
                 nc.gpsimd.tensor_scalar(out=dst, in0=src, scalar1=1.0, scalar2=0.0, op0=MULT, op1=ADD)
 
-        def do_interleave(g, half, engine, name="gi"):
-            gi[g, half] = two.tile([P, A_HALF, 4], BF16, align_bytes=64, name=name)
+        def do_interleave(g, half, engine, slot):
+            gi[g, half] = one.tile([P, A_HALF, 4], BF16, align_bytes=64, name="gi", tag=slot)
             src = gp[g][:, :, half * A_HALF : (half + 1) * A_HALF].rearrange("p t a -> p a t")
             interleave(engine, gi[g, half][:], src)
 
@@ -285,12 +289,11 @@ def tile_clipped_policy_head_grad_s13_kernel(
         do_transposes(0, 0)
         do_transposes(0, 1)
         do_w_interleave(1, "vector", 0, W_VECTOR)
+        nc.vector.tensor_copy(out=wt[:], in_=wt_raw[:])
+        do_diags("diags", range(0, 1), 1, 1)
         do_w_interleave(1, "scalar", W_VECTOR, A)
         do_cast(1)
         do_w_interleave(0, "scalar", 0, A)
-        do_diag(1, 0)
-        for h in range(HEAD_DIAGS):
-            do_diag(h)
 
         for h in range(HALVES):
             if h == 6:
@@ -305,7 +308,7 @@ def tile_clipped_policy_head_grad_s13_kernel(
                     do_aw(early, 1, psum_o, f"acc{early}")
                 do_aw(1, 0, psum_o, "acc2")
             if 4 <= h < HALVES - 1:
-                do_interleave((h - 4) // 2, h % 2, "scalar")
+                do_interleave((h - 4) // 2, h % 2, "scalar", f"gi{h % 2}")
             if h == HALVES - 1:
                 for i in range(2):
                     do_aw_sbuf(h - 1, i, "scalar")
@@ -322,23 +325,17 @@ def tile_clipped_policy_head_grad_s13_kernel(
                     if h % 2 == 0:
                         gp[h // 2 - 1] = two.tile([P, 4, A], BF16, align_bytes=64, name="gp")
                     if h >= 3:
-                        do_pool_residual(h - 2 if h > 3 else 0, h)
-                    if h == HALVES - 1:
-                        do_aw_sbuf(h, 1, "gpsimd")
-                    if h + HEAD_DIAGS - 4 < HALVES - 2 and h >= 4:
-                        do_diag(h + HEAD_DIAGS - 4)
-                if (h, c) == (1, 0):
-                    do_quant_w(0)
+                        do_pool_residual(h - 2 if h > 3 else 0, f"gi{(h - 1) % 2}" if h >= 5 else f"xg{(h - 1) % 2}")
                 do_transposes(h + 1, c)
             if h == 1:
+                do_quant_w(0)
+                do_diags("w_int0", range(3, 5), 1, 2)
                 do_logits(0, (0, 1))
             if h == 3:
                 do_residual(0, 1)
                 do_residual(1, 0)
             if h >= 3:
                 do_residual(h - 2, 1)
-            if h == 0:
-                nc.vector.tensor_copy(out=wt[:], in_=wt_raw[:])
             if h == HALVES - 1:
                 accs.append(psum_t.tile([P, A], F32, name="bank"))
                 for g in range(GROUPS - 3):
@@ -350,6 +347,7 @@ def tile_clipped_policy_head_grad_s13_kernel(
             do_quant_x(h)
             if h == 0:
                 do_quant_w(1)
+                do_diags("w_int1", range(1, 3), 1, 2)
             if 4 <= h < HALVES - 1:
                 do_quant_g((h - 4) // 2, h % 2)
             if h == HALVES - 1:
@@ -364,6 +362,7 @@ def tile_clipped_policy_head_grad_s13_kernel(
         for i in range(2):
             do_sigmoid(HALVES - 1, i)
         do_residual(HALVES - 2, 0)
+        do_aw_sbuf(HALVES - 1, 1, "vector")
         do_interleave(last - 1, 1, "vector", "gi_c")
         do_quant_g(last - 1, 0)
         do_residual(HALVES - 2, 1)

@@ -28,7 +28,7 @@ X_PASSES = D // K_PASS
 M_TILES = D // P
 EARLY = 4
 A_HALF = A // 2
-W_VECTOR = 256
+WARM_MATMULS = 5
 TAIL_SCALAR = 176
 
 
@@ -61,6 +61,8 @@ def tile_clipped_policy_head_grad_s13_kernel(
         xs_full = [keep.tile([P, 2 * P, 4], F32, align_bytes=64, name=f"xs_full{c}") for c in range(X_PASSES)]
         wt_raw = keep.tile([P, GROUPS, 4], BF16, align_bytes=64, name="wt_raw")
         wt = keep.tile([P, GROUPS, 4], F32, align_bytes=64, name="wt")
+        warm = keep.tile([P, 1], F32, align_bytes=64, name="warm")
+        zeros = keep.tile([P, A], BF16, align_bytes=64, name="zeros")
         ident = keep.tile([P, P], F32, align_bytes=64, name="ident")
         ident_bf = keep.tile([P, P], BF16, align_bytes=64, name="ident_bf")
 
@@ -82,6 +84,12 @@ def tile_clipped_policy_head_grad_s13_kernel(
         def load_h(g):
             nc.sync.dma_start(out=hw[g][:], in_=h_words[g])
 
+        nc.vector.memset(warm[:], 0.0)
+        nc.scalar.activation(out=warm[:], in_=warm[:], func=SIGMOID)
+        nc.vector.memset(zeros[:], 0.0)
+        idle = psum_z.tile([P, A], F32, name="zt")
+        for rep in range(WARM_MATMULS):
+            nc.tensor.matmul(idle[:], lhsT=zeros[:, :P], rhs=zeros[:], start=True, stop=True)
         make_identity(nc, ident[:])
         nc.vector.memset(hs[:], 0)
         nc.vector.tensor_copy(out=ident_bf[:], in_=ident[:])
@@ -193,14 +201,14 @@ def tile_clipped_policy_head_grad_s13_kernel(
                 if (h, i) != (HALVES - 2, 1):
                     do_sigmoid(h, i)
 
-        def do_diags(tag, groups, first, step):
-            ts = range(first, 4, step)
+        def do_diags(tag, groups):
+            ts = range(1, 4, 2)
             shape = [P, len(groups), len(ts), P]
             tile = keep.tile(shape, BF16, align_bytes=64, name="diags", tag=tag)
             nc.gpsimd.tensor_tensor(
                 out=tile[:],
                 in0=ident_bf[:].unsqueeze(1).unsqueeze(1).to_broadcast(shape),
-                in1=wt[:, groups.start : groups.stop, first:4:step].unsqueeze(3).to_broadcast(shape),
+                in1=wt[:, groups.start : groups.stop, 1:4:2].unsqueeze(3).to_broadcast(shape),
                 op=MULT,
             )
             for a, g in enumerate(groups):
@@ -245,17 +253,15 @@ def tile_clipped_policy_head_grad_s13_kernel(
             else:
                 nc.gpsimd.tensor_scalar(out=dst, in0=src, scalar1=1.0, scalar2=0.0, op0=MULT, op1=ADD)
 
-        def do_interleave(g, half, engine, slot):
-            gi[g, half] = one.tile([P, A_HALF, 4], BF16, align_bytes=64, name="gi", tag=slot)
-            src = gp[g][:, :, half * A_HALF : (half + 1) * A_HALF].rearrange("p t a -> p a t")
-            interleave(engine, gi[g, half][:], src)
+        def do_interleave(g, engine, lo, hi):
+            if g not in gi:
+                gi[g] = one.tile([P, A, 4], BF16, align_bytes=64, name="gi", tag=f"gi{g % 2}")
+            interleave(engine, gi[g][:, lo:hi, :], gp[g][:, :, lo:hi].rearrange("p t a -> p a t"))
 
-        def do_quant_g(g, half):
-            cols = slice(half * A_HALF, (half + 1) * A_HALF)
+        def do_quant_g(g):
             nc.vector.quantize_mx(
-                out=g_codes[g][:, cols].bitcast(FP8X4),
-                scales=g_scales[g][:, cols],
-                in_=gi[g, half][:].rearrange("p a t -> p (a t)"),
+                out=g_codes[g][:].bitcast(FP8X4), scales=g_scales[g][:],
+                in_=gi[g][:].rearrange("p a t -> p (a t)"),
             )
 
         def do_out(acc, m, g):
@@ -269,8 +275,19 @@ def tile_clipped_policy_head_grad_s13_kernel(
                 stop=(g == GROUPS - 1),
             )
 
-        def do_w_interleave(c, engine, lo, hi):
-            interleave(engine, w_int[c][:, lo:hi, :], w_raw[c][:, :, lo:hi].rearrange("p j n -> p n j"))
+        def do_w_interleave(c):
+            for half in range(2):
+                bank = psum_o.tile([P, A_HALF, 4], BF16, name=f"acc{2 * c + half}")
+                for q in range(2):
+                    cols = slice(half * A_HALF + q * P, half * A_HALF + (q + 1) * P)
+                    nc.tensor.matmul(
+                        bank[:, q * P : (q + 1) * P, :].rearrange("p n j -> p (n j)"),
+                        lhsT=ident_bf[:],
+                        rhs=w_raw[c][:, :, cols].rearrange("p j n -> p n j"),
+                        start=True,
+                        stop=True,
+                    )
+                nc.scalar.copy(out=w_int[c][:, half * A_HALF : (half + 1) * A_HALF, :], in_=bank[:])
 
         def do_quant_w(c):
             nc.vector.quantize_mx(
@@ -288,12 +305,11 @@ def tile_clipped_policy_head_grad_s13_kernel(
         nc.scalar.copy(out=xs_full[1][:], in_=spread[1])
         do_transposes(0, 0)
         do_transposes(0, 1)
-        do_w_interleave(1, "vector", 0, W_VECTOR)
         nc.vector.tensor_copy(out=wt[:], in_=wt_raw[:])
-        do_diags("diags", range(0, 1), 1, 1)
-        do_w_interleave(1, "scalar", W_VECTOR, A)
+        do_diags("diags", range(0, 3))
         do_cast(1)
-        do_w_interleave(0, "scalar", 0, A)
+        do_w_interleave(1)
+        do_w_interleave(0)
 
         for h in range(HALVES):
             if h == 6:
@@ -301,72 +317,60 @@ def tile_clipped_policy_head_grad_s13_kernel(
             if h >= 6:
                 for m in range(2 * (h % 2), 2 * (h % 2) + 2):
                     do_out(accs[m], m, (h - 6) // 2)
-            if h >= 4:
+            if h >= 2:
                 do_aw(h - 2, 1, psum_z, "zt")
-            if h == 1:
-                for early in range(2):
-                    do_aw(early, 1, psum_o, f"acc{early}")
-                do_aw(1, 0, psum_o, "acc2")
             if 4 <= h < HALVES - 1:
-                do_interleave((h - 4) // 2, h % 2, "scalar", f"gi{h % 2}")
+                do_interleave((h - 4) // 2, "scalar", A_HALF * (h % 2), A_HALF * (h % 2 + 1))
             if h == HALVES - 1:
                 for i in range(2):
                     do_aw_sbuf(h - 1, i, "scalar")
-            if h >= 3:
+            if h >= 2:
                 do_logits(h - 1, (0,))
             if h == HALVES - 1:
                 do_aw_sbuf(h, 0, "scalar")
             do_cast(h + 2)
             if h == HALVES - 2:
-                do_interleave(GROUPS - 3, 1, "scalar", "gi_a")
+                do_interleave(GROUPS - 3, "scalar", A_HALF, A)
             for c in range(X_PASSES):
                 do_scale(h, c)
                 if c == 0 and h >= 2:
                     if h % 2 == 0:
                         gp[h // 2 - 1] = two.tile([P, 4, A], BF16, align_bytes=64, name="gp")
-                    if h >= 3:
-                        do_pool_residual(h - 2 if h > 3 else 0, f"gi{(h - 1) % 2}" if h >= 5 else f"xg{(h - 1) % 2}")
+                    if h >= 2:
+                        do_pool_residual(h - 2, f"gi{(h // 2 - 1) % 2}" if h >= 6 and h % 2 == 0 else f"xg{(h - 1) % 2}")
+                if (h, c) == (1, 0):
+                    do_quant_w(0)
+                    do_diags("w_int0", range(4, 5))
                 do_transposes(h + 1, c)
-            if h == 1:
-                do_quant_w(0)
-                do_diags("w_int0", range(3, 5), 1, 2)
-                do_logits(0, (0, 1))
-            if h == 3:
-                do_residual(0, 1)
-                do_residual(1, 0)
-            if h >= 3:
+                if (h, c) == (1, 0):
+                    do_logits(0, (0,))
+            if h >= 2:
                 do_residual(h - 2, 1)
             if h == HALVES - 1:
                 accs.append(psum_t.tile([P, A], F32, name="bank"))
                 for g in range(GROUPS - 3):
                     do_out(accs[EARLY], EARLY, g)
-            if h == 2:
-                do_logits(1, (0, 1))
-            if h >= 3:
+            if h >= 1:
                 do_logits(h - 1, (1,))
             do_quant_x(h)
             if h == 0:
                 do_quant_w(1)
-                do_diags("w_int1", range(1, 3), 1, 2)
-            if 4 <= h < HALVES - 1:
-                do_quant_g((h - 4) // 2, h % 2)
-            if h == HALVES - 1:
-                do_quant_g(GROUPS - 3, 1)
+                do_diags("w_int1", range(3, 4))
+            if h >= 5 and h % 2 == 1:
+                do_quant_g((h - 5) // 2)
 
         last = GROUPS - 1
         gp[last] = two.tile([P, 4, A], BF16, align_bytes=64, name="gp")
-        do_interleave(last - 1, 0, "scalar", "gi_b")
+        do_interleave(last - 1, "scalar", 0, A_HALF)
         do_z(HALVES - 1, 0, psum_z, "zt")
         do_z(HALVES - 1, 1, psum_t, "bank")
         do_sigmoid(HALVES - 2, 1)
         for i in range(2):
             do_sigmoid(HALVES - 1, i)
+        do_interleave(last - 1, "scalar", A_HALF, A)
         do_residual(HALVES - 2, 0)
         do_aw_sbuf(HALVES - 1, 1, "vector")
-        do_interleave(last - 1, 1, "vector", "gi_c")
-        do_quant_g(last - 1, 0)
         do_residual(HALVES - 2, 1)
-        do_quant_g(last - 1, 1)
         for i in range(2):
             do_residual(HALVES - 1, i)
         for m in range(EARLY + 1):
@@ -375,13 +379,10 @@ def tile_clipped_policy_head_grad_s13_kernel(
             accs.append(pool.tile([P, A], F32, name=name))
             for g in range(last - 1):
                 do_out(accs[m], m, g)
-        gi[last] = one.tile([P, A, 4], BF16, align_bytes=64, name="gi_last")
-        for engine, lo, hi in (("scalar", 0, TAIL_SCALAR), ("vector", TAIL_SCALAR, A)):
-            interleave(engine, gi[last][:, lo:hi, :], gp[last][:, :, lo:hi].rearrange("p t a -> p a t"))
-        nc.vector.quantize_mx(
-            out=g_codes[last][:].bitcast(FP8X4), scales=g_scales[last][:],
-            in_=gi[last][:].rearrange("p a t -> p (a t)"),
-        )
+        do_interleave(last, "scalar", 0, TAIL_SCALAR)
+        do_interleave(last, "vector", TAIL_SCALAR, A)
+        do_quant_g(last - 1)
+        do_quant_g(last)
         for m in range(M_TILES):
             do_out(accs[m], m, last - 1)
             do_out(accs[m], m, last)

@@ -28,7 +28,6 @@ X_PASSES = D // K_PASS
 M_TILES = D // P
 EARLY = 4
 A_HALF = A // 2
-WARM_MATMULS = 5
 TAIL_SCALAR = 176
 
 
@@ -50,7 +49,10 @@ def tile_clipped_policy_head_grad_s13_kernel(
         x_raw = [keep.tile([P, 2 * D], U8, align_bytes=64, name=f"x_raw{h}") for h in range(HALVES)]
         act = [keep.tile([P, 4, A], BF16, align_bytes=64, name=f"act{g}") for g in range(GROUPS)]
         hw = [keep.tile([P, 2 * D], U8, align_bytes=64, name=f"hw{g}") for g in range(GROUPS)]
-        w_raw = [keep.tile([P, 4, A], BF16, align_bytes=64, name=f"w_raw{c}") for c in range(X_PASSES)]
+        w_raw = [
+            [keep.tile([P, 4, A_HALF], BF16, align_bytes=64, name=f"w_raw{c}_{half}") for half in range(2)]
+            for c in range(X_PASSES)
+        ]
         w_int = [keep.tile([P, A, 4], BF16, align_bytes=64, name=f"w_int{c}") for c in range(X_PASSES)]
         w_codes = [keep.tile([P, A], U32, align_bytes=64, name=f"w_codes{c}") for c in range(X_PASSES)]
         w_scales = [keep.tile([P, A], U8, align_bytes=64, name=f"w_scales{c}") for c in range(X_PASSES)]
@@ -58,11 +60,9 @@ def tile_clipped_policy_head_grad_s13_kernel(
         g_scales = [keep.tile([P, A], U8, align_bytes=64, name=f"g_scales{g}") for g in range(GROUPS)]
         hs = keep.tile([P, GROUPS, D // 4], I32, align_bytes=64, name="hs")
         xs = keep.tile([P, X_PASSES, 2, 2], F32, align_bytes=64, name="xs")
-        xs_full = [keep.tile([P, 2 * P, 4], F32, align_bytes=64, name=f"xs_full{c}") for c in range(X_PASSES)]
         wt_raw = keep.tile([P, GROUPS, 4], BF16, align_bytes=64, name="wt_raw")
         wt = keep.tile([P, GROUPS, 4], F32, align_bytes=64, name="wt")
         warm = keep.tile([P, 1], F32, align_bytes=64, name="warm")
-        zeros = keep.tile([P, A], BF16, align_bytes=64, name="zeros")
         ident = keep.tile([P, P], F32, align_bytes=64, name="ident")
         ident_bf = keep.tile([P, P], BF16, align_bytes=64, name="ident_bf")
 
@@ -72,9 +72,9 @@ def tile_clipped_policy_head_grad_s13_kernel(
             nc.sync.dma_start(out=x_raw[h][:], in_=src[:, lo * D : (lo + 2) * D])
 
         def load_w(c):
-            nc.sync.dma_start(
-                out=w_raw[c][:], in_=w[c * K_PASS : (c + 1) * K_PASS, :].rearrange("(p j) n -> p j n", j=4)
-            )
+            rows = w[c * K_PASS : (c + 1) * K_PASS, :].rearrange("(p j) n -> p j n", j=4)
+            for half in range(2):
+                nc.sync.dma_start(out=w_raw[c][half][:], in_=rows[:, :, half * A_HALF : (half + 1) * A_HALF])
 
         def load_act(g):
             nc.sync.dma_start(
@@ -86,10 +86,6 @@ def tile_clipped_policy_head_grad_s13_kernel(
 
         nc.vector.memset(warm[:], 0.0)
         nc.scalar.activation(out=warm[:], in_=warm[:], func=SIGMOID)
-        nc.vector.memset(zeros[:], 0.0)
-        idle = psum_z.tile([P, A], F32, name="zt")
-        for rep in range(WARM_MATMULS):
-            nc.tensor.matmul(idle[:], lhsT=zeros[:, :P], rhs=zeros[:], start=True, stop=True)
         make_identity(nc, ident[:])
         nc.vector.memset(hs[:], 0)
         nc.vector.tensor_copy(out=ident_bf[:], in_=ident[:])
@@ -99,8 +95,8 @@ def tile_clipped_policy_head_grad_s13_kernel(
             out=xs[:].rearrange("p c u e -> p c (u e)"),
             in_=x_scale.rearrange("o (c p t) -> p (o c) t", p=P, t=4),
         )
-        nc.sync.dma_start(out=wt_raw[:], in_=weight.rearrange("(g p t) -> p g t", p=P, t=4))
         load_w(1)
+        nc.sync.dma_start(out=wt_raw[:], in_=weight.rearrange("(g p t) -> p g t", p=P, t=4))
         load_x(1)
         load_w(0)
         load_x(2)
@@ -164,7 +160,7 @@ def tile_clipped_policy_head_grad_s13_kernel(
             nc.vector.tensor_tensor(
                 out=xg[h][:, c],
                 in0=banks[h, c][:].bitcast(BF16).rearrange("p u (r e) -> p r u e", e=2),
-                in1=xs_full[c][:].rearrange("p r (u e) -> p r u e", e=2),
+                in1=xs[:, c].unsqueeze(1).to_broadcast([P, 2 * P, 2, 2]),
                 op=MULT,
             )
 
@@ -275,19 +271,12 @@ def tile_clipped_policy_head_grad_s13_kernel(
                 stop=(g == GROUPS - 1),
             )
 
-        def do_w_interleave(c):
-            for half in range(2):
-                bank = psum_o.tile([P, A_HALF, 4], BF16, name=f"acc{2 * c + half}")
-                for q in range(2):
-                    cols = slice(half * A_HALF + q * P, half * A_HALF + (q + 1) * P)
-                    nc.tensor.matmul(
-                        bank[:, q * P : (q + 1) * P, :].rearrange("p n j -> p (n j)"),
-                        lhsT=ident_bf[:],
-                        rhs=w_raw[c][:, :, cols].rearrange("p j n -> p n j"),
-                        start=True,
-                        stop=True,
-                    )
-                nc.scalar.copy(out=w_int[c][:, half * A_HALF : (half + 1) * A_HALF, :], in_=bank[:])
+        def do_w_interleave(c, half, engine):
+            interleave(
+                engine,
+                w_int[c][:, half * A_HALF : (half + 1) * A_HALF, :],
+                w_raw[c][half][:].rearrange("p j n -> p n j"),
+            )
 
         def do_quant_w(c):
             nc.vector.quantize_mx(
@@ -298,18 +287,15 @@ def tile_clipped_policy_head_grad_s13_kernel(
         accs = []
 
         do_cast(0)
-        spread = [
-            xs[:, c].rearrange("p u e -> p (u e)").unsqueeze(1).to_broadcast([P, 2 * P, 4]) for c in range(X_PASSES)
-        ]
-        nc.vector.tensor_copy(out=xs_full[0][:], in_=spread[0])
-        nc.scalar.copy(out=xs_full[1][:], in_=spread[1])
         do_transposes(0, 0)
         do_transposes(0, 1)
+        do_w_interleave(1, 0, "vector")
+        do_w_interleave(1, 1, "scalar")
         nc.vector.tensor_copy(out=wt[:], in_=wt_raw[:])
         do_diags("diags", range(0, 3))
         do_cast(1)
-        do_w_interleave(1)
-        do_w_interleave(0)
+        for half in range(2):
+            do_w_interleave(0, half, "scalar")
 
         for h in range(HALVES):
             if h == 6:
@@ -317,7 +303,10 @@ def tile_clipped_policy_head_grad_s13_kernel(
             if h >= 6:
                 for m in range(2 * (h % 2), 2 * (h % 2) + 2):
                     do_out(accs[m], m, (h - 6) // 2)
-            if h >= 2:
+            if h == 1:
+                for early in range(2):
+                    do_aw(early, 1, psum_o, f"acc{early}")
+            if h >= 4:
                 do_aw(h - 2, 1, psum_z, "zt")
             if 4 <= h < HALVES - 1:
                 do_interleave((h - 4) // 2, "scalar", A_HALF * (h % 2), A_HALF * (h % 2 + 1))
@@ -341,9 +330,8 @@ def tile_clipped_policy_head_grad_s13_kernel(
                 if (h, c) == (1, 0):
                     do_quant_w(0)
                     do_diags("w_int0", range(4, 5))
-                do_transposes(h + 1, c)
-                if (h, c) == (1, 0):
                     do_logits(0, (0,))
+                do_transposes(h + 1, c)
             if h >= 2:
                 do_residual(h - 2, 1)
             if h == HALVES - 1:
@@ -352,10 +340,10 @@ def tile_clipped_policy_head_grad_s13_kernel(
                     do_out(accs[EARLY], EARLY, g)
             if h >= 1:
                 do_logits(h - 1, (1,))
-            do_quant_x(h)
             if h == 0:
                 do_quant_w(1)
                 do_diags("w_int1", range(3, 4))
+            do_quant_x(h)
             if h >= 5 and h % 2 == 1:
                 do_quant_g((h - 5) // 2)
 

@@ -60,7 +60,7 @@ def tile_clipped_policy_head_grad_s13_kernel(
         g_scales = [keep.tile([P, A], U8, align_bytes=64, name=f"g_scales{g}") for g in range(GROUPS)]
         hs = keep.tile([P, GROUPS, D // 4], I32, align_bytes=64, name="hs")
         xs = keep.tile([P, X_PASSES, 2, 2], F32, align_bytes=64, name="xs")
-        wt_raw = keep.tile([P, GROUPS, 4], BF16, align_bytes=64, name="wt_raw")
+        wt_rows = keep.tile([P, K_PASS], BF16, align_bytes=64, name="wt_rows")
         wt = keep.tile([P, GROUPS, 4], F32, align_bytes=64, name="wt")
         warm = keep.tile([P, 1], F32, align_bytes=64, name="warm")
         ident = keep.tile([P, P], F32, align_bytes=64, name="ident")
@@ -86,6 +86,7 @@ def tile_clipped_policy_head_grad_s13_kernel(
 
         nc.vector.memset(warm[:], 0.0)
         nc.scalar.activation(out=warm[:], in_=warm[:], func=SIGMOID)
+        nc.vector.memset(wt_rows[:], 0.0)
         make_identity(nc, ident[:])
         nc.vector.memset(hs[:], 0)
         nc.vector.tensor_copy(out=ident_bf[:], in_=ident[:])
@@ -96,9 +97,9 @@ def tile_clipped_policy_head_grad_s13_kernel(
             in_=x_scale.rearrange("o (c p t) -> p (o c) t", p=P, t=4),
         )
         load_w(1)
-        nc.sync.dma_start(out=wt_raw[:], in_=weight.rearrange("(g p t) -> p g t", p=P, t=4))
         load_x(1)
         load_w(0)
+        nc.sync.dma_start(out=wt_rows[:GROUPS, :], in_=weight.rearrange("(g k) -> g k", k=K_PASS))
         load_x(2)
         load_x(3)
         load_act(0)
@@ -211,6 +212,12 @@ def tile_clipped_policy_head_grad_s13_kernel(
                 for b, t in enumerate(ts):
                     diag[g, t] = tile[:, a, b, :]
 
+        def do_diags_scalar(g):
+            for t in (1, 3):
+                tile = keep.tile([P, P], BF16, align_bytes=64, name=f"diag{g}_{t}")
+                nc.scalar.activation(out=tile[:], in_=ident_bf[:], func=COPY, scale=wt[:, g, t : t + 1])
+                diag[g, t] = tile[:]
+
         def do_aw(h, i, pool, name):
             g, t = h // 2, 2 * (h % 2) + i
             aw[h, i] = pool.tile([P, A], F32, name=name)
@@ -289,11 +296,16 @@ def tile_clipped_policy_head_grad_s13_kernel(
         do_cast(0)
         do_transposes(0, 0)
         do_transposes(0, 1)
+        turned = psum_z.tile([P, 2, P], F32, name="zt")
+        for u in range(2):
+            nc.tensor.transpose(turned[:, u, :], wt_rows[:].bitcast(F32)[:, u::2], ident[:])
         do_w_interleave(1, 0, "vector")
         do_w_interleave(1, 1, "scalar")
-        nc.vector.tensor_copy(out=wt[:], in_=wt_raw[:])
-        do_diags("diags", range(0, 3))
         do_cast(1)
+        nc.scalar.copy(
+            out=wt[:].rearrange("p g (u e) -> p g u e", e=2),
+            in_=turned[:].bitcast(BF16).rearrange("p u (g e) -> p g u e", e=2)[:, :GROUPS],
+        )
         for half in range(2):
             do_w_interleave(0, half, "scalar")
 
@@ -318,6 +330,11 @@ def tile_clipped_policy_head_grad_s13_kernel(
             if h == HALVES - 1:
                 do_aw_sbuf(h, 0, "scalar")
             do_cast(h + 2)
+            if h == 2:
+                do_diags_scalar(2)
+            if h == 3:
+                do_diags_scalar(3)
+                do_diags_scalar(4)
             if h == HALVES - 2:
                 do_interleave(GROUPS - 3, "scalar", A_HALF, A)
             for c in range(X_PASSES):
@@ -329,7 +346,7 @@ def tile_clipped_policy_head_grad_s13_kernel(
                         do_pool_residual(h - 2, f"gi{(h // 2 - 1) % 2}" if h >= 6 and h % 2 == 0 else f"xg{(h - 1) % 2}")
                 if (h, c) == (1, 0):
                     do_quant_w(0)
-                    do_diags("w_int0", range(4, 5))
+                    do_diags("w_int0", range(1, 2))
                     do_logits(0, (0,))
                 do_transposes(h + 1, c)
             if h >= 2:
@@ -342,7 +359,7 @@ def tile_clipped_policy_head_grad_s13_kernel(
                 do_logits(h - 1, (1,))
             if h == 0:
                 do_quant_w(1)
-                do_diags("w_int1", range(3, 4))
+                do_diags("w_int1", range(0, 1))
             do_quant_x(h)
             if h >= 5 and h % 2 == 1:
                 do_quant_g((h - 5) // 2)

@@ -28,6 +28,7 @@ X_PASSES = D // K_PASS
 M_TILES = D // P
 EARLY = 4
 A_HALF = A // 2
+W_POOL = 384
 TAIL_SCALAR = 176
 
 
@@ -49,10 +50,7 @@ def tile_clipped_policy_head_grad_s13_kernel(
         x_raw = [keep.tile([P, 2 * D], U8, align_bytes=64, name=f"x_raw{h}") for h in range(HALVES)]
         act = [keep.tile([P, 4, A], BF16, align_bytes=64, name=f"act{g}") for g in range(GROUPS)]
         hw = [keep.tile([P, 2 * D], U8, align_bytes=64, name=f"hw{g}") for g in range(GROUPS)]
-        w_raw = [
-            [keep.tile([P, 4, A_HALF], BF16, align_bytes=64, name=f"w_raw{c}_{half}") for half in range(2)]
-            for c in range(X_PASSES)
-        ]
+        w_raw = [keep.tile([P, 4, A], BF16, align_bytes=64, name=f"w_raw{c}") for c in range(X_PASSES)]
         w_int = [keep.tile([P, A, 4], BF16, align_bytes=64, name=f"w_int{c}") for c in range(X_PASSES)]
         w_codes = [keep.tile([P, A], U32, align_bytes=64, name=f"w_codes{c}") for c in range(X_PASSES)]
         w_scales = [keep.tile([P, A], U8, align_bytes=64, name=f"w_scales{c}") for c in range(X_PASSES)]
@@ -72,14 +70,13 @@ def tile_clipped_policy_head_grad_s13_kernel(
             nc.sync.dma_start(out=x_raw[h][:], in_=src[:, lo * D : (lo + 2) * D])
 
         def load_w(c):
-            rows = w[c * K_PASS : (c + 1) * K_PASS, :].rearrange("(p j) n -> p j n", j=4)
-            for half in range(2):
-                nc.sync.dma_start(out=w_raw[c][half][:], in_=rows[:, :, half * A_HALF : (half + 1) * A_HALF])
-
-        def load_act(g):
             nc.sync.dma_start(
-                out=act[g][:], in_=action[g * K_PASS : (g + 1) * K_PASS, :].rearrange("(p t) a -> p t a", t=4)
+                out=w_raw[c][:], in_=w[c * K_PASS : (c + 1) * K_PASS, :].rearrange("(p j) n -> p j n", j=4)
             )
+
+        def load_act(g, lo=0, hi=4):
+            rows = action[g * K_PASS : (g + 1) * K_PASS, :].rearrange("(p t) a -> p t a", t=4)
+            nc.sync.dma_start(out=act[g][:, lo:hi, :], in_=rows[:, lo:hi, :])
 
         def load_h(g):
             nc.sync.dma_start(out=hw[g][:], in_=h_words[g])
@@ -96,13 +93,14 @@ def tile_clipped_policy_head_grad_s13_kernel(
             out=xs[:].rearrange("p c u e -> p c (u e)"),
             in_=x_scale.rearrange("o (c p t) -> p (o c) t", p=P, t=4),
         )
-        load_w(1)
         load_x(1)
-        load_w(0)
         nc.sync.dma_start(out=wt_rows[:GROUPS, :], in_=weight.rearrange("(g k) -> g k", k=K_PASS))
+        load_w(1)
         load_x(2)
+        load_w(0)
         load_x(3)
-        load_act(0)
+        load_act(0, 0, 2)
+        load_act(0, 2, 4)
         load_x(4)
         load_x(5)
         load_act(1)
@@ -198,22 +196,8 @@ def tile_clipped_policy_head_grad_s13_kernel(
                 if (h, i) != (HALVES - 2, 1):
                     do_sigmoid(h, i)
 
-        def do_diags(tag, groups):
-            ts = range(1, 4, 2)
-            shape = [P, len(groups), len(ts), P]
-            tile = keep.tile(shape, BF16, align_bytes=64, name="diags", tag=tag)
-            nc.gpsimd.tensor_tensor(
-                out=tile[:],
-                in0=ident_bf[:].unsqueeze(1).unsqueeze(1).to_broadcast(shape),
-                in1=wt[:, groups.start : groups.stop, 1:4:2].unsqueeze(3).to_broadcast(shape),
-                op=MULT,
-            )
-            for a, g in enumerate(groups):
-                for b, t in enumerate(ts):
-                    diag[g, t] = tile[:, a, b, :]
-
-        def do_diags_scalar(g):
-            for t in (1, 3):
+        def do_diags_scalar(g, tiles=(1, 3)):
+            for t in tiles:
                 tile = keep.tile([P, P], BF16, align_bytes=64, name=f"diag{g}_{t}")
                 nc.scalar.activation(out=tile[:], in_=ident_bf[:], func=COPY, scale=wt[:, g, t : t + 1])
                 diag[g, t] = tile[:]
@@ -278,12 +262,8 @@ def tile_clipped_policy_head_grad_s13_kernel(
                 stop=(g == GROUPS - 1),
             )
 
-        def do_w_interleave(c, half, engine):
-            interleave(
-                engine,
-                w_int[c][:, half * A_HALF : (half + 1) * A_HALF, :],
-                w_raw[c][half][:].rearrange("p j n -> p n j"),
-            )
+        def do_w_interleave(c, engine, lo, hi):
+            interleave(engine, w_int[c][:, lo:hi, :], w_raw[c][:, :, lo:hi].rearrange("p j n -> p n j"))
 
         def do_quant_w(c):
             nc.vector.quantize_mx(
@@ -294,30 +274,42 @@ def tile_clipped_policy_head_grad_s13_kernel(
         accs = []
 
         do_cast(0)
-        do_transposes(0, 0)
-        do_transposes(0, 1)
+        for c in range(X_PASSES):
+            do_transposes(0, c)
         turned = psum_z.tile([P, 2, P], F32, name="zt")
         for u in range(2):
             nc.tensor.transpose(turned[:, u, :], wt_rows[:].bitcast(F32)[:, u::2], ident[:])
-        do_w_interleave(1, 0, "vector")
-        do_w_interleave(1, 1, "scalar")
         do_cast(1)
+        do_w_interleave(1, "gpsimd", 0, W_POOL)
+        do_w_interleave(1, "scalar", W_POOL, A)
         nc.scalar.copy(
             out=wt[:].rearrange("p g (u e) -> p g u e", e=2),
             in_=turned[:].bitcast(BF16).rearrange("p u (g e) -> p g u e", e=2)[:, :GROUPS],
         )
-        for half in range(2):
-            do_w_interleave(0, half, "scalar")
+        do_cast(2)
+        do_diags_scalar(0, (1, 2, 3))
+        for c in range(X_PASSES):
+            do_scale(0, c)
+            do_transposes(1, c)
+        do_w_interleave(0, "scalar", 0, A)
+        for c in range(X_PASSES):
+            do_scale(1, c)
+            do_transposes(2, c)
+        do_quant_w(1)
+        do_quant_x(0)
+        do_quant_x(1)
+        do_quant_w(0)
+        do_cast(3)
+        for t in (1, 2, 3):
+            do_aw(t // 2, t % 2, psum_o, f"acc{t}")
+        do_logits(0, (0, 1))
 
-        for h in range(HALVES):
+        for h in range(2, HALVES):
             if h == 6:
                 accs.extend(psum_o.tile([P, A], F32, name=f"acc{m}") for m in range(EARLY))
             if h >= 6:
                 for m in range(2 * (h % 2), 2 * (h % 2) + 2):
                     do_out(accs[m], m, (h - 6) // 2)
-            if h == 1:
-                for early in range(2):
-                    do_aw(early, 1, psum_o, f"acc{early}")
             if h >= 4:
                 do_aw(h - 2, 1, psum_z, "zt")
             if 4 <= h < HALVES - 1:
@@ -325,41 +317,34 @@ def tile_clipped_policy_head_grad_s13_kernel(
             if h == HALVES - 1:
                 for i in range(2):
                     do_aw_sbuf(h - 1, i, "scalar")
-            if h >= 2:
+            if h >= 3:
                 do_logits(h - 1, (0,))
             if h == HALVES - 1:
                 do_aw_sbuf(h, 0, "scalar")
             do_cast(h + 2)
-            if h == 2:
-                do_diags_scalar(2)
-            if h == 3:
-                do_diags_scalar(3)
-                do_diags_scalar(4)
+            if h < 4:
+                for g in (2 * h - 3, 2 * h - 2):
+                    do_diags_scalar(g)
             if h == HALVES - 2:
                 do_interleave(GROUPS - 3, "scalar", A_HALF, A)
             for c in range(X_PASSES):
                 do_scale(h, c)
-                if c == 0 and h >= 2:
+                if c == 0:
                     if h % 2 == 0:
                         gp[h // 2 - 1] = two.tile([P, 4, A], BF16, align_bytes=64, name="gp")
-                    if h >= 2:
-                        do_pool_residual(h - 2, f"gi{(h // 2 - 1) % 2}" if h >= 6 and h % 2 == 0 else f"xg{(h - 1) % 2}")
-                if (h, c) == (1, 0):
-                    do_quant_w(0)
-                    do_diags("w_int0", range(1, 2))
-                    do_logits(0, (0,))
+                    if h >= 3:
+                        do_pool_residual(h - 2 if h > 3 else 0, f"gi{(h // 2 - 1) % 2}" if h >= 6 and h % 2 == 0 else f"xg{(h - 1) % 2}")
                 do_transposes(h + 1, c)
-            if h >= 2:
+            if h == 3:
+                do_residual(0, 1)
+                do_residual(1, 0)
+            if h >= 3:
                 do_residual(h - 2, 1)
             if h == HALVES - 1:
                 accs.append(psum_t.tile([P, A], F32, name="bank"))
                 for g in range(GROUPS - 3):
                     do_out(accs[EARLY], EARLY, g)
-            if h >= 1:
-                do_logits(h - 1, (1,))
-            if h == 0:
-                do_quant_w(1)
-                do_diags("w_int1", range(0, 1))
+            do_logits(h - 1, (0, 1) if h == 2 else (1,))
             do_quant_x(h)
             if h >= 5 and h % 2 == 1:
                 do_quant_g((h - 5) // 2)

@@ -60,7 +60,6 @@ def tile_clipped_policy_head_grad_s13_kernel(
         xs = keep.tile([P, X_PASSES, 2, 2], F32, align_bytes=64, name="xs")
         wt_rows = keep.tile([P, K_PASS], BF16, align_bytes=64, name="wt_rows")
         wt = keep.tile([P, GROUPS, 4], F32, align_bytes=64, name="wt")
-        warm = keep.tile([P, 1], F32, align_bytes=64, name="warm")
         ident = keep.tile([P, P], F32, align_bytes=64, name="ident")
         ident_bf = keep.tile([P, P], BF16, align_bytes=64, name="ident_bf")
 
@@ -81,8 +80,6 @@ def tile_clipped_policy_head_grad_s13_kernel(
         def load_h(g):
             nc.sync.dma_start(out=hw[g][:], in_=h_words[g])
 
-        nc.vector.memset(warm[:], 0.0)
-        nc.scalar.activation(out=warm[:], in_=warm[:], func=SIGMOID)
         nc.vector.memset(wt_rows[:], 0.0)
         make_identity(nc, ident[:])
         nc.vector.memset(hs[:], 0)

@@ -27,9 +27,13 @@ HALVES = 2 * GROUPS
 X_PASSES = D // K_PASS
 M_TILES = D // P
 EARLY = 4
-A_HALF = A // 2
-W_POOL = 384
+W_POOL = 256
 TAIL_SCALAR = 176
+TAIL_A = 256
+STEADY = 5
+G_FIRST = 192
+CAST_BUFS = 6
+OUT_BANK = (4, 5, 6, 7, 2, 3, 0, 1)
 
 
 def tile_clipped_policy_head_grad_s13_kernel(
@@ -42,9 +46,7 @@ def tile_clipped_policy_head_grad_s13_kernel(
         two = ctx.enter_context(tc.tile_pool(name="two", bufs=2))
         three = ctx.enter_context(tc.tile_pool(name="three", bufs=3))
         four = ctx.enter_context(tc.tile_pool(name="four", bufs=4))
-        psum_t = ctx.enter_context(tc.psum_pool(name="psum_t", bufs=2))
-        psum_z = ctx.enter_context(tc.psum_pool(name="psum_z", bufs=2))
-        psum_o = ctx.enter_context(tc.psum_pool(name="psum_o", bufs=1))
+        psum = ctx.enter_context(tc.psum_pool(name="psum", bufs=1))
         ctx.enter_context(tc.manual_schedule())
 
         x_raw = [keep.tile([P, 2 * D], U8, align_bytes=64, name=f"x_raw{h}") for h in range(HALVES)]
@@ -58,10 +60,9 @@ def tile_clipped_policy_head_grad_s13_kernel(
         g_scales = [keep.tile([P, A], U8, align_bytes=64, name=f"g_scales{g}") for g in range(GROUPS)]
         hs = keep.tile([P, GROUPS, D // 4], I32, align_bytes=64, name="hs")
         xs = keep.tile([P, X_PASSES, 2, 2], F32, align_bytes=64, name="xs")
-        wt_rows = keep.tile([P, K_PASS], BF16, align_bytes=64, name="wt_rows")
+        wt_bf = keep.tile([P, GROUPS, 4], BF16, align_bytes=64, name="wt_bf")
         wt = keep.tile([P, GROUPS, 4], F32, align_bytes=64, name="wt")
         ident = keep.tile([P, P], F32, align_bytes=64, name="ident")
-        ident_bf = keep.tile([P, P], BF16, align_bytes=64, name="ident_bf")
 
         def load_x(h):
             g, lo = h // 2, 2 * (h % 2)
@@ -73,45 +74,46 @@ def tile_clipped_policy_head_grad_s13_kernel(
                 out=w_raw[c][:], in_=w[c * K_PASS : (c + 1) * K_PASS, :].rearrange("(p j) n -> p j n", j=4)
             )
 
-        def load_act(g, lo=0, hi=4):
+        def load_act(g):
             rows = action[g * K_PASS : (g + 1) * K_PASS, :].rearrange("(p t) a -> p t a", t=4)
-            nc.sync.dma_start(out=act[g][:, lo:hi, :], in_=rows[:, lo:hi, :])
+            nc.sync.dma_start(out=act[g][:], in_=rows)
 
         def load_h(g):
             nc.sync.dma_start(out=hw[g][:], in_=h_words[g])
 
-        nc.vector.memset(wt_rows[:], 0.0)
         make_identity(nc, ident[:])
         nc.vector.memset(hs[:], 0)
-        nc.vector.tensor_copy(out=ident_bf[:], in_=ident[:])
 
         load_x(0)
         nc.sync.dma_start(
             out=xs[:].rearrange("p c u e -> p c (u e)"),
             in_=x_scale.rearrange("o (c p t) -> p (o c) t", p=P, t=4),
         )
-        load_x(1)
-        nc.sync.dma_start(out=wt_rows[:GROUPS, :], in_=weight.rearrange("(g k) -> g k", k=K_PASS))
-        load_w(1)
-        load_x(2)
         load_w(0)
+        load_x(1)
+        load_w(1)
+        nc.sync.dma_start(out=wt_bf[:], in_=weight.rearrange("(g p t) -> p g t", p=P, t=4))
+        load_x(2)
+        load_act(0)
         load_x(3)
-        load_act(0, 0, 2)
-        load_act(0, 2, 4)
         load_x(4)
         load_x(5)
         load_act(1)
+        load_x(6)
+        load_x(7)
         scales_src = h_scales.bitcast(I32).rearrange("g (q r) n -> r q g n", r=4)
         for r in range(4):
             nc.sync.dma_start(out=hs[r:P:32, :, :], in_=scales_src[r])
-        for g in range(GROUPS):
-            if g + 3 < GROUPS:
-                load_x(2 * g + 6)
-            load_h(g)
+        load_h(0)
+        load_act(2)
+        for h in range(8, HALVES):
+            load_x(h)
+        load_act(GROUPS - 1)
+        load_h(1)
+        for g in range(2, GROUPS):
             if g + 2 < GROUPS:
-                load_act(g + 2)
-            if g + 3 < GROUPS:
-                load_x(2 * g + 7)
+                load_act(g + 1)
+            load_h(g)
 
         cast = {}
         banks = {}
@@ -124,11 +126,12 @@ def tile_clipped_policy_head_grad_s13_kernel(
         aw = {}
         gp = {}
         gi = {}
+        accs = {}
 
         def do_cast(h):
             if h >= HALVES:
                 return
-            cast[h] = three.tile([P, 2 * D], BF16, align_bytes=64, name="cast")
+            cast[h] = one.tile([P, 2 * D], BF16, align_bytes=64, name="cast", bufs=CAST_BUFS)
             if h == 0:
                 for c in range(X_PASSES):
                     lo = slice(c * K_PASS, (c + 1) * K_PASS)
@@ -138,10 +141,13 @@ def tile_clipped_policy_head_grad_s13_kernel(
             else:
                 nc.scalar.copy(out=cast[h][:], in_=x_raw[h][:].bitcast(FP8))
 
+        def turn_bank(h, c):
+            return (c + max(h - STEADY, 0)) % 2
+
         def do_transposes(h, c):
             if h >= HALVES:
                 return
-            bank = psum_t.tile([P, 2, 2 * P], F32, name="bank")
+            bank = psum.tile([P, 2, 2 * P], F32, name="turned", tag=f"bank{turn_bank(h, c)}")
             banks[h, c] = bank
             for i in range(2):
                 words = cast[h][:, i * D : (i + 1) * D].bitcast(F32)
@@ -151,7 +157,7 @@ def tile_clipped_policy_head_grad_s13_kernel(
                     )
 
         def do_scale(h, c):
-            if c == 0:
+            if h not in xg:
                 xg[h] = one.tile([P, X_PASSES, 2 * P, 2, 2], BF16, align_bytes=64, name="xg", tag=f"xg{h % 2}")
             nc.vector.tensor_tensor(
                 out=xg[h][:, c],
@@ -169,8 +175,8 @@ def tile_clipped_policy_head_grad_s13_kernel(
                 in_=xg[h][:].rearrange("p c r u e -> p (c r u e)"),
             )
 
-        def do_z(h, i, pool, name):
-            zt = pool.tile([P, A], F32, name=name)
+        def do_z(h, i, bank):
+            zt = psum.tile([P, A], F32, name="zt", tag=f"bank{bank}")
             z[h, i] = zt
             for c in range(X_PASSES):
                 nc.tensor.matmul_mx(
@@ -184,24 +190,21 @@ def tile_clipped_policy_head_grad_s13_kernel(
                 )
 
         def do_sigmoid(h, i):
-            sig[h, i] = four.tile([P, A], F32, align_bytes=64, name="sig")
+            if i == 0:
+                sig[h, i] = three.tile([P, A], F32, align_bytes=64, name="sig")
+            else:
+                sig[h, i] = one.tile([P, A], F32, align_bytes=64, name="sig", tag=f"sig{h % 3}")
             nc.scalar.activation(out=sig[h, i][:], in_=z[h, i][:], func=SIGMOID)
 
-        def do_logits(h, tiles):
-            for i in tiles:
-                do_z(h, i, psum_z, "zt")
-                if (h, i) != (HALVES - 2, 1):
-                    do_sigmoid(h, i)
+        def do_diag(h):
+            g, t = h // 2, 2 * (h % 2) + 1
+            tile = keep.tile([P, P], BF16, align_bytes=64, name=f"diag{h}")
+            nc.scalar.activation(out=tile[:], in_=ident[:], func=COPY, scale=wt[:, g, t : t + 1])
+            diag[g, t] = tile[:]
 
-        def do_diags_scalar(g, tiles=(1, 3)):
-            for t in tiles:
-                tile = keep.tile([P, P], BF16, align_bytes=64, name=f"diag{g}_{t}")
-                nc.scalar.activation(out=tile[:], in_=ident_bf[:], func=COPY, scale=wt[:, g, t : t + 1])
-                diag[g, t] = tile[:]
-
-        def do_aw(h, i, pool, name):
+        def do_aw(h, i, bank):
             g, t = h // 2, 2 * (h % 2) + i
-            aw[h, i] = pool.tile([P, A], F32, name=name)
+            aw[h, i] = psum.tile([P, A], F32, name="aw", tag=f"bank{bank}")
             nc.tensor.matmul(aw[h, i][:], lhsT=diag[g, t], rhs=act[g][:, t, :], start=True, stop=True)
 
         def do_residual(h, i):
@@ -219,15 +222,10 @@ def tile_clipped_policy_head_grad_s13_kernel(
                 out=gp[g][:, t, :], in0=part[:], scalar1=wt[:, g, t : t + 1], scalar2=0.0, op0=MULT, op1=ADD
             )
 
-        def do_aw_sbuf(h, i, engine):
+        def do_aw_sbuf(h, i):
             g, t = h // 2, 2 * (h % 2) + i
             aw[h, i] = four.tile([P, A], F32, align_bytes=64, name="aw_sbuf")
-            if engine == "scalar":
-                nc.scalar.activation(out=aw[h, i][:], in_=act[g][:, t, :], func=COPY, scale=wt[:, g, t : t + 1])
-            else:
-                nc.vector.tensor_scalar(
-                    out=aw[h, i][:], in0=act[g][:, t, :], scalar1=wt[:, g, t : t + 1], scalar2=None, op0=MULT
-                )
+            nc.scalar.activation(out=aw[h, i][:], in_=act[g][:, t, :], func=COPY, scale=wt[:, g, t : t + 1])
 
         def interleave(engine, dst, src):
             if engine == "vector":
@@ -248,9 +246,11 @@ def tile_clipped_policy_head_grad_s13_kernel(
                 in_=gi[g][:].rearrange("p a t -> p (a t)"),
             )
 
-        def do_out(acc, m, g):
+        def do_out(m, g):
+            if g == 0:
+                accs[m] = psum.tile([P, A], F32, name="acc", tag=f"bank{OUT_BANK[m]}")
             nc.tensor.matmul_mx(
-                out=acc[:],
+                out=accs[m][:],
                 lhsT=hw[g][:, 2 * P * m : 2 * P * (m + 1)].bitcast(FP4X4),
                 lhsT_scale=hs[:, g, 32 * m : 32 * (m + 1)].bitcast(U8),
                 rhs=g_codes[g][:].bitcast(FP8X4),
@@ -268,111 +268,111 @@ def tile_clipped_policy_head_grad_s13_kernel(
                 in_=w_int[c][:].rearrange("p n j -> p (n j)"),
             )
 
-        accs = []
+        last = GROUPS - 1
 
         do_cast(0)
+        do_w_interleave(0, "vector", 0, A)
         for c in range(X_PASSES):
             do_transposes(0, c)
-        turned = psum_z.tile([P, 2, P], F32, name="zt")
-        for u in range(2):
-            nc.tensor.transpose(turned[:, u, :], wt_rows[:].bitcast(F32)[:, u::2], ident[:])
         do_cast(1)
         do_w_interleave(1, "gpsimd", 0, W_POOL)
         do_w_interleave(1, "scalar", W_POOL, A)
-        nc.scalar.copy(
-            out=wt[:].rearrange("p g (u e) -> p g u e", e=2),
-            in_=turned[:].bitcast(BF16).rearrange("p u (g e) -> p g u e", e=2)[:, :GROUPS],
-        )
         do_cast(2)
-        do_diags_scalar(0, (1, 2, 3))
+        nc.scalar.copy(out=wt[:], in_=wt_bf[:])
         for c in range(X_PASSES):
             do_scale(0, c)
             do_transposes(1, c)
-        do_w_interleave(0, "scalar", 0, A)
+        do_quant_w(0)
+        do_quant_x(0)
+        do_quant_w(1)
+        do_cast(3)
+        for i in range(2):
+            do_z(0, i, 2 + i)
+            do_sigmoid(0, i)
+        do_diag(0)
         for c in range(X_PASSES):
             do_scale(1, c)
             do_transposes(2, c)
-        do_quant_w(1)
-        do_quant_x(0)
+        do_aw(0, 1, 4)
         do_quant_x(1)
-        do_quant_w(0)
-        do_cast(3)
-        for t in (1, 2, 3):
-            do_aw(t // 2, t % 2, psum_o, f"acc{t}")
-        do_logits(0, (0, 1))
 
         for h in range(2, HALVES):
-            if h == 6:
-                accs.extend(psum_o.tile([P, A], F32, name=f"acc{m}") for m in range(EARLY))
-            if h >= 6:
-                for m in range(2 * (h % 2), 2 * (h % 2) + 2):
-                    do_out(accs[m], m, (h - 6) // 2)
-            if h >= 4:
-                do_aw(h - 2, 1, psum_z, "zt")
-            if 4 <= h < HALVES - 1:
-                do_interleave((h - 4) // 2, "scalar", A_HALF * (h % 2), A_HALF * (h % 2 + 1))
-            if h == HALVES - 1:
-                for i in range(2):
-                    do_aw_sbuf(h - 1, i, "scalar")
-            if h >= 3:
-                do_logits(h - 1, (0,))
-            if h == HALVES - 1:
-                do_aw_sbuf(h, 0, "scalar")
-            do_cast(h + 2)
+            steady = h >= STEADY
+            early = [(m, (h - 5) // 2) for m in range(2 * (1 - h % 2), 2 * (1 - h % 2) + 2) if steady]
+            if h % 2 == 0:
+                gp[h // 2 - 1] = two.tile([P, 4, A], BF16, align_bytes=64, name="gp")
             if h < 4:
-                for g in (2 * h - 3, 2 * h - 2):
-                    do_diags_scalar(g)
-            if h == HALVES - 2:
-                do_interleave(GROUPS - 3, "scalar", A_HALF, A)
-            for c in range(X_PASSES):
-                do_scale(h, c)
-                if c == 0:
-                    if h % 2 == 0:
-                        gp[h // 2 - 1] = two.tile([P, 4, A], BF16, align_bytes=64, name="gp")
-                    if h >= 3:
-                        do_pool_residual(h - 2 if h > 3 else 0, f"gi{(h // 2 - 1) % 2}" if h >= 6 and h % 2 == 0 else f"xg{(h - 1) % 2}")
-                do_transposes(h + 1, c)
-            if h == 3:
-                do_residual(0, 1)
-                do_residual(1, 0)
-            if h >= 3:
+                do_cast(2 * h)
+            elif h % 2 == 1:
+                do_cast((h + 13) // 2)
+            do_z(h - 1, 0, 2)
+            do_sigmoid(h - 1, 0)
+            if steady:
+                do_z(h - 1, 1, 3)
+                do_sigmoid(h - 1, 1)
+            if h < HALVES - 1:
+                do_diag(h - 1)
+            if h < 4:
+                do_cast(2 * h + 1)
+            if h in (5, 7, 9, 10):
+                do_aw_sbuf(HALVES - 2 + (h > 8), (h // 2) % 2)
+            do_scale(h, 0)
+            do_pool_residual(h - 2, f"xg{(h - 1) % 2}" if h == 2 or (h >= 5 and h % 2 == 1) else f"sig{h % 3}")
+            if steady:
+                if h % 2 == 1:
+                    do_out(*early.pop())
+                if h > STEADY:
+                    do_aw(h - 2, 1, turn_bank(h, 0))
+                for m, g in early:
+                    do_out(m, g)
+                do_scale(h, 1)
+                do_transposes(h + 1, 0)
                 do_residual(h - 2, 1)
-            if h == HALVES - 1:
-                accs.append(psum_t.tile([P, A], F32, name="bank"))
-                for g in range(GROUPS - 3):
-                    do_out(accs[EARLY], EARLY, g)
-            do_logits(h - 1, (0, 1) if h == 2 else (1,))
+                do_transposes(h + 1, 1)
+            else:
+                do_transposes(h + 1, 0)
+                do_z(h - 1, 1, 3)
+                do_sigmoid(h - 1, 1)
+                do_scale(h, 1)
+                do_transposes(h + 1, 1)
+                do_aw(h - 1, 1, 3 + h)
+                do_residual(h - 2, 1)
+            if h == 4:
+                do_cast(8)
+            if h % 2 == 1:
+                do_interleave((h - 3) // 2, "scalar", 0, A if h < HALVES - 1 else TAIL_A)
             do_quant_x(h)
-            if h >= 5 and h % 2 == 1:
-                do_quant_g((h - 5) // 2)
+            if h >= 4 and h % 2 == 0:
+                do_quant_g((h - 4) // 2)
 
-        last = GROUPS - 1
         gp[last] = two.tile([P, 4, A], BF16, align_bytes=64, name="gp")
-        do_interleave(last - 1, "scalar", 0, A_HALF)
-        do_z(HALVES - 1, 0, psum_z, "zt")
-        do_z(HALVES - 1, 1, psum_t, "bank")
-        do_sigmoid(HALVES - 2, 1)
+        for m in (2, 3):
+            do_out(m, last - 2)
+        for g in range(last - 1):
+            do_out(EARLY, g)
         for i in range(2):
+            do_z(HALVES - 1, i, i)
             do_sigmoid(HALVES - 1, i)
-        do_interleave(last - 1, "scalar", A_HALF, A)
+        for g in range(last - 1):
+            do_out(EARLY + 1, g)
         do_residual(HALVES - 2, 0)
-        do_aw_sbuf(HALVES - 1, 1, "vector")
+        do_interleave(last - 1, "vector", TAIL_A, A)
         do_residual(HALVES - 2, 1)
+        do_quant_g(last - 1)
         for i in range(2):
             do_residual(HALVES - 1, i)
-        for m in range(EARLY + 1):
-            do_out(accs[m], m, last - 2)
-        for m, pool, name in ((5, psum_z, "zt"), (6, psum_z, "zt"), (7, psum_t, "bank")):
-            accs.append(pool.tile([P, A], F32, name=name))
-            for g in range(last - 1):
-                do_out(accs[m], m, g)
+        for m in range(EARLY + 2):
+            do_out(m, last - 1)
+        for g in range(last):
+            do_out(EARLY + 2, g)
         do_interleave(last, "scalar", 0, TAIL_SCALAR)
         do_interleave(last, "vector", TAIL_SCALAR, A)
-        do_quant_g(last - 1)
         do_quant_g(last)
         for m in range(M_TILES):
-            do_out(accs[m], m, last - 1)
-            do_out(accs[m], m, last)
+            if m == M_TILES - 1:
+                for g in range(last):
+                    do_out(m, g)
+            do_out(m, last)
             res = keep.tile([P, A], F32, align_bytes=64, name=f"res{m}")
             if m % 2 == 0:
                 nc.vector.tensor_copy(out=res[:], in_=accs[m][:])

@@ -27,12 +27,14 @@ HALVES = 2 * GROUPS
 X_PASSES = D // K_PASS
 M_TILES = D // P
 EARLY = 4
-W_POOL = 256
+W_POOL = 384
+W_FIRST = 160
 TAIL_SCALAR = 176
 TAIL_A = 256
-STEADY = 5
+STEADY = 3
+FIRST_OUT = 5
 G_FIRST = 192
-CAST_BUFS = 6
+CAST_BUFS = 3
 OUT_BANK = (4, 5, 6, 7, 2, 3, 0, 1)
 
 
@@ -60,7 +62,7 @@ def tile_clipped_policy_head_grad_s13_kernel(
         g_scales = [keep.tile([P, A], U8, align_bytes=64, name=f"g_scales{g}") for g in range(GROUPS)]
         hs = keep.tile([P, GROUPS, D // 4], I32, align_bytes=64, name="hs")
         xs = keep.tile([P, X_PASSES, 2, 2], F32, align_bytes=64, name="xs")
-        wt_bf = keep.tile([P, GROUPS, 4], BF16, align_bytes=64, name="wt_bf")
+        wt_rows = keep.tile([P, K_PASS], BF16, align_bytes=64, name="wt_rows")
         wt = keep.tile([P, GROUPS, 4], F32, align_bytes=64, name="wt")
         ident = keep.tile([P, P], F32, align_bytes=64, name="ident")
 
@@ -74,13 +76,14 @@ def tile_clipped_policy_head_grad_s13_kernel(
                 out=w_raw[c][:], in_=w[c * K_PASS : (c + 1) * K_PASS, :].rearrange("(p j) n -> p j n", j=4)
             )
 
-        def load_act(g):
+        def load_act(g, lo=0, hi=4):
             rows = action[g * K_PASS : (g + 1) * K_PASS, :].rearrange("(p t) a -> p t a", t=4)
-            nc.sync.dma_start(out=act[g][:], in_=rows)
+            nc.sync.dma_start(out=act[g][:, lo:hi, :], in_=rows[:, lo:hi, :])
 
         def load_h(g):
             nc.sync.dma_start(out=hw[g][:], in_=h_words[g])
 
+        nc.vector.memset(wt_rows[:], 0.0)
         make_identity(nc, ident[:])
         nc.vector.memset(hs[:], 0)
 
@@ -89,31 +92,27 @@ def tile_clipped_policy_head_grad_s13_kernel(
             out=xs[:].rearrange("p c u e -> p c (u e)"),
             in_=x_scale.rearrange("o (c p t) -> p (o c) t", p=P, t=4),
         )
-        load_w(0)
         load_x(1)
+        load_w(0)
         load_w(1)
-        nc.sync.dma_start(out=wt_bf[:], in_=weight.rearrange("(g p t) -> p g t", p=P, t=4))
+        nc.sync.dma_start(out=wt_rows[:GROUPS, :], in_=weight.rearrange("(g k) -> g k", k=K_PASS))
         load_x(2)
-        load_act(0)
+        load_act(0, 0, 2)
         load_x(3)
         load_x(4)
+        load_act(0, 2, 4)
         load_x(5)
-        load_act(1)
         load_x(6)
-        load_x(7)
+        load_act(1)
         scales_src = h_scales.bitcast(I32).rearrange("g (q r) n -> r q g n", r=4)
         for r in range(4):
             nc.sync.dma_start(out=hs[r:P:32, :, :], in_=scales_src[r])
-        load_h(0)
-        load_act(2)
-        for h in range(8, HALVES):
-            load_x(h)
-        load_act(GROUPS - 1)
-        load_h(1)
-        for g in range(2, GROUPS):
-            if g + 2 < GROUPS:
-                load_act(g + 1)
+        for g in range(GROUPS):
             load_h(g)
+            for h in range(2 * g + 7, min(2 * g + 9, HALVES)):
+                load_x(h)
+            if g + 2 < GROUPS:
+                load_act(g + 2)
 
         cast = {}
         banks = {}
@@ -142,7 +141,7 @@ def tile_clipped_policy_head_grad_s13_kernel(
                 nc.scalar.copy(out=cast[h][:], in_=x_raw[h][:].bitcast(FP8))
 
         def turn_bank(h, c):
-            return (c + max(h - STEADY, 0)) % 2
+            return 2 + c if h == 1 else (c + max(h - STEADY, 0)) % 2
 
         def do_transposes(h, c):
             if h >= HALVES:
@@ -175,10 +174,11 @@ def tile_clipped_policy_head_grad_s13_kernel(
                 in_=xg[h][:].rearrange("p c r u e -> p (c r u e)"),
             )
 
-        def do_z(h, i, bank):
-            zt = psum.tile([P, A], F32, name="zt", tag=f"bank{bank}")
-            z[h, i] = zt
-            for c in range(X_PASSES):
+        def do_z(h, i, bank, passes=range(X_PASSES)):
+            if (h, i) not in z:
+                z[h, i] = psum.tile([P, A], F32, name="zt", tag=f"bank{bank}")
+            zt = z[h, i]
+            for c in passes:
                 nc.tensor.matmul_mx(
                     out=zt[:],
                     lhsT=x_codes[h][:, c, i * P : (i + 1) * P].bitcast(FP8X4),
@@ -196,11 +196,24 @@ def tile_clipped_policy_head_grad_s13_kernel(
                 sig[h, i] = one.tile([P, A], F32, align_bytes=64, name="sig", tag=f"sig{h % 3}")
             nc.scalar.activation(out=sig[h, i][:], in_=z[h, i][:], func=SIGMOID)
 
-        def do_diag(h):
-            g, t = h // 2, 2 * (h % 2) + 1
-            tile = keep.tile([P, P], BF16, align_bytes=64, name=f"diag{h}")
+        def do_diag(h, i):
+            g, t = h // 2, 2 * (h % 2) + i
+            tile = keep.tile([P, P], BF16, align_bytes=64, name=f"diag{h}_{i}")
             nc.scalar.activation(out=tile[:], in_=ident[:], func=COPY, scale=wt[:, g, t : t + 1])
             diag[g, t] = tile[:]
+
+        def do_diags_pool(g_lo, g_hi):
+            n = g_hi - g_lo
+            tile = keep.tile([P, n, 2, P], BF16, align_bytes=64, name="diags", tag="w_int1")
+            nc.gpsimd.tensor_tensor(
+                out=tile[:],
+                in0=ident[:].unsqueeze(1).unsqueeze(1).to_broadcast([P, n, 2, P]),
+                in1=wt[:, g_lo:g_hi, 1::2].unsqueeze(3).to_broadcast([P, n, 2, P]),
+                op=MULT,
+            )
+            for g in range(g_lo, g_hi):
+                for j in range(2):
+                    diag[g, 2 * j + 1] = tile[:, g - g_lo, j, :]
 
         def do_aw(h, i, bank):
             g, t = h // 2, 2 * (h % 2) + i
@@ -271,74 +284,83 @@ def tile_clipped_policy_head_grad_s13_kernel(
         last = GROUPS - 1
 
         do_cast(0)
-        do_w_interleave(0, "vector", 0, A)
         for c in range(X_PASSES):
             do_transposes(0, c)
         do_cast(1)
-        do_w_interleave(1, "gpsimd", 0, W_POOL)
-        do_w_interleave(1, "scalar", W_POOL, A)
+        for c in range(X_PASSES):
+            do_transposes(1, c)
+        do_w_interleave(0, "gpsimd", 0, W_POOL)
+        do_w_interleave(0, "scalar", W_POOL, A)
+        do_w_interleave(1, "scalar", 0, W_FIRST)
         do_cast(2)
-        nc.scalar.copy(out=wt[:], in_=wt_bf[:])
+        do_w_interleave(1, "scalar", W_FIRST, A)
+        turned = psum.tile([P, 2, P], F32, name="turned", tag="bank7")
+        for u in range(2):
+            nc.tensor.transpose(turned[:, u, :], wt_rows[:].bitcast(F32)[:, u::2], ident[:])
+        nc.scalar.copy(
+            out=wt[:].rearrange("p g (u e) -> p g u e", e=2),
+            in_=turned[:].bitcast(BF16).rearrange("p u (g e) -> p g u e", e=2)[:, :GROUPS],
+        )
         for c in range(X_PASSES):
             do_scale(0, c)
-            do_transposes(1, c)
-        do_quant_w(0)
-        do_quant_x(0)
-        do_quant_w(1)
-        do_cast(3)
-        for i in range(2):
-            do_z(0, i, 2 + i)
-            do_sigmoid(0, i)
-        do_diag(0)
         for c in range(X_PASSES):
-            do_scale(1, c)
             do_transposes(2, c)
-        do_aw(0, 1, 4)
+            do_scale(1, c)
+        do_diag(0, 0)
+        do_diag(0, 1)
+        do_diag(1, 1)
+        do_cast(3)
+        do_quant_x(0)
+        do_quant_w(0)
         do_quant_x(1)
+        do_quant_w(1)
+        for c in range(X_PASSES):
+            for i in range(2):
+                do_z(0, i, 2 + i, (c,))
+        for i in range(2):
+            do_sigmoid(0, i)
+        gp[0] = two.tile([P, 4, A], BF16, align_bytes=64, name="gp")
+        for c in range(X_PASSES):
+            do_scale(2, c)
+            do_transposes(3, c)
+            do_z(1, c, 6 + c)
+        do_diags_pool(1, 3)
+        do_sigmoid(1, 0)
+        do_cast(4)
+        do_sigmoid(1, 1)
+        for i in range(2):
+            do_aw(0, i, 4 + i)
+        do_quant_x(2)
 
-        for h in range(2, HALVES):
-            steady = h >= STEADY
-            early = [(m, (h - 5) // 2) for m in range(2 * (1 - h % 2), 2 * (1 - h % 2) + 2) if steady]
+        for h in range(STEADY, HALVES):
             if h % 2 == 0:
                 gp[h // 2 - 1] = two.tile([P, 4, A], BF16, align_bytes=64, name="gp")
-            if h < 4:
-                do_cast(2 * h)
-            elif h % 2 == 1:
-                do_cast((h + 13) // 2)
+            if h % 2 == 1:
+                do_cast(h + 2)
             do_z(h - 1, 0, 2)
             do_sigmoid(h - 1, 0)
-            if steady:
-                do_z(h - 1, 1, 3)
-                do_sigmoid(h - 1, 1)
-            if h < HALVES - 1:
-                do_diag(h - 1)
-            if h < 4:
-                do_cast(2 * h + 1)
-            if h in (5, 7, 9, 10):
-                do_aw_sbuf(HALVES - 2 + (h > 8), (h // 2) % 2)
             do_scale(h, 0)
-            do_pool_residual(h - 2, f"xg{(h - 1) % 2}" if h == 2 or (h >= 5 and h % 2 == 1) else f"sig{h % 3}")
-            if steady:
-                if h % 2 == 1:
-                    do_out(*early.pop())
-                if h > STEADY:
-                    do_aw(h - 2, 1, turn_bank(h, 0))
-                for m, g in early:
-                    do_out(m, g)
-                do_scale(h, 1)
-                do_transposes(h + 1, 0)
-                do_residual(h - 2, 1)
-                do_transposes(h + 1, 1)
-            else:
-                do_transposes(h + 1, 0)
-                do_z(h - 1, 1, 3)
-                do_sigmoid(h - 1, 1)
-                do_scale(h, 1)
-                do_transposes(h + 1, 1)
-                do_aw(h - 1, 1, 3 + h)
-                do_residual(h - 2, 1)
-            if h == 4:
-                do_cast(8)
+            do_pool_residual(h - 2, f"xg{(h - 1) % 2}" if h % 2 == 1 else f"sig{h % 3}")
+            if h >= FIRST_OUT:
+                for m in range(EARLY - 1) if h % 2 == 1 else (EARLY - 1,):
+                    do_out(m, (h - FIRST_OUT) // 2)
+            do_aw(h - 2, 1, turn_bank(h, 0))
+            do_z(h - 1, 1, 3)
+            do_sigmoid(h - 1, 1)
+            do_scale(h, 1)
+            do_transposes(h + 1, 0)
+            if h == STEADY:
+                for i in range(2):
+                    do_residual(0, i)
+            do_residual(h - 2, 1)
+            do_transposes(h + 1, 1)
+            if h % 2 == 0:
+                do_cast(h + 2)
+            if 6 <= h < HALVES - 2:
+                do_diag(h, 1)
+            if h == HALVES - 2:
+                for k in range(4):
+                    do_aw_sbuf(h + k // 2, k % 2)
             if h % 2 == 1:
                 do_interleave((h - 3) // 2, "scalar", 0, A if h < HALVES - 1 else TAIL_A)
             do_quant_x(h)
@@ -346,8 +368,7 @@ def tile_clipped_policy_head_grad_s13_kernel(
                 do_quant_g((h - 4) // 2)
 
         gp[last] = two.tile([P, 4, A], BF16, align_bytes=64, name="gp")
-        for m in (2, 3):
-            do_out(m, last - 2)
+        do_out(EARLY - 1, last - 2)
         for g in range(last - 1):
             do_out(EARLY, g)
         for i in range(2):

@@ -30,7 +30,8 @@ EARLY = 4
 W_POOL = 384
 W_FIRST = 160
 TAIL_SCALAR = 176
-TAIL_A = 256
+TAIL_A = 224
+TAIL_B = 448
 STEADY = 3
 FIRST_OUT = 5
 G_FIRST = 192
@@ -55,7 +56,7 @@ def tile_clipped_policy_head_grad_s13_kernel(
         act = [keep.tile([P, 4, A], BF16, align_bytes=64, name=f"act{g}") for g in range(GROUPS)]
         hw = [keep.tile([P, 2 * D], U8, align_bytes=64, name=f"hw{g}") for g in range(GROUPS)]
         w_raw = [keep.tile([P, 4, A], BF16, align_bytes=64, name=f"w_raw{c}") for c in range(X_PASSES)]
-        w_int = [keep.tile([P, A, 4], BF16, align_bytes=64, name=f"w_int{c}") for c in range(X_PASSES)]
+        w_int = [one.tile([P, A, 4], BF16, align_bytes=64, name=f"w_int{c}") for c in range(X_PASSES)]
         w_codes = [keep.tile([P, A], U32, align_bytes=64, name=f"w_codes{c}") for c in range(X_PASSES)]
         w_scales = [keep.tile([P, A], U8, align_bytes=64, name=f"w_scales{c}") for c in range(X_PASSES)]
         g_codes = [keep.tile([P, A], U32, align_bytes=64, name=f"g_codes{g}") for g in range(GROUPS)]
@@ -83,10 +84,14 @@ def tile_clipped_policy_head_grad_s13_kernel(
         def load_h(g):
             nc.sync.dma_start(out=hw[g][:], in_=h_words[g])
 
+        zeros = keep.tile([P, A], BF16, align_bytes=64, name="zeros")
+        nc.vector.memset(zeros[:], 0.0)
         nc.vector.memset(wt_rows[:], 0.0)
         make_identity(nc, ident[:])
         nc.vector.memset(hs[:], 0)
 
+        warm = keep.tile([P, 1], F32, align_bytes=64, name="warm")
+        nc.scalar.activation(out=warm[:], in_=zeros[:, :1], func=SIGMOID)
         load_x(0)
         nc.sync.dma_start(
             out=xs[:].rearrange("p c u e -> p c (u e)"),
@@ -202,19 +207,6 @@ def tile_clipped_policy_head_grad_s13_kernel(
             nc.scalar.activation(out=tile[:], in_=ident[:], func=COPY, scale=wt[:, g, t : t + 1])
             diag[g, t] = tile[:]
 
-        def do_diags_pool(g_lo, g_hi):
-            n = g_hi - g_lo
-            tile = keep.tile([P, n, 2, P], BF16, align_bytes=64, name="diags", tag="w_int1")
-            nc.gpsimd.tensor_tensor(
-                out=tile[:],
-                in0=ident[:].unsqueeze(1).unsqueeze(1).to_broadcast([P, n, 2, P]),
-                in1=wt[:, g_lo:g_hi, 1::2].unsqueeze(3).to_broadcast([P, n, 2, P]),
-                op=MULT,
-            )
-            for g in range(g_lo, g_hi):
-                for j in range(2):
-                    diag[g, 2 * j + 1] = tile[:, g - g_lo, j, :]
-
         def do_aw(h, i, bank):
             g, t = h // 2, 2 * (h % 2) + i
             aw[h, i] = psum.tile([P, A], F32, name="aw", tag=f"bank{bank}")
@@ -283,6 +275,13 @@ def tile_clipped_policy_head_grad_s13_kernel(
 
         last = GROUPS - 1
 
+        idle = psum.tile([P, A], F32, name="idle", tag="bank4")
+
+        def do_warm(n):
+            for k in range(n):
+                nc.tensor.matmul(idle[:], lhsT=zeros[:, :P], rhs=zeros[:], start=True, stop=True)
+
+        do_warm(4)
         do_cast(0)
         for c in range(X_PASSES):
             do_transposes(0, c)
@@ -306,10 +305,10 @@ def tile_clipped_policy_head_grad_s13_kernel(
         for c in range(X_PASSES):
             do_transposes(2, c)
             do_scale(1, c)
-        do_diag(0, 0)
-        do_diag(0, 1)
-        do_diag(1, 1)
         do_cast(3)
+        do_diag(0, 0)
+        for k in range(4):
+            do_diag(k, 1)
         do_quant_x(0)
         do_quant_w(0)
         do_quant_x(1)
@@ -318,18 +317,18 @@ def tile_clipped_policy_head_grad_s13_kernel(
             for i in range(2):
                 do_z(0, i, 2 + i, (c,))
         for i in range(2):
+            do_aw(0, i, 4 + i)
+        for i in range(2):
             do_sigmoid(0, i)
         gp[0] = two.tile([P, 4, A], BF16, align_bytes=64, name="gp")
         for c in range(X_PASSES):
             do_scale(2, c)
             do_transposes(3, c)
             do_z(1, c, 6 + c)
-        do_diags_pool(1, 3)
         do_sigmoid(1, 0)
         do_cast(4)
         do_sigmoid(1, 1)
-        for i in range(2):
-            do_aw(0, i, 4 + i)
+        do_residual(0, 0)
         do_quant_x(2)
 
         for h in range(STEADY, HALVES):
@@ -350,14 +349,13 @@ def tile_clipped_policy_head_grad_s13_kernel(
             do_scale(h, 1)
             do_transposes(h + 1, 0)
             if h == STEADY:
-                for i in range(2):
-                    do_residual(0, i)
+                do_residual(0, 1)
             do_residual(h - 2, 1)
             do_transposes(h + 1, 1)
             if h % 2 == 0:
                 do_cast(h + 2)
-            if 6 <= h < HALVES - 2:
-                do_diag(h, 1)
+            if h < HALVES - 3:
+                do_diag(h + 1, 1)
             if h == HALVES - 2:
                 for k in range(4):
                     do_aw_sbuf(h + k // 2, k % 2)
@@ -369,30 +367,28 @@ def tile_clipped_policy_head_grad_s13_kernel(
 
         gp[last] = two.tile([P, 4, A], BF16, align_bytes=64, name="gp")
         do_out(EARLY - 1, last - 2)
-        for g in range(last - 1):
+        for g in range(last - 2):
             do_out(EARLY, g)
         for i in range(2):
             do_z(HALVES - 1, i, i)
             do_sigmoid(HALVES - 1, i)
-        for g in range(last - 1):
-            do_out(EARLY + 1, g)
-        do_residual(HALVES - 2, 0)
-        do_interleave(last - 1, "vector", TAIL_A, A)
-        do_residual(HALVES - 2, 1)
-        do_quant_g(last - 1)
-        for i in range(2):
-            do_residual(HALVES - 1, i)
-        for m in range(EARLY + 2):
-            do_out(m, last - 1)
-        for g in range(last):
-            do_out(EARLY + 2, g)
+        for g in range(last - 2, last - 1):
+            do_out(EARLY, g)
+        do_interleave(last - 1, "scalar", TAIL_B, A)
+        for m in range(EARLY + 1, M_TILES):
+            for g in range(last - 1):
+                do_out(m, g)
+        for h in (HALVES - 2, HALVES - 1):
+            for i in range(2):
+                do_residual(h, i)
+            if h == HALVES - 2:
+                do_interleave(last - 1, "vector", TAIL_A, TAIL_B)
         do_interleave(last, "scalar", 0, TAIL_SCALAR)
         do_interleave(last, "vector", TAIL_SCALAR, A)
+        do_quant_g(last - 1)
         do_quant_g(last)
         for m in range(M_TILES):
-            if m == M_TILES - 1:
-                for g in range(last):
-                    do_out(m, g)
+            do_out(m, last - 1)
             do_out(m, last)
             res = keep.tile([P, A], F32, align_bytes=64, name=f"res{m}")
             if m % 2 == 0:

@@ -201,10 +201,12 @@ def tile_clipped_policy_head_grad_s13_kernel(
                 sig[h, i] = one.tile([P, A], F32, align_bytes=64, name="sig", tag=f"sig{h % 3}")
             nc.scalar.activation(out=sig[h, i][:], in_=z[h, i][:], func=SIGMOID)
 
-        def do_diag(h, i):
+        def do_diag(h, i, slot=None):
             g, t = h // 2, 2 * (h % 2) + i
-            tile = keep.tile([P, P], BF16, align_bytes=64, name=f"diag{h}_{i}")
-            nc.scalar.activation(out=tile[:], in_=ident[:], func=COPY, scale=wt[:, g, t : t + 1])
+            tile = one.tile([P, P], BF16, align_bytes=64, name="diag", tag=slot or f"diag{h}_{i}")
+            nc.gpsimd.tensor_scalar(
+                out=tile[:], in0=ident[:], scalar1=wt[:, g, t : t + 1], scalar2=0.0, op0=MULT, op1=ADD
+            )
             diag[g, t] = tile[:]
 
         def do_aw(h, i, bank):
@@ -223,6 +225,8 @@ def tile_clipped_policy_head_grad_s13_kernel(
             g, t = h // 2, 2 * (h % 2)
             part = one.tile([P, A], F32, align_bytes=64, name="part", tag=slot)
             nc.gpsimd.tensor_tensor(out=part[:], in0=sig[h, 0][:], in1=act[g][:, t, :], op=SUB)
+            if h + 3 < HALVES - 2:
+                do_diag(h + 3, 1)
             nc.gpsimd.tensor_scalar(
                 out=gp[g][:, t, :], in0=part[:], scalar1=wt[:, g, t : t + 1], scalar2=0.0, op0=MULT, op1=ADD
             )
@@ -292,7 +296,6 @@ def tile_clipped_policy_head_grad_s13_kernel(
         do_w_interleave(0, "scalar", W_POOL, A)
         do_w_interleave(1, "scalar", 0, W_FIRST)
         do_cast(2)
-        do_w_interleave(1, "scalar", W_FIRST, A)
         turned = psum.tile([P, 2, P], F32, name="turned", tag="bank7")
         for u in range(2):
             nc.tensor.transpose(turned[:, u, :], wt_rows[:].bitcast(F32)[:, u::2], ident[:])
@@ -300,19 +303,20 @@ def tile_clipped_policy_head_grad_s13_kernel(
             out=wt[:].rearrange("p g (u e) -> p g u e", e=2),
             in_=turned[:].bitcast(BF16).rearrange("p u (g e) -> p g u e", e=2)[:, :GROUPS],
         )
+        do_w_interleave(1, "scalar", W_FIRST, A)
         for c in range(X_PASSES):
             do_scale(0, c)
         for c in range(X_PASSES):
             do_transposes(2, c)
             do_scale(1, c)
         do_cast(3)
-        do_diag(0, 0)
-        for k in range(4):
-            do_diag(k, 1)
         do_quant_x(0)
         do_quant_w(0)
         do_quant_x(1)
         do_quant_w(1)
+        do_diag(0, 0, "w_int1")
+        for k in range(4):
+            do_diag(k, 1)
         for c in range(X_PASSES):
             for i in range(2):
                 do_z(0, i, 2 + i, (c,))
@@ -325,9 +329,9 @@ def tile_clipped_policy_head_grad_s13_kernel(
             do_scale(2, c)
             do_transposes(3, c)
             do_z(1, c, 6 + c)
-        do_sigmoid(1, 0)
         do_cast(4)
-        do_sigmoid(1, 1)
+        for i in range(2):
+            do_sigmoid(1, i)
         do_residual(0, 0)
         do_quant_x(2)
 
@@ -354,8 +358,6 @@ def tile_clipped_policy_head_grad_s13_kernel(
             do_transposes(h + 1, 1)
             if h % 2 == 0:
                 do_cast(h + 2)
-            if h < HALVES - 3:
-                do_diag(h + 1, 1)
             if h == HALVES - 2:
                 for k in range(4):
                     do_aw_sbuf(h + k // 2, k % 2)

@@ -34,9 +34,11 @@ TAIL_A = 224
 TAIL_B = 448
 STEADY = 3
 FIRST_OUT = 5
+RING = (0, 1, 3)
+G_FIRST = 208
 G_FIRST = 192
 CAST_BUFS = 3
-OUT_BANK = (4, 5, 6, 7, 2, 3, 0, 1)
+OUT_BANK = (4, 5, 6, 7, 2, 0, 3, 1)
 
 
 def tile_clipped_policy_head_grad_s13_kernel(
@@ -146,7 +148,7 @@ def tile_clipped_policy_head_grad_s13_kernel(
                 nc.scalar.copy(out=cast[h][:], in_=x_raw[h][:].bitcast(FP8))
 
         def turn_bank(h, c):
-            return 2 + c if h == 1 else (c + max(h - STEADY, 0)) % 2
+            return 2 + c if h == 1 else RING[(c - max(h - STEADY, 0)) % 3]
 
         def do_transposes(h, c):
             if h >= HALVES:
@@ -338,31 +340,38 @@ def tile_clipped_policy_head_grad_s13_kernel(
         for h in range(STEADY, HALVES):
             if h % 2 == 0:
                 gp[h // 2 - 1] = two.tile([P, 4, A], BF16, align_bytes=64, name="gp")
-            if h % 2 == 1:
+                do_interleave((h - 4) // 2, "scalar", G_FIRST, A)
+            else:
                 do_cast(h + 2)
             do_z(h - 1, 0, 2)
             do_sigmoid(h - 1, 0)
+            if h == HALVES - 1:
+                for k in range(2):
+                    do_aw_sbuf(h, k)
             do_scale(h, 0)
             do_pool_residual(h - 2, f"xg{(h - 1) % 2}" if h % 2 == 1 else f"sig{h % 3}")
             if h >= FIRST_OUT:
                 for m in range(EARLY - 1) if h % 2 == 1 else (EARLY - 1,):
                     do_out(m, (h - FIRST_OUT) // 2)
             do_aw(h - 2, 1, turn_bank(h, 0))
-            do_z(h - 1, 1, 3)
-            do_sigmoid(h - 1, 1)
-            do_scale(h, 1)
             do_transposes(h + 1, 0)
+            do_scale(h, 1)
+            do_z(h - 1, 1, turn_bank(h, 1) if h + 1 < HALVES else turn_bank(h, 2))
             if h == STEADY:
                 do_residual(0, 1)
             do_residual(h - 2, 1)
             do_transposes(h + 1, 1)
             if h % 2 == 0:
                 do_cast(h + 2)
-            if h == HALVES - 2:
-                for k in range(4):
-                    do_aw_sbuf(h + k // 2, k % 2)
+            if h == HALVES - 1:
+                do_sigmoid(h - 1, 1)
             if h % 2 == 1:
-                do_interleave((h - 3) // 2, "scalar", 0, A if h < HALVES - 1 else TAIL_A)
+                do_interleave((h - 3) // 2, "scalar", 0, G_FIRST if h < HALVES - 1 else TAIL_A)
+            if h < HALVES - 1:
+                do_sigmoid(h - 1, 1)
+            if h == HALVES - 2:
+                for k in range(2):
+                    do_aw_sbuf(h, k)
             do_quant_x(h)
             if h >= 4 and h % 2 == 0:
                 do_quant_g((h - 4) // 2)
@@ -372,7 +381,7 @@ def tile_clipped_policy_head_grad_s13_kernel(
         for g in range(last - 2):
             do_out(EARLY, g)
         for i in range(2):
-            do_z(HALVES - 1, i, i)
+            do_z(HALVES - 1, i, turn_bank(HALVES - 1, 1 - i))
             do_sigmoid(HALVES - 1, i)
         for g in range(last - 2, last - 1):
             do_out(EARLY, g)

@@ -34,6 +34,7 @@ TAIL_A = 224
 TAIL_B = 448
 STEADY = 3
 FIRST_OUT = 5
+POOL_DIAGS = 3
 RING = (0, 1, 3)
 G_FIRST = 208
 G_FIRST = 192
@@ -203,13 +204,24 @@ def tile_clipped_policy_head_grad_s13_kernel(
                 sig[h, i] = one.tile([P, A], F32, align_bytes=64, name="sig", tag=f"sig{h % 3}")
             nc.scalar.activation(out=sig[h, i][:], in_=z[h, i][:], func=SIGMOID)
 
-        def do_diag(h, i, slot=None):
+        def do_diag(h, i):
             g, t = h // 2, 2 * (h % 2) + i
-            tile = one.tile([P, P], BF16, align_bytes=64, name="diag", tag=slot or f"diag{h}_{i}")
-            nc.gpsimd.tensor_scalar(
-                out=tile[:], in0=ident[:], scalar1=wt[:, g, t : t + 1], scalar2=0.0, op0=MULT, op1=ADD
-            )
+            tile = keep.tile([P, P], BF16, align_bytes=64, name=f"diag{h}_{i}")
+            nc.scalar.activation(out=tile[:], in_=ident[:], func=COPY, scale=wt[:, g, t : t + 1])
             diag[g, t] = tile[:]
+
+        def do_diags_pool(g_lo, g_hi):
+            n = g_hi - g_lo
+            tile = one.tile([P, n, 2, P], BF16, align_bytes=64, name="diags", tag="w_int1")
+            nc.gpsimd.tensor_tensor(
+                out=tile[:],
+                in0=ident[:].unsqueeze(1).unsqueeze(1).to_broadcast([P, n, 2, P]),
+                in1=wt[:, g_lo:g_hi, 1::2].unsqueeze(3).to_broadcast([P, n, 2, P]),
+                op=MULT,
+            )
+            for g in range(g_lo, g_hi):
+                for j in range(2):
+                    diag[g, 2 * j + 1] = tile[:, g - g_lo, j, :]
 
         def do_aw(h, i, bank):
             g, t = h // 2, 2 * (h % 2) + i
@@ -227,8 +239,6 @@ def tile_clipped_policy_head_grad_s13_kernel(
             g, t = h // 2, 2 * (h % 2)
             part = one.tile([P, A], F32, align_bytes=64, name="part", tag=slot)
             nc.gpsimd.tensor_tensor(out=part[:], in0=sig[h, 0][:], in1=act[g][:, t, :], op=SUB)
-            if h + 3 < HALVES - 2:
-                do_diag(h + 3, 1)
             nc.gpsimd.tensor_scalar(
                 out=gp[g][:, t, :], in0=part[:], scalar1=wt[:, g, t : t + 1], scalar2=0.0, op0=MULT, op1=ADD
             )
@@ -312,13 +322,14 @@ def tile_clipped_policy_head_grad_s13_kernel(
             do_transposes(2, c)
             do_scale(1, c)
         do_cast(3)
+        do_diag(0, 0)
+        for k in range(2 * POOL_DIAGS):
+            do_diag(k, 1)
         do_quant_x(0)
         do_quant_w(0)
         do_quant_x(1)
         do_quant_w(1)
-        do_diag(0, 0, "w_int1")
-        for k in range(4):
-            do_diag(k, 1)
+        do_diags_pool(POOL_DIAGS, GROUPS - 1)
         for c in range(X_PASSES):
             for i in range(2):
                 do_z(0, i, 2 + i, (c,))

@@ -87,14 +87,10 @@ def tile_clipped_policy_head_grad_s13_kernel(
         def load_h(g):
             nc.sync.dma_start(out=hw[g][:], in_=h_words[g])
 
-        zeros = keep.tile([P, A], BF16, align_bytes=64, name="zeros")
-        nc.vector.memset(zeros[:], 0.0)
         nc.vector.memset(wt_rows[:], 0.0)
         make_identity(nc, ident[:])
         nc.vector.memset(hs[:], 0)
 
-        warm = keep.tile([P, 1], F32, align_bytes=64, name="warm")
-        nc.scalar.activation(out=warm[:], in_=zeros[:, :1], func=SIGMOID)
         load_x(0)
         nc.sync.dma_start(
             out=xs[:].rearrange("p c u e -> p c (u e)"),
@@ -291,13 +287,6 @@ def tile_clipped_policy_head_grad_s13_kernel(
 
         last = GROUPS - 1
 
-        idle = psum.tile([P, A], F32, name="idle", tag="bank4")
-
-        def do_warm(n):
-            for k in range(n):
-                nc.tensor.matmul(idle[:], lhsT=zeros[:, :P], rhs=zeros[:], start=True, stop=True)
-
-        do_warm(4)
         do_cast(0)
         for c in range(X_PASSES):
             do_transposes(0, c)

@@ -29,17 +29,24 @@ M_TILES = D // P
 EARLY = 4
 W_POOL = 384
 W_FIRST = 160
-TAIL_SCALAR = 176
-TAIL_A = 224
-TAIL_B = 448
+TAIL_SCALAR = 112
+TAIL_A = 176
+TAIL_B = 384
+PRE = 1
+SCALAR_STORES = (0, 1, 2, 4, 6, 8)
 STEADY = 3
 FIRST_OUT = 5
+A_HALF = A // 2
+WARM = 4
 POOL_DIAGS = 3
 RING = (0, 1, 3)
 G_FIRST = 208
 G_FIRST = 192
 CAST_BUFS = 3
-OUT_BANK = (4, 5, 6, 7, 2, 0, 3, 1)
+PIECES = (
+    (0, (0, 1), 4), (0, (2, 3), 5), (0, (4, 5), 6), (0, (6, 7), 7),
+    (1, (0, 1), 2), (1, (2, 3), 0), (1, (4, 5), 3), (1, (6,), 1), (1, (7,), 4),
+)
 
 
 def tile_clipped_policy_head_grad_s13_kernel(
@@ -87,10 +94,17 @@ def tile_clipped_policy_head_grad_s13_kernel(
         def load_h(g):
             nc.sync.dma_start(out=hw[g][:], in_=h_words[g])
 
+        nc.vector.memset(ident[:], 0.0)
         nc.vector.memset(wt_rows[:], 0.0)
-        make_identity(nc, ident[:])
         nc.vector.memset(hs[:], 0)
+        make_identity(nc, ident[:], nomemset=True)
 
+        warm = keep.tile([P, 1], F32, align_bytes=64, name="warm")
+        nc.scalar.activation(out=warm[:], in_=wt_rows[:, :1], func=SIGMOID)
+        idle = psum.tile([P, A], F32, name="idle", tag="bank4")
+
+        for k in range(WARM):
+            nc.tensor.matmul(idle[:], lhsT=wt_rows[:, :P], rhs=wt_rows[:], start=True, stop=True)
         load_x(0)
         nc.sync.dma_start(
             out=xs[:].rearrange("p c u e -> p c (u e)"),
@@ -126,6 +140,9 @@ def tile_clipped_policy_head_grad_s13_kernel(
         z = {}
         sig = {}
         diag = {}
+        sig_last = keep.tile([P, 2, A], F32, align_bytes=64, name="sig_last")
+        for i in range(2):
+            sig[HALVES - 1, i] = sig_last[:, i, :]
         aw = {}
         gp = {}
         gi = {}
@@ -257,24 +274,63 @@ def tile_clipped_policy_head_grad_s13_kernel(
                 gi[g] = one.tile([P, A, 4], BF16, align_bytes=64, name="gi", tag=f"gi{g % 2}")
             interleave(engine, gi[g][:, lo:hi, :], gp[g][:, :, lo:hi].rearrange("p t a -> p a t"))
 
-        def do_quant_g(g):
+        def do_quant_g(g, lo=0, hi=A):
             nc.vector.quantize_mx(
-                out=g_codes[g][:].bitcast(FP8X4), scales=g_scales[g][:],
-                in_=gi[g][:].rearrange("p a t -> p (a t)"),
+                out=g_codes[g][:, lo:hi].bitcast(FP8X4), scales=g_scales[g][:, lo:hi],
+                in_=gi[g][:, lo:hi, :].rearrange("p a t -> p (a t)"),
             )
 
-        def do_out(m, g):
-            if g == 0:
-                accs[m] = psum.tile([P, A], F32, name="acc", tag=f"bank{OUT_BANK[m]}")
-            nc.tensor.matmul_mx(
-                out=accs[m][:],
-                lhsT=hw[g][:, 2 * P * m : 2 * P * (m + 1)].bitcast(FP4X4),
-                lhsT_scale=hs[:, g, 32 * m : 32 * (m + 1)].bitcast(U8),
-                rhs=g_codes[g][:].bitcast(FP8X4),
-                rhs_scale=g_scales[g][:],
-                start=(g == 0),
-                stop=(g == GROUPS - 1),
+        def do_store(b):
+            f, tiles, bank = PIECES[b]
+            res = keep.tile([P, len(tiles), A_HALF], F32, align_bytes=64, name=f"res{b}")
+            src = accs[b][:].rearrange("p s q n -> p s (q n)")
+            if b in SCALAR_STORES:
+                nc.scalar.copy(out=res[:], in_=src)
+            else:
+                nc.vector.tensor_copy(out=res[:], in_=src)
+            rows = out[tiles[0] * P : (tiles[-1] + 1) * P, f * A_HALF : (f + 1) * A_HALF]
+            nc.sync.dma_start(out=rows.rearrange("(s p) n -> p s n", p=P), in_=res[:])
+
+        def do_logits_half(h, f, bank):
+            cols = slice(f * A_HALF, (f + 1) * A_HALF)
+            zh = psum.tile([P, 2, A_HALF], F32, name="zh", tag=f"bank{bank}")
+            for i in range(2):
+                for c in range(X_PASSES):
+                    nc.tensor.matmul_mx(
+                        out=zh[:, i, :],
+                        lhsT=x_codes[h][:, c, i * P : (i + 1) * P].bitcast(FP8X4),
+                        lhsT_scale=x_scales[h][:, c, i * P : (i + 1) * P],
+                        rhs=w_codes[c][:, cols].bitcast(FP8X4),
+                        rhs_scale=w_scales[c][:, cols],
+                        start=(c == 0),
+                        stop=(c == X_PASSES - 1),
+                    )
+            nc.scalar.activation(out=sig_last[:, :, cols], in_=zh[:], func=SIGMOID)
+
+        def do_residual_half(h, i, f):
+            g, t = h // 2, 2 * (h % 2) + i
+            cols = slice(f * A_HALF, (f + 1) * A_HALF)
+            nc.vector.scalar_tensor_tensor(
+                out=gp[g][:, t, cols], in0=sig[h, i][:, cols], scalar=wt[:, g, t : t + 1], in1=aw[h, i][:, cols],
+                op0=MULT, op1=SUB,
             )
+
+        def do_out(b, g):
+            f, tiles, bank = PIECES[b]
+            if g == 0:
+                accs[b] = psum.tile([P, len(tiles), 2, P], F32, name="acc", tag=f"bank{bank}")
+            for s, m in enumerate(tiles):
+                for q in range(2):
+                    cols = slice((2 * f + q) * P, (2 * f + q + 1) * P)
+                    nc.tensor.matmul_mx(
+                        out=accs[b][:, s, q, :],
+                        lhsT=hw[g][:, 2 * P * m : 2 * P * (m + 1)].bitcast(FP4X4),
+                        lhsT_scale=hs[:, g, 32 * m : 32 * (m + 1)].bitcast(U8),
+                        rhs=g_codes[g][:, cols].bitcast(FP8X4),
+                        rhs_scale=g_scales[g][:, cols],
+                        start=(g == 0 and s == 0 and q == 0),
+                        stop=(g == GROUPS - 1 and s == len(tiles) - 1 and q == 1),
+                    )
 
         def do_w_interleave(c, engine, lo, hi):
             interleave(engine, w_int[c][:, lo:hi, :], w_raw[c][:, :, lo:hi].rearrange("p j n -> p n j"))
@@ -376,34 +432,48 @@ def tile_clipped_policy_head_grad_s13_kernel(
             if h >= 4 and h % 2 == 0:
                 do_quant_g((h - 4) // 2)
 
+        h = HALVES - 1
         gp[last] = two.tile([P, 4, A], BF16, align_bytes=64, name="gp")
         do_out(EARLY - 1, last - 2)
         for g in range(last - 2):
             do_out(EARLY, g)
+        for f in range(2):
+            do_logits_half(h, f, turn_bank(h, 1 - f))
+        do_out(EARLY, last - 2)
+        do_residual_half(h - 1, 0, 0)
+        do_interleave(last - 1, "vector", TAIL_A, A_HALF)
+        do_residual_half(h - 1, 1, 0)
+        do_residual_half(h - 1, 0, 1)
+        do_quant_g(last - 1, 0, A_HALF)
+        do_out(EARLY + 1, 0)
+        for b in range(EARLY):
+            do_out(b, last - 1)
         for i in range(2):
-            do_z(HALVES - 1, i, turn_bank(HALVES - 1, 1 - i))
-            do_sigmoid(HALVES - 1, i)
-        for g in range(last - 2, last - 1):
-            do_out(EARLY, g)
-        do_interleave(last - 1, "scalar", TAIL_B, A)
-        for m in range(EARLY + 1, M_TILES):
-            for g in range(last - 1):
-                do_out(m, g)
-        for h in (HALVES - 2, HALVES - 1):
-            for i in range(2):
-                do_residual(h, i)
-            if h == HALVES - 2:
-                do_interleave(last - 1, "vector", TAIL_A, TAIL_B)
+            do_residual_half(h, i, 0)
         do_interleave(last, "scalar", 0, TAIL_SCALAR)
-        do_interleave(last, "vector", TAIL_SCALAR, A)
-        do_quant_g(last - 1)
-        do_quant_g(last)
-        for m in range(M_TILES):
-            do_out(m, last - 1)
-            do_out(m, last)
-            res = keep.tile([P, A], F32, align_bytes=64, name=f"res{m}")
-            if m % 2 == 0:
-                nc.vector.tensor_copy(out=res[:], in_=accs[m][:])
-            else:
-                nc.scalar.copy(out=res[:], in_=accs[m][:])
-            nc.sync.dma_start(out=out[m * P : (m + 1) * P, :], in_=res[:])
+        do_residual_half(h - 1, 1, 1)
+        do_interleave(last, "vector", TAIL_SCALAR, A_HALF)
+        do_residual_half(h, 0, 1)
+        do_quant_g(last, 0, A_HALF)
+        for g in range(1, last - 1):
+            do_out(EARLY + 1, g)
+        for g in range(PRE):
+            do_out(EARLY + 2, g)
+        for b in range(EARLY):
+            do_out(b, last)
+        do_interleave(last - 1, "scalar", A_HALF, TAIL_B)
+        do_residual_half(h, 1, 1)
+        do_interleave(last - 1, "vector", TAIL_B, A)
+        do_store(0)
+        do_interleave(last, "vector", A_HALF, A)
+        do_store(1)
+        do_quant_g(last - 1, A_HALF, A)
+        do_quant_g(last, A_HALF, A)
+        for b in range(2, EARLY):
+            do_store(b)
+        for g in range(PRE, last - 1):
+            do_out(EARLY + 2, g)
+        for b in range(EARLY, len(PIECES)):
+            for g in range(last - 1 if b < EARLY + 3 else 0, GROUPS):
+                do_out(b, g)
+            do_store(b)

@@ -23,30 +23,31 @@ COPY = mybir.ActivationFunctionType.Copy
 P = 128
 K_PASS = 512
 GROUPS = T // K_PASS
-HALVES = 2 * GROUPS
+STEPS = 2 * GROUPS
 X_PASSES = D // K_PASS
-M_TILES = D // P
-EARLY = 4
-W_POOL = 384
-W_FIRST = 160
-TAIL_SCALAR = 112
-TAIL_A = 176
-TAIL_B = 384
-PRE = 1
-SCALAR_STORES = (0, 1, 2, 4, 6, 8)
-STEADY = 3
-FIRST_OUT = 5
-A_HALF = A // 2
+HALF = A // 2
+POOL_COLS = 832
+OWN_COLS = 2 * A - POOL_COLS
+FIRST_POOL = 0
+CAST_BUFS = 5
+XG_BUFS = 3
+CODE_BUFS = 6
+SIG_BUFS = 3
+GI_BUFS = 3
+PLANE_BUFS = 4
+RES_BUFS = 9
 WARM = 4
-POOL_DIAGS = 3
-RING = (0, 1, 3)
-G_FIRST = 208
-G_FIRST = 192
-CAST_BUFS = 3
+W_POOL = 256
+W_OWN = 256
+STEADY = 2
+EARLY_BANKS = (0, 4, 6)
+EARLY_STEPS = 6
+FIRST_OUT = 5
 PIECES = (
     (0, (0, 1), 4), (0, (2, 3), 5), (0, (4, 5), 6), (0, (6, 7), 7),
-    (1, (0, 1), 2), (1, (2, 3), 0), (1, (4, 5), 3), (1, (6,), 1), (1, (7,), 4),
+    (1, (0, 1), 0), (1, (2, 3), 1), (1, (4, 5), 2), (1, (6,), 3), (1, (7,), 4),
 )
+LAST_SPLIT = 96
 
 
 def tile_clipped_policy_head_grad_s13_kernel(
@@ -56,26 +57,26 @@ def tile_clipped_policy_head_grad_s13_kernel(
     with ExitStack() as ctx:
         keep = ctx.enter_context(tc.tile_pool(name="keep", bufs=1))
         one = ctx.enter_context(tc.tile_pool(name="one", bufs=1))
-        two = ctx.enter_context(tc.tile_pool(name="two", bufs=2))
-        three = ctx.enter_context(tc.tile_pool(name="three", bufs=3))
-        four = ctx.enter_context(tc.tile_pool(name="four", bufs=4))
         psum = ctx.enter_context(tc.psum_pool(name="psum", bufs=1))
         ctx.enter_context(tc.manual_schedule())
 
-        x_raw = [keep.tile([P, 2 * D], U8, align_bytes=64, name=f"x_raw{h}") for h in range(HALVES)]
+        x_raw = [keep.tile([P, 2 * D], U8, align_bytes=64, name=f"x_raw{h}") for h in range(STEPS)]
         act = [keep.tile([P, 4, A], BF16, align_bytes=64, name=f"act{g}") for g in range(GROUPS)]
         hw = [keep.tile([P, 2 * D], U8, align_bytes=64, name=f"hw{g}") for g in range(GROUPS)]
         w_raw = [keep.tile([P, 4, A], BF16, align_bytes=64, name=f"w_raw{c}") for c in range(X_PASSES)]
-        w_int = [one.tile([P, A, 4], BF16, align_bytes=64, name=f"w_int{c}") for c in range(X_PASSES)]
+        w_int = [keep.tile([P, A, 4], BF16, align_bytes=64, name=f"w_int{c}") for c in range(X_PASSES)]
         w_codes = [keep.tile([P, A], U32, align_bytes=64, name=f"w_codes{c}") for c in range(X_PASSES)]
         w_scales = [keep.tile([P, A], U8, align_bytes=64, name=f"w_scales{c}") for c in range(X_PASSES)]
         g_codes = [keep.tile([P, A], U32, align_bytes=64, name=f"g_codes{g}") for g in range(GROUPS)]
         g_scales = [keep.tile([P, A], U8, align_bytes=64, name=f"g_scales{g}") for g in range(GROUPS)]
+        diff = [keep.tile([P, 2 * A], F32, align_bytes=64, name=f"diff{h}") for h in range(STEPS)]
         hs = keep.tile([P, GROUPS, D // 4], I32, align_bytes=64, name="hs")
         xs = keep.tile([P, X_PASSES, 2, 2], F32, align_bytes=64, name="xs")
-        wt_rows = keep.tile([P, K_PASS], BF16, align_bytes=64, name="wt_rows")
+        wt_raw = keep.tile([P, GROUPS, 4], BF16, align_bytes=64, name="wt_raw")
         wt = keep.tile([P, GROUPS, 4], F32, align_bytes=64, name="wt")
         ident = keep.tile([P, P], F32, align_bytes=64, name="ident")
+        zeros = keep.tile([P, A], BF16, align_bytes=64, name="zeros")
+        warm = keep.tile([P, 1], F32, align_bytes=64, name="warm")
 
         def load_x(h):
             g, lo = h // 2, 2 * (h % 2)
@@ -94,172 +95,134 @@ def tile_clipped_policy_head_grad_s13_kernel(
         def load_h(g):
             nc.sync.dma_start(out=hw[g][:], in_=h_words[g])
 
-        nc.vector.memset(ident[:], 0.0)
-        nc.vector.memset(wt_rows[:], 0.0)
-        nc.vector.memset(hs[:], 0)
-        make_identity(nc, ident[:], nomemset=True)
+        def load_x_scale():
+            nc.sync.dma_start(
+                out=xs[:].rearrange("p c u e -> p c (u e)"),
+                in_=x_scale.rearrange("o (c p t) -> p (o c) t", p=P, t=4),
+            )
 
-        warm = keep.tile([P, 1], F32, align_bytes=64, name="warm")
-        nc.scalar.activation(out=warm[:], in_=wt_rows[:, :1], func=SIGMOID)
-        idle = psum.tile([P, A], F32, name="idle", tag="bank4")
+        def load_weight():
+            nc.sync.dma_start(out=wt_raw[:], in_=weight.rearrange("(g p t) -> p g t", p=P, t=4))
 
-        for k in range(WARM):
-            nc.tensor.matmul(idle[:], lhsT=wt_rows[:, :P], rhs=wt_rows[:], start=True, stop=True)
-        load_x(0)
-        nc.sync.dma_start(
-            out=xs[:].rearrange("p c u e -> p c (u e)"),
-            in_=x_scale.rearrange("o (c p t) -> p (o c) t", p=P, t=4),
-        )
-        load_x(1)
-        load_w(0)
-        load_w(1)
-        nc.sync.dma_start(out=wt_rows[:GROUPS, :], in_=weight.rearrange("(g k) -> g k", k=K_PASS))
-        load_x(2)
-        load_act(0, 0, 2)
-        load_x(3)
-        load_x(4)
-        load_act(0, 2, 4)
-        load_x(5)
-        load_x(6)
-        load_act(1)
-        scales_src = h_scales.bitcast(I32).rearrange("g (q r) n -> r q g n", r=4)
-        for r in range(4):
-            nc.sync.dma_start(out=hs[r:P:32, :, :], in_=scales_src[r])
-        for g in range(GROUPS):
-            load_h(g)
-            for h in range(2 * g + 7, min(2 * g + 9, HALVES)):
-                load_x(h)
-            if g + 2 < GROUPS:
-                load_act(g + 2)
+        def load_h_scales():
+            scales_src = h_scales.bitcast(I32).rearrange("g (q r) n -> r q g n", r=4)
+            for r in range(4):
+                nc.sync.dma_start(out=hs[r:P:32, :, :], in_=scales_src[r])
 
-        cast = {}
-        banks = {}
-        xg = {}
-        x_codes = {}
-        x_scales = {}
-        z = {}
-        sig = {}
-        diag = {}
-        sig_last = keep.tile([P, 2, A], F32, align_bytes=64, name="sig_last")
-        for i in range(2):
-            sig[HALVES - 1, i] = sig_last[:, i, :]
-        aw = {}
-        gp = {}
-        gi = {}
-        accs = {}
+        cast, turned, xg, x_codes, x_scales = {}, {}, {}, {}, {}
+        z, sig, planes, gi, accs = {}, {}, {}, {}, {}
 
-        def do_cast(h):
-            if h >= HALVES:
-                return
-            cast[h] = one.tile([P, 2 * D], BF16, align_bytes=64, name="cast", bufs=CAST_BUFS)
-            if h == 0:
-                for c in range(X_PASSES):
-                    lo = slice(c * K_PASS, (c + 1) * K_PASS)
-                    hi = slice(D + c * K_PASS, D + (c + 1) * K_PASS)
-                    nc.vector.tensor_copy(out=cast[h][:, lo], in_=x_raw[h][:, lo].bitcast(FP8))
-                    nc.scalar.copy(out=cast[h][:, hi], in_=x_raw[h][:, hi].bitcast(FP8))
+        def token_slot(h, i):
+            return h // 2, 2 * (h % 2) + i
+
+        def half_cols(f):
+            return slice(f * HALF, (f + 1) * HALF)
+
+        def do_cast(h, engine="scalar", lo=0, hi=2 * D):
+            if h not in cast:
+                cast[h] = one.tile([P, 2 * D], BF16, align_bytes=64, name="cast", bufs=CAST_BUFS)
+            if engine == "vector":
+                nc.vector.tensor_copy(out=cast[h][:, lo:hi], in_=x_raw[h][:, lo:hi].bitcast(FP8))
             else:
-                nc.scalar.copy(out=cast[h][:], in_=x_raw[h][:].bitcast(FP8))
+                nc.scalar.copy(out=cast[h][:, lo:hi], in_=x_raw[h][:, lo:hi].bitcast(FP8))
 
-        def turn_bank(h, c):
-            return 2 + c if h == 1 else RING[(c - max(h - STEADY, 0)) % 3]
-
-        def do_transposes(h, c):
-            if h >= HALVES:
-                return
-            bank = psum.tile([P, 2, 2 * P], F32, name="turned", tag=f"bank{turn_bank(h, c)}")
-            banks[h, c] = bank
+        def do_turn(h, c, bank):
+            turned[h, c] = psum.tile([P, 2, 2 * P], F32, name="turned", tag=f"bank{bank}")
             for i in range(2):
                 words = cast[h][:, i * D : (i + 1) * D].bitcast(F32)
                 for u in range(2):
                     nc.tensor.transpose(
-                        bank[:, u, i * P : (i + 1) * P], words[:, 256 * c + u : 256 * (c + 1) : 2], ident[:]
+                        turned[h, c][:, u, i * P : (i + 1) * P], words[:, 256 * c + u : 256 * (c + 1) : 2], ident[:]
                     )
 
         def do_scale(h, c):
-            if h not in xg:
-                xg[h] = one.tile([P, X_PASSES, 2 * P, 2, 2], BF16, align_bytes=64, name="xg", tag=f"xg{h % 2}")
+            if c == 0 and FIRST_POOL <= h - 1 < STEPS - 2:
+                xg[h, c] = diff[h - 1][:, A:].bitcast(BF16).rearrange("p (r u e) -> p r u e", u=2, e=2)
+            else:
+                tile = one.tile([P, 2 * P, 2, 2], BF16, align_bytes=64, name="xg", bufs=XG_BUFS)
+                xg[h, c] = tile[:]
             nc.vector.tensor_tensor(
-                out=xg[h][:, c],
-                in0=banks[h, c][:].bitcast(BF16).rearrange("p u (r e) -> p r u e", e=2),
+                out=xg[h, c],
+                in0=turned[h, c][:].bitcast(BF16).rearrange("p u (r e) -> p r u e", e=2),
                 in1=xs[:, c].unsqueeze(1).to_broadcast([P, 2 * P, 2, 2]),
                 op=MULT,
             )
 
-        def do_quant_x(h):
-            x_codes[h] = three.tile([P, X_PASSES, 2 * P], U32, align_bytes=64, name="x_codes")
-            x_scales[h] = three.tile([P, X_PASSES, 2 * P], U8, align_bytes=64, name="x_scales")
+        def do_quant_x(h, c):
+            x_codes[h, c] = one.tile([P, 2 * P], U32, align_bytes=64, name="x_codes", bufs=CODE_BUFS)
+            x_scales[h, c] = one.tile([P, 2 * P], U8, align_bytes=64, name="x_scales", bufs=CODE_BUFS)
             nc.vector.quantize_mx(
-                out=x_codes[h][:].rearrange("p c r -> p (c r)").bitcast(FP8X4),
-                scales=x_scales[h][:].rearrange("p c r -> p (c r)"),
-                in_=xg[h][:].rearrange("p c r u e -> p (c r u e)"),
+                out=x_codes[h, c][:].bitcast(FP8X4),
+                scales=x_scales[h, c][:],
+                in_=xg[h, c].rearrange("p r u e -> p (r u e)"),
+            )
+
+        def logits_pass(dst, h, i, c, cols):
+            nc.tensor.matmul_mx(
+                out=dst,
+                lhsT=x_codes[h, c][:, i * P : (i + 1) * P].bitcast(FP8X4),
+                lhsT_scale=x_scales[h, c][:, i * P : (i + 1) * P],
+                rhs=w_codes[c][:, cols].bitcast(FP8X4),
+                rhs_scale=w_scales[c][:, cols],
+                start=(c == 0),
+                stop=(c == X_PASSES - 1),
             )
 
         def do_z(h, i, bank, passes=range(X_PASSES)):
             if (h, i) not in z:
                 z[h, i] = psum.tile([P, A], F32, name="zt", tag=f"bank{bank}")
-            zt = z[h, i]
             for c in passes:
-                nc.tensor.matmul_mx(
-                    out=zt[:],
-                    lhsT=x_codes[h][:, c, i * P : (i + 1) * P].bitcast(FP8X4),
-                    lhsT_scale=x_scales[h][:, c, i * P : (i + 1) * P],
-                    rhs=w_codes[c][:].bitcast(FP8X4),
-                    rhs_scale=w_scales[c][:],
-                    start=(c == 0),
-                    stop=(c == X_PASSES - 1),
-                )
+                logits_pass(z[h, i][:], h, i, c, slice(0, A))
+
+        def sig_tile(h):
+            if h not in sig:
+                sig[h] = one.tile([P, 2 * A], F32, align_bytes=64, name="sig", bufs=SIG_BUFS)
+            return sig[h]
 
         def do_sigmoid(h, i):
-            if i == 0:
-                sig[h, i] = three.tile([P, A], F32, align_bytes=64, name="sig")
+            nc.scalar.activation(out=sig_tile(h)[:, i * A : (i + 1) * A], in_=z[h, i][:], func=SIGMOID)
+
+        def do_z_half(h, f, bank):
+            z[h, "half", f] = psum.tile([P, 2, HALF], F32, name="zh", tag=f"bank{bank}")
+            for i in range(2):
+                for c in range(X_PASSES):
+                    logits_pass(z[h, "half", f][:, i, :], h, i, c, half_cols(f))
+
+        def do_sigmoid_half(h, f):
+            both = sig_tile(h)[:].rearrange("p (i a) -> p i a", i=2)
+            nc.scalar.activation(out=both[:, :, half_cols(f)], in_=z[h, "half", f][:], func=SIGMOID)
+
+        def do_diff(h, engine, lo, hi):
+            g, t = token_slot(h, 0)
+            taken = act[g][:, t : t + 2, :].rearrange("p i a -> p (i a)")
+            op = nc.gpsimd.tensor_tensor if engine == "gpsimd" else nc.vector.tensor_tensor
+            op(out=diff[h][:, lo:hi], in0=sig[h][:, lo:hi], in1=taken[:, lo:hi], op=SUB)
+
+        def do_diff_half(h, f):
+            g, t = token_slot(h, 0)
+            nc.vector.tensor_tensor(
+                out=diff[h][:].rearrange("p (i a) -> p i a", i=2)[:, :, half_cols(f)],
+                in0=sig[h][:].rearrange("p (i a) -> p i a", i=2)[:, :, half_cols(f)],
+                in1=act[g][:, t : t + 2, half_cols(f)],
+                op=SUB,
+            )
+
+        def do_weigh(h, i, f, engine):
+            g, t = token_slot(h, i)
+            if (g, f) not in planes:
+                planes[g, f] = one.tile([P, 4, HALF], BF16, align_bytes=64, name="planes", bufs=PLANE_BUFS)
+            src = diff[h][:, i * A + f * HALF : i * A + (f + 1) * HALF]
+            if engine == "scalar":
+                nc.scalar.activation(out=planes[g, f][:, t, :], in_=src, func=COPY, scale=wt[:, g, t : t + 1])
             else:
-                sig[h, i] = one.tile([P, A], F32, align_bytes=64, name="sig", tag=f"sig{h % 3}")
-            nc.scalar.activation(out=sig[h, i][:], in_=z[h, i][:], func=SIGMOID)
+                nc.vector.tensor_scalar(
+                    out=planes[g, f][:, t, :], in0=src, scalar1=wt[:, g, t : t + 1], scalar2=None, op0=MULT
+                )
 
-        def do_diag(h, i):
-            g, t = h // 2, 2 * (h % 2) + i
-            tile = keep.tile([P, P], BF16, align_bytes=64, name=f"diag{h}_{i}")
-            nc.scalar.activation(out=tile[:], in_=ident[:], func=COPY, scale=wt[:, g, t : t + 1])
-            diag[g, t] = tile[:]
-
-        def do_diags_pool(g_lo, g_hi):
-            n = g_hi - g_lo
-            tile = one.tile([P, n, 2, P], BF16, align_bytes=64, name="diags", tag="w_int1")
-            nc.gpsimd.tensor_tensor(
-                out=tile[:],
-                in0=ident[:].unsqueeze(1).unsqueeze(1).to_broadcast([P, n, 2, P]),
-                in1=wt[:, g_lo:g_hi, 1::2].unsqueeze(3).to_broadcast([P, n, 2, P]),
-                op=MULT,
-            )
-            for g in range(g_lo, g_hi):
-                for j in range(2):
-                    diag[g, 2 * j + 1] = tile[:, g - g_lo, j, :]
-
-        def do_aw(h, i, bank):
-            g, t = h // 2, 2 * (h % 2) + i
-            aw[h, i] = psum.tile([P, A], F32, name="aw", tag=f"bank{bank}")
-            nc.tensor.matmul(aw[h, i][:], lhsT=diag[g, t], rhs=act[g][:, t, :], start=True, stop=True)
-
-        def do_residual(h, i):
-            g, t = h // 2, 2 * (h % 2) + i
-            nc.vector.scalar_tensor_tensor(
-                out=gp[g][:, t, :], in0=sig[h, i][:], scalar=wt[:, g, t : t + 1], in1=aw[h, i][:],
-                op0=MULT, op1=SUB,
-            )
-
-        def do_pool_residual(h, slot):
-            g, t = h // 2, 2 * (h % 2)
-            part = one.tile([P, A], F32, align_bytes=64, name="part", tag=slot)
-            nc.gpsimd.tensor_tensor(out=part[:], in0=sig[h, 0][:], in1=act[g][:, t, :], op=SUB)
-            nc.gpsimd.tensor_scalar(
-                out=gp[g][:, t, :], in0=part[:], scalar1=wt[:, g, t : t + 1], scalar2=0.0, op0=MULT, op1=ADD
-            )
-
-        def do_aw_sbuf(h, i):
-            g, t = h // 2, 2 * (h % 2) + i
-            aw[h, i] = four.tile([P, A], F32, align_bytes=64, name="aw_sbuf")
-            nc.scalar.activation(out=aw[h, i][:], in_=act[g][:, t, :], func=COPY, scale=wt[:, g, t : t + 1])
+        def do_weigh_late(g, engine):
+            for h in (2 * g, 2 * g + 1):
+                for i in range(2):
+                    do_weigh(h, i, 1, engine)
 
         def interleave(engine, dst, src):
             if engine == "vector":
@@ -269,68 +232,41 @@ def tile_clipped_policy_head_grad_s13_kernel(
             else:
                 nc.gpsimd.tensor_scalar(out=dst, in0=src, scalar1=1.0, scalar2=0.0, op0=MULT, op1=ADD)
 
-        def do_interleave(g, engine, lo, hi):
-            if g not in gi:
-                gi[g] = one.tile([P, A, 4], BF16, align_bytes=64, name="gi", tag=f"gi{g % 2}")
-            interleave(engine, gi[g][:, lo:hi, :], gp[g][:, :, lo:hi].rearrange("p t a -> p a t"))
+        def do_interleave(g, f, engine, lo=0, hi=HALF):
+            if (g, f) not in gi:
+                gi[g, f] = one.tile([P, HALF, 4], BF16, align_bytes=64, name="gi", bufs=GI_BUFS)
+            interleave(engine, gi[g, f][:, lo:hi, :], planes[g, f][:, :, lo:hi].rearrange("p t a -> p a t"))
 
-        def do_quant_g(g, lo=0, hi=A):
+        def do_quant_g(g, f):
             nc.vector.quantize_mx(
-                out=g_codes[g][:, lo:hi].bitcast(FP8X4), scales=g_scales[g][:, lo:hi],
-                in_=gi[g][:, lo:hi, :].rearrange("p a t -> p (a t)"),
-            )
-
-        def do_store(b):
-            f, tiles, bank = PIECES[b]
-            res = keep.tile([P, len(tiles), A_HALF], F32, align_bytes=64, name=f"res{b}")
-            src = accs[b][:].rearrange("p s q n -> p s (q n)")
-            if b in SCALAR_STORES:
-                nc.scalar.copy(out=res[:], in_=src)
-            else:
-                nc.vector.tensor_copy(out=res[:], in_=src)
-            rows = out[tiles[0] * P : (tiles[-1] + 1) * P, f * A_HALF : (f + 1) * A_HALF]
-            nc.sync.dma_start(out=rows.rearrange("(s p) n -> p s n", p=P), in_=res[:])
-
-        def do_logits_half(h, f, bank):
-            cols = slice(f * A_HALF, (f + 1) * A_HALF)
-            zh = psum.tile([P, 2, A_HALF], F32, name="zh", tag=f"bank{bank}")
-            for i in range(2):
-                for c in range(X_PASSES):
-                    nc.tensor.matmul_mx(
-                        out=zh[:, i, :],
-                        lhsT=x_codes[h][:, c, i * P : (i + 1) * P].bitcast(FP8X4),
-                        lhsT_scale=x_scales[h][:, c, i * P : (i + 1) * P],
-                        rhs=w_codes[c][:, cols].bitcast(FP8X4),
-                        rhs_scale=w_scales[c][:, cols],
-                        start=(c == 0),
-                        stop=(c == X_PASSES - 1),
-                    )
-            nc.scalar.activation(out=sig_last[:, :, cols], in_=zh[:], func=SIGMOID)
-
-        def do_residual_half(h, i, f):
-            g, t = h // 2, 2 * (h % 2) + i
-            cols = slice(f * A_HALF, (f + 1) * A_HALF)
-            nc.vector.scalar_tensor_tensor(
-                out=gp[g][:, t, cols], in0=sig[h, i][:, cols], scalar=wt[:, g, t : t + 1], in1=aw[h, i][:, cols],
-                op0=MULT, op1=SUB,
+                out=g_codes[g][:, half_cols(f)].bitcast(FP8X4), scales=g_scales[g][:, half_cols(f)],
+                in_=gi[g, f][:].rearrange("p a t -> p (a t)"),
             )
 
         def do_out(b, g):
             f, tiles, bank = PIECES[b]
             if g == 0:
-                accs[b] = psum.tile([P, len(tiles), 2, P], F32, name="acc", tag=f"bank{bank}")
+                accs[b] = psum.tile([P, len(tiles), HALF], F32, name="acc", tag=f"bank{bank}")
             for s, m in enumerate(tiles):
-                for q in range(2):
-                    cols = slice((2 * f + q) * P, (2 * f + q + 1) * P)
-                    nc.tensor.matmul_mx(
-                        out=accs[b][:, s, q, :],
-                        lhsT=hw[g][:, 2 * P * m : 2 * P * (m + 1)].bitcast(FP4X4),
-                        lhsT_scale=hs[:, g, 32 * m : 32 * (m + 1)].bitcast(U8),
-                        rhs=g_codes[g][:, cols].bitcast(FP8X4),
-                        rhs_scale=g_scales[g][:, cols],
-                        start=(g == 0 and s == 0 and q == 0),
-                        stop=(g == GROUPS - 1 and s == len(tiles) - 1 and q == 1),
-                    )
+                nc.tensor.matmul_mx(
+                    out=accs[b][:, s, :],
+                    lhsT=hw[g][:, 2 * P * m : 2 * P * (m + 1)].bitcast(FP4X4),
+                    lhsT_scale=hs[:, g, 32 * m : 32 * (m + 1)].bitcast(U8),
+                    rhs=g_codes[g][:, half_cols(f)].bitcast(FP8X4),
+                    rhs_scale=g_scales[g][:, half_cols(f)],
+                    start=(g == 0 and s == 0),
+                    stop=(g == GROUPS - 1 and s == len(tiles) - 1),
+                )
+
+        def do_store(b, engine):
+            f, tiles, bank = PIECES[b]
+            res = one.tile([P, len(tiles), HALF], F32, align_bytes=64, name="res", bufs=RES_BUFS)
+            if engine == "scalar":
+                nc.scalar.copy(out=res[:], in_=accs[b][:])
+            else:
+                nc.vector.tensor_copy(out=res[:], in_=accs[b][:])
+            rows = out[tiles[0] * P : (tiles[-1] + 1) * P, half_cols(f)]
+            nc.sync.dma_start(out=rows.rearrange("(s p) n -> p s n", p=P), in_=res[:])
 
         def do_w_interleave(c, engine, lo, hi):
             interleave(engine, w_int[c][:, lo:hi, :], w_raw[c][:, :, lo:hi].rearrange("p j n -> p n j"))
@@ -342,138 +278,164 @@ def tile_clipped_policy_head_grad_s13_kernel(
             )
 
         last = GROUPS - 1
+        end = STEPS - 1
 
-        do_cast(0)
+        nc.vector.memset(ident[:], 0.0)
+        nc.vector.memset(zeros[:], 0.0)
+        nc.vector.memset(hs[:], 0)
+        make_identity(nc, ident[:], nomemset=True)
+        nc.scalar.activation(out=warm[:], in_=zeros[:, :1], func=SIGMOID)
+        idle = psum.tile([P, A], F32, name="idle", tag="bank7")
+        for k in range(WARM):
+            nc.tensor.matmul(idle[:], lhsT=zeros[:, :P], rhs=zeros[:], start=True, stop=True)
+
+        load_x(0)
+        load_x_scale()
+        load_w(0)
+        load_x(1)
+        load_w(1)
+        load_x(2)
+        load_x(3)
+        load_weight()
+        load_act(0, 0, 2)
+        load_x(4)
+        load_x(5)
+        load_act(0, 2, 4)
+        load_x(6)
+        load_act(1)
+        load_h_scales()
+        for g in range(GROUPS):
+            load_h(g)
+            for h in range(2 * g + 7, min(2 * g + 9, STEPS)):
+                load_x(h)
+            if g + 2 < GROUPS:
+                load_act(g + 2)
+
+        def turn_bank(h, c):
+            return c + (EARLY_BANKS[h % 3] if h < EARLY_STEPS else 0)
+
         for c in range(X_PASSES):
-            do_transposes(0, c)
-        do_cast(1)
+            do_cast(0, "vector", c * K_PASS, (c + 1) * K_PASS)
+            do_cast(0, "scalar", D + c * K_PASS, D + (c + 1) * K_PASS)
         for c in range(X_PASSES):
-            do_transposes(1, c)
+            do_turn(0, c, turn_bank(0, c))
         do_w_interleave(0, "gpsimd", 0, W_POOL)
         do_w_interleave(0, "scalar", W_POOL, A)
-        do_w_interleave(1, "scalar", 0, W_FIRST)
-        do_cast(2)
-        turned = psum.tile([P, 2, P], F32, name="turned", tag="bank7")
-        for u in range(2):
-            nc.tensor.transpose(turned[:, u, :], wt_rows[:].bitcast(F32)[:, u::2], ident[:])
-        nc.scalar.copy(
-            out=wt[:].rearrange("p g (u e) -> p g u e", e=2),
-            in_=turned[:].bitcast(BF16).rearrange("p u (g e) -> p g u e", e=2)[:, :GROUPS],
-        )
-        do_w_interleave(1, "scalar", W_FIRST, A)
+        do_cast(1)
+        do_w_interleave(1, "scalar", W_OWN, A)
         for c in range(X_PASSES):
             do_scale(0, c)
-        for c in range(X_PASSES):
-            do_transposes(2, c)
-            do_scale(1, c)
-        do_cast(3)
-        do_diag(0, 0)
-        for k in range(2 * POOL_DIAGS):
-            do_diag(k, 1)
-        do_quant_x(0)
+            do_turn(1, c, turn_bank(1, c))
+        do_cast(2)
+        do_quant_x(0, 0)
         do_quant_w(0)
-        do_quant_x(1)
+        do_w_interleave(1, "vector", 0, W_OWN)
+        do_quant_x(0, 1)
         do_quant_w(1)
-        do_diags_pool(POOL_DIAGS, GROUPS - 1)
         for c in range(X_PASSES):
             for i in range(2):
                 do_z(0, i, 2 + i, (c,))
-        for i in range(2):
-            do_aw(0, i, 4 + i)
+        for c in range(X_PASSES):
+            do_turn(2, c, turn_bank(2, c))
+        do_cast(3)
         for i in range(2):
             do_sigmoid(0, i)
-        gp[0] = two.tile([P, 4, A], BF16, align_bytes=64, name="gp")
         for c in range(X_PASSES):
-            do_scale(2, c)
-            do_transposes(3, c)
-            do_z(1, c, 6 + c)
+            do_scale(1, c)
         do_cast(4)
-        for i in range(2):
-            do_sigmoid(1, i)
-        do_residual(0, 0)
-        do_quant_x(2)
+        do_quant_x(1, 0)
+        nc.vector.tensor_copy(out=wt[:], in_=wt_raw[:])
+        do_quant_x(1, 1)
 
-        for h in range(STEADY, HALVES):
-            if h % 2 == 0:
-                gp[h // 2 - 1] = two.tile([P, 4, A], BF16, align_bytes=64, name="gp")
-                do_interleave((h - 4) // 2, "scalar", G_FIRST, A)
-            else:
-                do_cast(h + 2)
+        for h in range(STEADY, STEPS):
+            do_diff(h - 2, "gpsimd", OWN_COLS, 2 * A)
             do_z(h - 1, 0, 2)
             do_sigmoid(h - 1, 0)
-            if h == HALVES - 1:
-                for k in range(2):
-                    do_aw_sbuf(h, k)
+            if h < FIRST_OUT:
+                do_turn(h + 1, 0, turn_bank(h + 1, 0))
+            do_z(h - 1, 1, 3)
+            do_sigmoid(h - 1, 1)
             do_scale(h, 0)
-            do_pool_residual(h - 2, f"xg{(h - 1) % 2}" if h % 2 == 1 else f"sig{h % 3}")
-            if h >= FIRST_OUT:
-                for m in range(EARLY - 1) if h % 2 == 1 else (EARLY - 1,):
-                    do_out(m, (h - FIRST_OUT) // 2)
-            do_aw(h - 2, 1, turn_bank(h, 0))
-            do_transposes(h + 1, 0)
+            if FIRST_OUT <= h < end:
+                do_turn(h + 1, 0, turn_bank(h + 1, 0))
+            if h == end:
+                for b in range(4):
+                    do_out(b, last - 2)
+            elif h >= FIRST_OUT:
+                for b in (0, 1) if h % 2 == 1 else (2, 3):
+                    do_out(b, (h - FIRST_OUT) // 2)
             do_scale(h, 1)
-            do_z(h - 1, 1, turn_bank(h, 1) if h + 1 < HALVES else turn_bank(h, 2))
-            if h == STEADY:
-                do_residual(0, 1)
-            do_residual(h - 2, 1)
-            do_transposes(h + 1, 1)
-            if h % 2 == 0:
-                do_cast(h + 2)
-            if h == HALVES - 1:
-                do_sigmoid(h - 1, 1)
+            if h < end:
+                do_turn(h + 1, 1, turn_bank(h + 1, 1))
+            do_weigh(h - 2, 1, 0, "scalar")
+            if h + 3 < STEPS:
+                do_cast(h + 3)
+            do_diff(h - 2, "vector", 0, OWN_COLS)
+            if h % 2 == 0 and h >= 4:
+                do_quant_g((h - 4) // 2, 0)
+            do_quant_x(h, 0)
+            do_weigh(h - 2, 0, 0, "vector")
+            do_quant_x(h, 1)
             if h % 2 == 1:
-                do_interleave((h - 3) // 2, "scalar", 0, G_FIRST if h < HALVES - 1 else TAIL_A)
-            if h < HALVES - 1:
-                do_sigmoid(h - 1, 1)
-            if h == HALVES - 2:
-                for k in range(2):
-                    do_aw_sbuf(h, k)
-            do_quant_x(h)
-            if h >= 4 and h % 2 == 0:
-                do_quant_g((h - 4) // 2)
+                do_interleave((h - 3) // 2, 0, "scalar")
+            if h == end - 2:
+                do_weigh_late(0, "scalar")
+            if h == end - 1:
+                do_interleave(0, 1, "scalar")
 
-        h = HALVES - 1
-        gp[last] = two.tile([P, 4, A], BF16, align_bytes=64, name="gp")
-        do_out(EARLY - 1, last - 2)
-        for g in range(last - 2):
-            do_out(EARLY, g)
         for f in range(2):
-            do_logits_half(h, f, turn_bank(h, 1 - f))
-        do_out(EARLY, last - 2)
-        do_residual_half(h - 1, 0, 0)
-        do_interleave(last - 1, "vector", TAIL_A, A_HALF)
-        do_residual_half(h - 1, 1, 0)
-        do_residual_half(h - 1, 0, 1)
-        do_quant_g(last - 1, 0, A_HALF)
-        do_out(EARLY + 1, 0)
-        for b in range(EARLY):
-            do_out(b, last - 1)
+            do_z_half(end, f, 2 + f)
+            do_sigmoid_half(end, f)
+        do_diff_half(end - 1, 0)
+        do_quant_g(0, 1)
         for i in range(2):
-            do_residual_half(h, i, 0)
-        do_interleave(last, "scalar", 0, TAIL_SCALAR)
-        do_residual_half(h - 1, 1, 1)
-        do_interleave(last, "vector", TAIL_SCALAR, A_HALF)
-        do_residual_half(h, 0, 1)
-        do_quant_g(last, 0, A_HALF)
-        for g in range(1, last - 1):
-            do_out(EARLY + 1, g)
-        for g in range(PRE):
-            do_out(EARLY + 2, g)
-        for b in range(EARLY):
+            do_weigh(end - 1, i, 0, "vector")
+        do_weigh_late(1, "vector")
+        do_quant_g(last - 1, 0)
+        for b in (4, 5):
+            do_out(b, 0)
+        for b in range(4):
+            do_out(b, last - 1)
+        do_interleave(1, 1, "scalar")
+        do_diff_half(end, 0)
+        do_weigh_late(2, "vector")
+        for i in range(2):
+            do_weigh(end, i, 0, "vector")
+        do_diff_half(end - 1, 1)
+        do_interleave(last, 0, "scalar", 0, LAST_SPLIT)
+        do_interleave(last, 0, "vector", LAST_SPLIT, HALF)
+        do_interleave(2, 1, "scalar")
+        do_quant_g(1, 1)
+        do_quant_g(last, 0)
+        do_out(6, 0)
+        do_out(7, 0)
+        for b in range(4):
             do_out(b, last)
-        do_interleave(last - 1, "scalar", A_HALF, TAIL_B)
-        do_residual_half(h, 1, 1)
-        do_interleave(last - 1, "vector", TAIL_B, A)
-        do_store(0)
-        do_interleave(last, "vector", A_HALF, A)
-        do_store(1)
-        do_quant_g(last - 1, A_HALF, A)
-        do_quant_g(last, A_HALF, A)
-        for b in range(2, EARLY):
-            do_store(b)
-        for g in range(PRE, last - 1):
-            do_out(EARLY + 2, g)
-        for b in range(EARLY, len(PIECES)):
-            for g in range(last - 1 if b < EARLY + 3 else 0, GROUPS):
+        for b in (4, 5, 6, 7):
+            do_out(b, 1)
+        do_weigh_late(3, "vector")
+        do_diff_half(end, 1)
+        do_interleave(3, 1, "vector")
+        do_store(0, "scalar")
+        do_store(1, "scalar")
+        do_quant_g(2, 1)
+        do_weigh_late(4, "vector")
+        do_quant_g(3, 1)
+        do_store(2, "scalar")
+        do_interleave(4, 1, "scalar")
+        do_store(3, "scalar")
+        for h in (end - 1, end):
+            for i in range(2):
+                do_weigh(h, i, 1, "vector")
+        for g in (2, 3):
+            for b in (4, 5, 6, 7):
                 do_out(b, g)
-            do_store(b)
+        for g in range(last - 1):
+            do_out(8, g)
+        do_interleave(last, 1, "vector")
+        do_quant_g(4, 1)
+        do_quant_g(last, 1)
+        for b in range(4, len(PIECES)):
+            for g in (last - 1, last):
+                do_out(b, g)
+            do_store(b, "vector" if b % 2 == 0 else "scalar")

@@ -26,16 +26,15 @@ GROUPS = T // K_PASS
 STEPS = 2 * GROUPS
 X_PASSES = D // K_PASS
 HALF = A // 2
-POOL_COLS = 832
+POOL_COLS = 864
 OWN_COLS = 2 * A - POOL_COLS
 FIRST_POOL = 0
-CAST_BUFS = 5
+CAST_BUFS = 6
 XG_BUFS = 3
 CODE_BUFS = 6
 SIG_BUFS = 3
-GI_BUFS = 3
-PLANE_BUFS = 4
-RES_BUFS = 9
+GI_BUFS = 4
+PLANE_BUFS = 5
 WARM = 4
 W_POOL = 256
 W_OWN = 256
@@ -43,11 +42,15 @@ STEADY = 2
 EARLY_BANKS = (0, 4, 6)
 EARLY_STEPS = 6
 FIRST_OUT = 5
+QUARTER = A // 4
 PIECES = (
-    (0, (0, 1), 4), (0, (2, 3), 5), (0, (4, 5), 6), (0, (6, 7), 7),
-    (1, (0, 1), 0), (1, (2, 3), 1), (1, (4, 5), 2), (1, (6,), 3), (1, (7,), 4),
+    (0, HALF, (0, 1), 4), (0, HALF, (2, 3), 5), (0, HALF, (4, 5), 6), (0, HALF, (6, 7), 7),
+    (HALF, QUARTER, (0, 1, 2, 3), 0), (HALF, QUARTER, (4, 5, 6, 7), 1),
+    (HALF + QUARTER, QUARTER, (0, 1, 2, 3), 2), (HALF + QUARTER, QUARTER, (4, 5), 3),
+    (HALF + QUARTER, QUARTER, (6, 7), 4),
 )
 LAST_SPLIT = 96
+EXTRA_HALVES = 2
 
 
 def tile_clipped_policy_head_grad_s13_kernel(
@@ -64,12 +67,12 @@ def tile_clipped_policy_head_grad_s13_kernel(
         act = [keep.tile([P, 4, A], BF16, align_bytes=64, name=f"act{g}") for g in range(GROUPS)]
         hw = [keep.tile([P, 2 * D], U8, align_bytes=64, name=f"hw{g}") for g in range(GROUPS)]
         w_raw = [keep.tile([P, 4, A], BF16, align_bytes=64, name=f"w_raw{c}") for c in range(X_PASSES)]
-        w_int = [keep.tile([P, A, 4], BF16, align_bytes=64, name=f"w_int{c}") for c in range(X_PASSES)]
+        w_int = [one.tile([P, A, 4], BF16, align_bytes=64, name=f"w_int{c}") for c in range(X_PASSES)]
         w_codes = [keep.tile([P, A], U32, align_bytes=64, name=f"w_codes{c}") for c in range(X_PASSES)]
         w_scales = [keep.tile([P, A], U8, align_bytes=64, name=f"w_scales{c}") for c in range(X_PASSES)]
         g_codes = [keep.tile([P, A], U32, align_bytes=64, name=f"g_codes{g}") for g in range(GROUPS)]
         g_scales = [keep.tile([P, A], U8, align_bytes=64, name=f"g_scales{g}") for g in range(GROUPS)]
-        diff = [keep.tile([P, 2 * A], F32, align_bytes=64, name=f"diff{h}") for h in range(STEPS)]
+        diff = {h: keep.tile([P, 2 * A], F32, align_bytes=64, name=f"diff{h}") for h in range(STEPS - 2)}
         hs = keep.tile([P, GROUPS, D // 4], I32, align_bytes=64, name="hs")
         xs = keep.tile([P, X_PASSES, 2, 2], F32, align_bytes=64, name="xs")
         wt_raw = keep.tile([P, GROUPS, 4], BF16, align_bytes=64, name="wt_raw")
@@ -82,6 +85,14 @@ def tile_clipped_policy_head_grad_s13_kernel(
             g, lo = h // 2, 2 * (h % 2)
             src = x_bytes[g * K_PASS : (g + 1) * K_PASS, :].rearrange("(p t) k -> p (t k)", t=4)
             nc.sync.dma_start(out=x_raw[h][:], in_=src[:, lo * D : (lo + 2) * D])
+
+        def load_x_pass(h, c):
+            g, lo = h // 2, 2 * (h % 2)
+            cols = slice(c * K_PASS, (c + 1) * K_PASS)
+            src = x_bytes[g * K_PASS : (g + 1) * K_PASS, :].rearrange("(p t) k -> p t k", t=4)
+            nc.sync.dma_start(
+                out=x_raw[h][:].rearrange("p (i k) -> p i k", i=2)[:, :, cols], in_=src[:, lo : lo + 2, cols]
+            )
 
         def load_w(c):
             nc.sync.dma_start(
@@ -110,7 +121,7 @@ def tile_clipped_policy_head_grad_s13_kernel(
                 nc.sync.dma_start(out=hs[r:P:32, :, :], in_=scales_src[r])
 
         cast, turned, xg, x_codes, x_scales = {}, {}, {}, {}, {}
-        z, sig, planes, gi, accs = {}, {}, {}, {}, {}
+        z, sig, planes, gi, accs, diag, aw = {}, {}, {}, {}, {}, {}, {}
 
         def token_slot(h, i):
             return h // 2, 2 * (h % 2) + i
@@ -125,6 +136,10 @@ def tile_clipped_policy_head_grad_s13_kernel(
                 nc.vector.tensor_copy(out=cast[h][:, lo:hi], in_=x_raw[h][:, lo:hi].bitcast(FP8))
             else:
                 nc.scalar.copy(out=cast[h][:, lo:hi], in_=x_raw[h][:, lo:hi].bitcast(FP8))
+
+        def do_cast_half(k):
+            if k < 2 * STEPS:
+                do_cast(k // 2, "scalar", (k % 2) * D, (k % 2 + 1) * D)
 
         def do_turn(h, c, bank):
             turned[h, c] = psum.tile([P, 2, 2 * P], F32, name="turned", tag=f"bank{bank}")
@@ -198,31 +213,51 @@ def tile_clipped_policy_head_grad_s13_kernel(
             op = nc.gpsimd.tensor_tensor if engine == "gpsimd" else nc.vector.tensor_tensor
             op(out=diff[h][:, lo:hi], in0=sig[h][:, lo:hi], in1=taken[:, lo:hi], op=SUB)
 
-        def do_diff_half(h, f):
-            g, t = token_slot(h, 0)
-            nc.vector.tensor_tensor(
-                out=diff[h][:].rearrange("p (i a) -> p i a", i=2)[:, :, half_cols(f)],
-                in0=sig[h][:].rearrange("p (i a) -> p i a", i=2)[:, :, half_cols(f)],
-                in1=act[g][:, t : t + 2, half_cols(f)],
-                op=SUB,
-            )
-
-        def do_weigh(h, i, f, engine):
-            g, t = token_slot(h, i)
+        def plane_tile(g, f):
             if (g, f) not in planes:
                 planes[g, f] = one.tile([P, 4, HALF], BF16, align_bytes=64, name="planes", bufs=PLANE_BUFS)
-            src = diff[h][:, i * A + f * HALF : i * A + (f + 1) * HALF]
-            if engine == "scalar":
-                nc.scalar.activation(out=planes[g, f][:, t, :], in_=src, func=COPY, scale=wt[:, g, t : t + 1])
-            else:
-                nc.vector.tensor_scalar(
-                    out=planes[g, f][:, t, :], in0=src, scalar1=wt[:, g, t : t + 1], scalar2=None, op0=MULT
-                )
+            return planes[g, f]
 
-        def do_weigh_late(g, engine):
+        def do_weigh(h, i, f, engine, lo=0, hi=HALF):
+            g, t = token_slot(h, i)
+            src = diff[h][:, i * A + f * HALF + lo : i * A + f * HALF + hi]
+            dst = plane_tile(g, f)[:, t, lo:hi]
+            if engine == "scalar":
+                nc.scalar.activation(out=dst, in_=src, func=COPY, scale=wt[:, g, t : t + 1])
+            else:
+                nc.vector.tensor_scalar(out=dst, in0=src, scalar1=wt[:, g, t : t + 1], scalar2=None, op0=MULT)
+
+        def do_diag(h, i):
+            g, t = token_slot(h, i)
+            diag[h, i] = keep.tile([P, P], BF16, align_bytes=64, name=f"diag{h}_{i}")
+            nc.scalar.activation(out=diag[h, i][:], in_=ident[:], func=COPY, scale=wt[:, g, t : t + 1])
+
+        def do_aw(h, i, bank):
+            g, t = token_slot(h, i)
+            aw[h, i] = psum.tile([P, A], F32, name="aw", tag=f"bank{bank}")
+            nc.tensor.matmul(aw[h, i][:], lhsT=diag[h, i][:], rhs=act[g][:, t, :], start=True, stop=True)
+
+        def do_aw_pool(h, slot):
+            tile = one.tile([P, 2, A], F32, align_bytes=64, name="aw_pool", tag=slot)
+            for i in range(2):
+                g, t = token_slot(h, i)
+                nc.gpsimd.tensor_scalar(
+                    out=tile[:, i, :], in0=act[g][:, t, :], scalar1=wt[:, g, t : t + 1], scalar2=0.0,
+                    op0=MULT, op1=ADD,
+                )
+                aw[h, i] = tile[:, i, :]
+
+        def do_residual(h, i, f, lo=0, hi=HALF):
+            g, t = token_slot(h, i)
+            nc.vector.scalar_tensor_tensor(
+                out=plane_tile(g, f)[:, t, lo:hi], in0=sig[h][:, i * A + f * HALF + lo : i * A + f * HALF + hi],
+                scalar=wt[:, g, t : t + 1], in1=aw[h, i][:, f * HALF + lo : f * HALF + hi], op0=MULT, op1=SUB,
+            )
+
+        def do_weigh_late(g, engine, lo=0, hi=HALF):
             for h in (2 * g, 2 * g + 1):
                 for i in range(2):
-                    do_weigh(h, i, 1, engine)
+                    do_weigh(h, i, 1, engine, lo, hi)
 
         def interleave(engine, dst, src):
             if engine == "vector":
@@ -237,35 +272,37 @@ def tile_clipped_policy_head_grad_s13_kernel(
                 gi[g, f] = one.tile([P, HALF, 4], BF16, align_bytes=64, name="gi", bufs=GI_BUFS)
             interleave(engine, gi[g, f][:, lo:hi, :], planes[g, f][:, :, lo:hi].rearrange("p t a -> p a t"))
 
-        def do_quant_g(g, f):
+        def do_quant_g(g, f, lo=0, hi=HALF):
+            cols = slice(f * HALF + lo, f * HALF + hi)
             nc.vector.quantize_mx(
-                out=g_codes[g][:, half_cols(f)].bitcast(FP8X4), scales=g_scales[g][:, half_cols(f)],
-                in_=gi[g, f][:].rearrange("p a t -> p (a t)"),
+                out=g_codes[g][:, cols].bitcast(FP8X4), scales=g_scales[g][:, cols],
+                in_=gi[g, f][:, lo:hi, :].rearrange("p a t -> p (a t)"),
             )
 
         def do_out(b, g):
-            f, tiles, bank = PIECES[b]
+            lo, width, tiles, bank = PIECES[b]
+            cols = slice(lo, lo + width)
             if g == 0:
-                accs[b] = psum.tile([P, len(tiles), HALF], F32, name="acc", tag=f"bank{bank}")
+                accs[b] = psum.tile([P, len(tiles), width], F32, name="acc", tag=f"bank{bank}")
             for s, m in enumerate(tiles):
                 nc.tensor.matmul_mx(
                     out=accs[b][:, s, :],
                     lhsT=hw[g][:, 2 * P * m : 2 * P * (m + 1)].bitcast(FP4X4),
                     lhsT_scale=hs[:, g, 32 * m : 32 * (m + 1)].bitcast(U8),
-                    rhs=g_codes[g][:, half_cols(f)].bitcast(FP8X4),
-                    rhs_scale=g_scales[g][:, half_cols(f)],
+                    rhs=g_codes[g][:, cols].bitcast(FP8X4),
+                    rhs_scale=g_scales[g][:, cols],
                     start=(g == 0 and s == 0),
                     stop=(g == GROUPS - 1 and s == len(tiles) - 1),
                 )
 
         def do_store(b, engine):
-            f, tiles, bank = PIECES[b]
-            res = one.tile([P, len(tiles), HALF], F32, align_bytes=64, name="res", bufs=RES_BUFS)
+            lo, width, tiles, bank = PIECES[b]
+            res = keep.tile([P, len(tiles), width], F32, align_bytes=64, name=f"res{b}")
             if engine == "scalar":
                 nc.scalar.copy(out=res[:], in_=accs[b][:])
             else:
                 nc.vector.tensor_copy(out=res[:], in_=accs[b][:])
-            rows = out[tiles[0] * P : (tiles[-1] + 1) * P, half_cols(f)]
+            rows = out[tiles[0] * P : (tiles[-1] + 1) * P, lo : lo + width]
             nc.sync.dma_start(out=rows.rearrange("(s p) n -> p s n", p=P), in_=res[:])
 
         def do_w_interleave(c, engine, lo, hi):
@@ -292,11 +329,12 @@ def tile_clipped_policy_head_grad_s13_kernel(
         load_x(0)
         load_x_scale()
         load_w(0)
+        load_weight()
         load_x(1)
         load_w(1)
         load_x(2)
+        load_act(GROUPS - 1, 2, 4)
         load_x(3)
-        load_weight()
         load_act(0, 0, 2)
         load_x(4)
         load_x(5)
@@ -309,7 +347,7 @@ def tile_clipped_policy_head_grad_s13_kernel(
             for h in range(2 * g + 7, min(2 * g + 9, STEPS)):
                 load_x(h)
             if g + 2 < GROUPS:
-                load_act(g + 2)
+                load_act(g + 2, 0, 4 if g + 2 < GROUPS - 1 else 2)
 
         def turn_bank(h, c):
             return c + (EARLY_BANKS[h % 3] if h < EARLY_STEPS else 0)
@@ -322,6 +360,7 @@ def tile_clipped_policy_head_grad_s13_kernel(
         do_w_interleave(0, "gpsimd", 0, W_POOL)
         do_w_interleave(0, "scalar", W_POOL, A)
         do_cast(1)
+        nc.scalar.copy(out=wt[:], in_=wt_raw[:])
         do_w_interleave(1, "scalar", W_OWN, A)
         for c in range(X_PASSES):
             do_scale(0, c)
@@ -332,6 +371,7 @@ def tile_clipped_policy_head_grad_s13_kernel(
         do_w_interleave(1, "vector", 0, W_OWN)
         do_quant_x(0, 1)
         do_quant_w(1)
+        do_aw_pool(STEPS - 1, "w_int1")
         for c in range(X_PASSES):
             for i in range(2):
                 do_z(0, i, 2 + i, (c,))
@@ -339,18 +379,24 @@ def tile_clipped_policy_head_grad_s13_kernel(
             do_turn(2, c, turn_bank(2, c))
         do_cast(3)
         for i in range(2):
+            do_diag(STEPS - 2, i)
+        for i in range(2):
             do_sigmoid(0, i)
         for c in range(X_PASSES):
             do_scale(1, c)
         do_cast(4)
         do_quant_x(1, 0)
-        nc.vector.tensor_copy(out=wt[:], in_=wt_raw[:])
         do_quant_x(1, 1)
 
         for h in range(STEADY, STEPS):
+            extra = min(h - STEADY, EXTRA_HALVES)
+            first_half = 2 * (h + 3) + extra
             do_diff(h - 2, "gpsimd", OWN_COLS, 2 * A)
             do_z(h - 1, 0, 2)
             do_sigmoid(h - 1, 0)
+            if extra < EXTRA_HALVES:
+                do_cast_half(first_half)
+                first_half = first_half + 1
             if h < FIRST_OUT:
                 do_turn(h + 1, 0, turn_bank(h + 1, 0))
             do_z(h - 1, 1, 3)
@@ -361,81 +407,101 @@ def tile_clipped_policy_head_grad_s13_kernel(
             if h == end:
                 for b in range(4):
                     do_out(b, last - 2)
+                do_aw(end - 1, 0, 0)
             elif h >= FIRST_OUT:
                 for b in (0, 1) if h % 2 == 1 else (2, 3):
                     do_out(b, (h - FIRST_OUT) // 2)
             do_scale(h, 1)
             if h < end:
                 do_turn(h + 1, 1, turn_bank(h + 1, 1))
+            if h == end:
+                do_interleave(1, 1, "scalar")
             do_weigh(h - 2, 1, 0, "scalar")
-            if h + 3 < STEPS:
-                do_cast(h + 3)
+            for k in range(2):
+                do_cast_half(first_half + k)
+            if h == end:
+                break
             do_diff(h - 2, "vector", 0, OWN_COLS)
             if h % 2 == 0 and h >= 4:
                 do_quant_g((h - 4) // 2, 0)
             do_quant_x(h, 0)
             do_weigh(h - 2, 0, 0, "vector")
             do_quant_x(h, 1)
+            if h == end - 2:
+                for i in range(2):
+                    do_weigh(2, i, 1, "scalar")
             if h % 2 == 1:
                 do_interleave((h - 3) // 2, 0, "scalar")
-            if h == end - 2:
+            if h == end - 3:
                 do_weigh_late(0, "scalar")
+            if h == end - 2:
+                for i in range(2):
+                    do_weigh(3, i, 1, "scalar")
             if h == end - 1:
                 do_interleave(0, 1, "scalar")
 
+        do_aw(end - 1, 1, 1)
+        for c in range(X_PASSES):
+            do_quant_x(end, c)
+        do_quant_g(0, 1)
         for f in range(2):
             do_z_half(end, f, 2 + f)
-            do_sigmoid_half(end, f)
-        do_diff_half(end - 1, 0)
-        do_quant_g(0, 1)
-        for i in range(2):
-            do_weigh(end - 1, i, 0, "vector")
-        do_weigh_late(1, "vector")
-        do_quant_g(last - 1, 0)
-        for b in (4, 5):
+        do_sigmoid_half(end, 0)
+        do_diff(end - 2, "vector", 0, OWN_COLS)
+        do_residual(end - 1, 0, 0)
+        do_weigh(end - 2, 0, 0, "vector")
+        do_residual(end - 1, 0, 1)
+        do_interleave(last - 1, 0, "scalar")
+        do_sigmoid_half(end, 1)
+        for f in range(2):
+            do_residual(end - 1, 1, f)
+        do_quant_g(1, 1)
+        for b in (4, 6, 5):
             do_out(b, 0)
-        for b in range(4):
-            do_out(b, last - 1)
-        do_interleave(1, 1, "scalar")
-        do_diff_half(end, 0)
-        do_weigh_late(2, "vector")
+        for b in (4, 5, 6):
+            do_out(b, 1)
         for i in range(2):
-            do_weigh(end, i, 0, "vector")
-        do_diff_half(end - 1, 1)
+            do_residual(end, i, 0)
+        for i in range(2):
+            do_weigh(4, i, 1, "vector")
+        do_quant_g(last - 1, 0)
         do_interleave(last, 0, "scalar", 0, LAST_SPLIT)
         do_interleave(last, 0, "vector", LAST_SPLIT, HALF)
-        do_interleave(2, 1, "scalar")
-        do_quant_g(1, 1)
+        for i in range(2):
+            do_weigh(5, i, 1, "vector")
         do_quant_g(last, 0)
-        do_out(6, 0)
-        do_out(7, 0)
+        do_weigh_late(3, "scalar")
+        for b in range(3):
+            do_out(b, last - 1)
         for b in range(4):
+            if b >= 3:
+                do_out(b, last - 1)
             do_out(b, last)
-        for b in (4, 5, 6, 7):
-            do_out(b, 1)
-        do_weigh_late(3, "vector")
-        do_diff_half(end, 1)
-        do_interleave(3, 1, "vector")
-        do_store(0, "scalar")
-        do_store(1, "scalar")
-        do_quant_g(2, 1)
+        for g in range(2):
+            do_out(7, g)
         do_weigh_late(4, "vector")
-        do_quant_g(3, 1)
-        do_store(2, "scalar")
-        do_interleave(4, 1, "scalar")
-        do_store(3, "scalar")
-        for h in (end - 1, end):
-            for i in range(2):
-                do_weigh(h, i, 1, "vector")
-        for g in (2, 3):
-            for b in (4, 5, 6, 7):
-                do_out(b, g)
-        for g in range(last - 1):
+        for i in range(2):
+            do_residual(end, i, 1)
+        for b in range(4):
+            do_store(b, "scalar")
+        for g in range(2):
             do_out(8, g)
-        do_interleave(last, 1, "vector")
-        do_quant_g(4, 1)
-        do_quant_g(last, 1)
-        for b in range(4, len(PIECES)):
-            for g in (last - 1, last):
+        for lo in (0, QUARTER):
+            for g in range(2, GROUPS):
+                engine = "scalar" if lo > 0 and g in (3, 4) else "vector"
+                do_interleave(g, 1, engine, lo, lo + QUARTER)
+                if g > 2:
+                    do_quant_g(g - 1, 1, lo, lo + QUARTER)
+            do_quant_g(last, 1, lo, lo + QUARTER)
+        for g in (2, 3):
+            for b in (4, 5):
+                do_out(b, g)
+        for b in (4, 5):
+            for g in (4, 5):
+                do_out(b, g)
+        do_store(4, "scalar")
+        do_store(5, "scalar")
+        for b in range(6, len(PIECES)):
+            for g in range(2, GROUPS):
                 do_out(b, g)
             do_store(b, "vector" if b % 2 == 0 else "scalar")

@@ -36,7 +36,7 @@ SIG_BUFS = 3
 GI_BUFS = 4
 PLANE_BUFS = 5
 WARM = 4
-W_POOL = 256
+W_POOL = 192
 W_OWN = 256
 STEADY = 2
 EARLY_BANKS = (0, 4, 6)
@@ -47,10 +47,10 @@ PIECES = (
     (0, HALF, (0, 1), 4), (0, HALF, (2, 3), 5), (0, HALF, (4, 5), 6), (0, HALF, (6, 7), 7),
     (HALF, QUARTER, (0, 1, 2, 3), 0), (HALF, QUARTER, (4, 5, 6, 7), 1),
     (HALF + QUARTER, QUARTER, (0, 1, 2, 3), 2), (HALF + QUARTER, QUARTER, (4, 5), 3),
-    (HALF + QUARTER, QUARTER, (6, 7), 4),
+    (HALF + QUARTER, QUARTER, (6,), 4), (HALF + QUARTER, QUARTER, (7,), 5),
 )
 LAST_SPLIT = 96
-EXTRA_HALVES = 2
+HEAD_CASTS = 5
 
 
 def tile_clipped_policy_head_grad_s13_kernel(
@@ -328,9 +328,9 @@ def tile_clipped_policy_head_grad_s13_kernel(
 
         load_x(0)
         load_x_scale()
+        load_x(1)
         load_w(0)
         load_weight()
-        load_x(1)
         load_w(1)
         load_x(2)
         load_act(GROUPS - 1, 2, 4)
@@ -357,11 +357,11 @@ def tile_clipped_policy_head_grad_s13_kernel(
             do_cast(0, "scalar", D + c * K_PASS, D + (c + 1) * K_PASS)
         for c in range(X_PASSES):
             do_turn(0, c, turn_bank(0, c))
+        do_cast(1)
         do_w_interleave(0, "gpsimd", 0, W_POOL)
         do_w_interleave(0, "scalar", W_POOL, A)
-        do_cast(1)
-        nc.scalar.copy(out=wt[:], in_=wt_raw[:])
         do_w_interleave(1, "scalar", W_OWN, A)
+        nc.scalar.copy(out=wt[:], in_=wt_raw[:])
         for c in range(X_PASSES):
             do_scale(0, c)
             do_turn(1, c, turn_bank(1, c))
@@ -388,88 +388,88 @@ def tile_clipped_policy_head_grad_s13_kernel(
         do_quant_x(1, 0)
         do_quant_x(1, 1)
 
+        halves = list(range(2 * HEAD_CASTS, 2 * STEPS))
+        early_late = [(h, i) for h in range(2) for i in range(2)]
         for h in range(STEADY, STEPS):
-            extra = min(h - STEADY, EXTRA_HALVES)
-            first_half = 2 * (h + 3) + extra
             do_diff(h - 2, "gpsimd", OWN_COLS, 2 * A)
             do_z(h - 1, 0, 2)
             do_sigmoid(h - 1, 0)
-            if extra < EXTRA_HALVES:
-                do_cast_half(first_half)
-                first_half = first_half + 1
+            if h < STEADY + 2:
+                do_cast_half(halves.pop(0))
             if h < FIRST_OUT:
                 do_turn(h + 1, 0, turn_bank(h + 1, 0))
             do_z(h - 1, 1, 3)
             do_sigmoid(h - 1, 1)
+            pieces = []
+            if h >= FIRST_OUT:
+                pieces = [0, 1] if h % 2 == 1 else [2, 3]
+            if h == end:
+                pieces = [0, 1, 2, 3]
+            before = len(pieces) if h % 2 == 1 else 1
+            for b in pieces[:before]:
+                do_out(b, (h - FIRST_OUT) // 2)
             do_scale(h, 0)
             if FIRST_OUT <= h < end:
                 do_turn(h + 1, 0, turn_bank(h + 1, 0))
+            for b in pieces[before:]:
+                do_out(b, (h - FIRST_OUT) // 2)
             if h == end:
-                for b in range(4):
-                    do_out(b, last - 2)
                 do_aw(end - 1, 0, 0)
-            elif h >= FIRST_OUT:
-                for b in (0, 1) if h % 2 == 1 else (2, 3):
-                    do_out(b, (h - FIRST_OUT) // 2)
             do_scale(h, 1)
             if h < end:
                 do_turn(h + 1, 1, turn_bank(h + 1, 1))
-            if h == end:
-                do_interleave(1, 1, "scalar")
             do_weigh(h - 2, 1, 0, "scalar")
-            for k in range(2):
-                do_cast_half(first_half + k)
             if h == end:
                 break
+            for k in range(min(1 if h % 2 == 1 else 2, len(halves))):
+                do_cast_half(halves.pop(0))
+            if h >= 4 and early_late and (h % 2 == 0 or not halves):
+                do_weigh(*early_late.pop(0), 1, "scalar")
             do_diff(h - 2, "vector", 0, OWN_COLS)
             if h % 2 == 0 and h >= 4:
                 do_quant_g((h - 4) // 2, 0)
             do_quant_x(h, 0)
             do_weigh(h - 2, 0, 0, "vector")
             do_quant_x(h, 1)
-            if h == end - 2:
-                for i in range(2):
-                    do_weigh(2, i, 1, "scalar")
             if h % 2 == 1:
                 do_interleave((h - 3) // 2, 0, "scalar")
-            if h == end - 3:
-                do_weigh_late(0, "scalar")
-            if h == end - 2:
-                for i in range(2):
-                    do_weigh(3, i, 1, "scalar")
             if h == end - 1:
                 do_interleave(0, 1, "scalar")
+                for i in range(2):
+                    do_weigh(2, i, 1, "scalar")
 
         do_aw(end - 1, 1, 1)
+        for i in range(2):
+            do_weigh(3, i, 1, "scalar")
         for c in range(X_PASSES):
             do_quant_x(end, c)
+        do_diff(end - 2, "vector", 0, OWN_COLS)
         do_quant_g(0, 1)
+        do_weigh(end - 2, 0, 0, "vector")
         for f in range(2):
             do_z_half(end, f, 2 + f)
         do_sigmoid_half(end, 0)
-        do_diff(end - 2, "vector", 0, OWN_COLS)
-        do_residual(end - 1, 0, 0)
-        do_weigh(end - 2, 0, 0, "vector")
-        do_residual(end - 1, 0, 1)
+        for f in range(2):
+            do_residual(end - 1, 0, f)
         do_interleave(last - 1, 0, "scalar")
         do_sigmoid_half(end, 1)
-        for f in range(2):
-            do_residual(end - 1, 1, f)
+        do_residual(end - 1, 1, 0)
+        do_interleave(1, 1, "vector")
+        do_residual(end - 1, 1, 1)
         do_quant_g(1, 1)
-        for b in (4, 6, 5):
-            do_out(b, 0)
-        for b in (4, 5, 6):
-            do_out(b, 1)
+        for g in range(2):
+            for b in (4, 6, 5):
+                do_out(b, g)
         for i in range(2):
             do_residual(end, i, 0)
-        for i in range(2):
-            do_weigh(4, i, 1, "vector")
         do_quant_g(last - 1, 0)
         do_interleave(last, 0, "scalar", 0, LAST_SPLIT)
         do_interleave(last, 0, "vector", LAST_SPLIT, HALF)
         for i in range(2):
-            do_weigh(5, i, 1, "vector")
+            do_weigh(4, i, 1, "vector")
         do_quant_g(last, 0)
+        for i in range(2):
+            do_weigh(5, i, 1, "vector")
         do_weigh_late(3, "scalar")
         for b in range(3):
             do_out(b, last - 1)
@@ -477,31 +477,38 @@ def tile_clipped_policy_head_grad_s13_kernel(
             if b >= 3:
                 do_out(b, last - 1)
             do_out(b, last)
-        for g in range(2):
-            do_out(7, g)
-        do_weigh_late(4, "vector")
-        for i in range(2):
-            do_residual(end, i, 1)
         for b in range(4):
             do_store(b, "scalar")
-        for g in range(2):
-            do_out(8, g)
-        for lo in (0, QUARTER):
-            for g in range(2, GROUPS):
-                engine = "scalar" if lo > 0 and g in (3, 4) else "vector"
-                do_interleave(g, 1, engine, lo, lo + QUARTER)
-                if g > 2:
-                    do_quant_g(g - 1, 1, lo, lo + QUARTER)
-            do_quant_g(last, 1, lo, lo + QUARTER)
+        do_weigh_late(4, "vector", 0, QUARTER)
+        do_interleave(2, 1, "vector", 0, QUARTER)
+        for i in range(2):
+            do_residual(end, i, 1, 0, QUARTER)
+        do_quant_g(2, 1, 0, QUARTER)
+        for g in range(3, GROUPS):
+            do_interleave(g, 1, "vector", 0, QUARTER)
+            if g > 3:
+                do_quant_g(g - 1, 1, 0, QUARTER)
+        do_weigh_late(4, "vector", QUARTER, HALF)
+        do_quant_g(last, 1, 0, QUARTER)
+        for g in (2, 3):
+            do_interleave(g, 1, "scalar", QUARTER, HALF)
+        for i in range(2):
+            do_residual(end, i, 1, QUARTER, HALF)
+        for g in (4, 5):
+            do_interleave(g, 1, "vector", QUARTER, HALF)
+            do_quant_g(g - 2, 1, QUARTER, HALF)
+        for g in (4, 5):
+            do_quant_g(g, 1, QUARTER, HALF)
         for g in (2, 3):
             for b in (4, 5):
                 do_out(b, g)
+            do_out(7, g - 2)
         for b in (4, 5):
             for g in (4, 5):
                 do_out(b, g)
         do_store(4, "scalar")
         do_store(5, "scalar")
         for b in range(6, len(PIECES)):
-            for g in range(2, GROUPS):
+            for g in range(2 if b < 8 else 0, GROUPS):
                 do_out(b, g)
             do_store(b, "vector" if b % 2 == 0 else "scalar")

@@ -26,15 +26,15 @@ GROUPS = T // K_PASS
 STEPS = 2 * GROUPS
 X_PASSES = D // K_PASS
 HALF = A // 2
-POOL_COLS = 864
-OWN_COLS = 2 * A - POOL_COLS
+POOL_COLS = 896
+DEFER_FROM = 2
 FIRST_POOL = 0
-CAST_BUFS = 6
+CAST_BUFS = 5
 XG_BUFS = 3
 CODE_BUFS = 6
-SIG_BUFS = 3
-GI_BUFS = 4
-PLANE_BUFS = 5
+SIG_BUFS = 10
+GI_BUFS = 5
+PLANE_BUFS = 4
 WARM = 4
 W_POOL = 192
 W_OWN = 256
@@ -72,7 +72,8 @@ def tile_clipped_policy_head_grad_s13_kernel(
         w_scales = [keep.tile([P, A], U8, align_bytes=64, name=f"w_scales{c}") for c in range(X_PASSES)]
         g_codes = [keep.tile([P, A], U32, align_bytes=64, name=f"g_codes{g}") for g in range(GROUPS)]
         g_scales = [keep.tile([P, A], U8, align_bytes=64, name=f"g_scales{g}") for g in range(GROUPS)]
-        diff = {h: keep.tile([P, 2 * A], F32, align_bytes=64, name=f"diff{h}") for h in range(STEPS - 2)}
+        diff_g = [keep.tile([P, 4 * A], F32, align_bytes=64, name=f"diff{g}") for g in range(GROUPS - 1)]
+        diff = [diff_g[h // 2][:, (h % 2) * 2 * A : (h % 2 + 1) * 2 * A] for h in range(STEPS - 2)]
         hs = keep.tile([P, GROUPS, D // 4], I32, align_bytes=64, name="hs")
         xs = keep.tile([P, X_PASSES, 2, 2], F32, align_bytes=64, name="xs")
         wt_raw = keep.tile([P, GROUPS, 4], BF16, align_bytes=64, name="wt_raw")
@@ -121,7 +122,7 @@ def tile_clipped_policy_head_grad_s13_kernel(
                 nc.sync.dma_start(out=hs[r:P:32, :, :], in_=scales_src[r])
 
         cast, turned, xg, x_codes, x_scales = {}, {}, {}, {}, {}
-        z, sig, planes, gi, accs, diag, aw = {}, {}, {}, {}, {}, {}, {}
+        z, sig, planes, gi, accs, diag, aw, pairs = {}, {}, {}, {}, {}, {}, {}, {}
 
         def token_slot(h, i):
             return h // 2, 2 * (h % 2) + i
@@ -152,7 +153,7 @@ def tile_clipped_policy_head_grad_s13_kernel(
 
         def do_scale(h, c):
             if c == 0 and FIRST_POOL <= h - 1 < STEPS - 2:
-                xg[h, c] = diff[h - 1][:, A:].bitcast(BF16).rearrange("p (r u e) -> p r u e", u=2, e=2)
+                xg[h, c] = diff[h - 1][:, :A].bitcast(BF16).rearrange("p (r u e) -> p r u e", u=2, e=2)
             else:
                 tile = one.tile([P, 2 * P, 2, 2], BF16, align_bytes=64, name="xg", bufs=XG_BUFS)
                 xg[h, c] = tile[:]
@@ -254,10 +255,18 @@ def tile_clipped_policy_head_grad_s13_kernel(
                 scalar=wt[:, g, t : t + 1], in1=aw[h, i][:, f * HALF + lo : f * HALF + hi], op0=MULT, op1=SUB,
             )
 
-        def do_weigh_late(g, engine, lo=0, hi=HALF):
+        def do_weigh_late(g, engine):
             for h in (2 * g, 2 * g + 1):
                 for i in range(2):
-                    do_weigh(h, i, 1, engine, lo, hi)
+                    do_weigh(h, i, 1, engine)
+
+        def do_weigh_pair(g, i, engine, lo=0, hi=HALF):
+            for h in (2 * g, 2 * g + 1):
+                do_weigh(h, i, 1, engine, lo, hi)
+
+        def do_diff_rest(g):
+            for h in (2 * g, 2 * g + 1):
+                do_diff(h, "vector", POOL_COLS, 2 * A)
 
         def interleave(engine, dst, src):
             if engine == "vector":
@@ -272,6 +281,16 @@ def tile_clipped_policy_head_grad_s13_kernel(
                 gi[g, f] = one.tile([P, HALF, 4], BF16, align_bytes=64, name="gi", bufs=GI_BUFS)
             interleave(engine, gi[g, f][:, lo:hi, :], planes[g, f][:, :, lo:hi].rearrange("p t a -> p a t"))
 
+        def do_weigh_turn(g, lo, hi):
+            if (g, 1) not in gi:
+                gi[g, 1] = one.tile([P, HALF, 4], BF16, align_bytes=64, name="gi", bufs=GI_BUFS)
+            nc.vector.tensor_tensor(
+                out=gi[g, 1][:, lo:hi, :],
+                in0=diff_g[g][:].rearrange("p (t a) -> p a t", t=4)[:, HALF + lo : HALF + hi, :],
+                in1=wt[:, g, :].unsqueeze(1).to_broadcast([P, hi - lo, 4]),
+                op=MULT,
+            )
+
         def do_quant_g(g, f, lo=0, hi=HALF):
             cols = slice(f * HALF + lo, f * HALF + hi)
             nc.vector.quantize_mx(
@@ -282,6 +301,7 @@ def tile_clipped_policy_head_grad_s13_kernel(
         def do_out(b, g):
             lo, width, tiles, bank = PIECES[b]
             cols = slice(lo, lo + width)
+            closing = GROUPS - 1 if lo < HALF + QUARTER else GROUPS - 2
             if g == 0:
                 accs[b] = psum.tile([P, len(tiles), width], F32, name="acc", tag=f"bank{bank}")
             for s, m in enumerate(tiles):
@@ -292,18 +312,21 @@ def tile_clipped_policy_head_grad_s13_kernel(
                     rhs=g_codes[g][:, cols].bitcast(FP8X4),
                     rhs_scale=g_scales[g][:, cols],
                     start=(g == 0 and s == 0),
-                    stop=(g == GROUPS - 1 and s == len(tiles) - 1),
+                    stop=(g == closing and s == len(tiles) - 1),
                 )
 
         def do_store(b, engine):
             lo, width, tiles, bank = PIECES[b]
-            res = keep.tile([P, len(tiles), width], F32, align_bytes=64, name=f"res{b}")
+            if b // 2 not in pairs:
+                pairs[b // 2] = one.tile([P, 2 * A], F32, align_bytes=64, name="res", tag="cast", bufs=CAST_BUFS)
+            at = (b % 2) * A
+            res = pairs[b // 2][:, at : at + len(tiles) * width].rearrange("p (s n) -> p s n", n=width)
             if engine == "scalar":
-                nc.scalar.copy(out=res[:], in_=accs[b][:])
+                nc.scalar.copy(out=res, in_=accs[b][:])
             else:
-                nc.vector.tensor_copy(out=res[:], in_=accs[b][:])
+                nc.vector.tensor_copy(out=res, in_=accs[b][:])
             rows = out[tiles[0] * P : (tiles[-1] + 1) * P, lo : lo + width]
-            nc.sync.dma_start(out=rows.rearrange("(s p) n -> p s n", p=P), in_=res[:])
+            nc.sync.dma_start(out=rows.rearrange("(s p) n -> p s n", p=P), in_=res)
 
         def do_w_interleave(c, engine, lo, hi):
             interleave(engine, w_int[c][:, lo:hi, :], w_raw[c][:, :, lo:hi].rearrange("p j n -> p n j"))
@@ -389,9 +412,8 @@ def tile_clipped_policy_head_grad_s13_kernel(
         do_quant_x(1, 1)
 
         halves = list(range(2 * HEAD_CASTS, 2 * STEPS))
-        early_late = [(h, i) for h in range(2) for i in range(2)]
         for h in range(STEADY, STEPS):
-            do_diff(h - 2, "gpsimd", OWN_COLS, 2 * A)
+            do_diff(h - 2, "gpsimd", 0, POOL_COLS)
             do_z(h - 1, 0, 2)
             do_sigmoid(h - 1, 0)
             if h < STEADY + 2:
@@ -405,27 +427,25 @@ def tile_clipped_policy_head_grad_s13_kernel(
                 pieces = [0, 1] if h % 2 == 1 else [2, 3]
             if h == end:
                 pieces = [0, 1, 2, 3]
-            before = len(pieces) if h % 2 == 1 else 1
-            for b in pieces[:before]:
+            for b in pieces:
                 do_out(b, (h - FIRST_OUT) // 2)
             do_scale(h, 0)
             if FIRST_OUT <= h < end:
                 do_turn(h + 1, 0, turn_bank(h + 1, 0))
-            for b in pieces[before:]:
-                do_out(b, (h - FIRST_OUT) // 2)
             if h == end:
                 do_aw(end - 1, 0, 0)
             do_scale(h, 1)
             if h < end:
                 do_turn(h + 1, 1, turn_bank(h + 1, 1))
+            if h == end:
+                do_interleave(0, 1, "scalar")
             do_weigh(h - 2, 1, 0, "scalar")
             if h == end:
                 break
             for k in range(min(1 if h % 2 == 1 else 2, len(halves))):
                 do_cast_half(halves.pop(0))
-            if h >= 4 and early_late and (h % 2 == 0 or not halves):
-                do_weigh(*early_late.pop(0), 1, "scalar")
-            do_diff(h - 2, "vector", 0, OWN_COLS)
+            if h - 2 < DEFER_FROM:
+                do_diff(h - 2, "vector", POOL_COLS, 2 * A)
             if h % 2 == 0 and h >= 4:
                 do_quant_g((h - 4) // 2, 0)
             do_quant_x(h, 0)
@@ -434,43 +454,39 @@ def tile_clipped_policy_head_grad_s13_kernel(
             if h % 2 == 1:
                 do_interleave((h - 3) // 2, 0, "scalar")
             if h == end - 1:
-                do_interleave(0, 1, "scalar")
-                for i in range(2):
-                    do_weigh(2, i, 1, "scalar")
+                do_weigh_late(0, "scalar")
 
         do_aw(end - 1, 1, 1)
-        for i in range(2):
-            do_weigh(3, i, 1, "scalar")
         for c in range(X_PASSES):
             do_quant_x(end, c)
-        do_diff(end - 2, "vector", 0, OWN_COLS)
-        do_quant_g(0, 1)
         do_weigh(end - 2, 0, 0, "vector")
         for f in range(2):
             do_z_half(end, f, 2 + f)
         do_sigmoid_half(end, 0)
         for f in range(2):
             do_residual(end - 1, 0, f)
+        do_quant_g(0, 1)
         do_interleave(last - 1, 0, "scalar")
         do_sigmoid_half(end, 1)
-        do_residual(end - 1, 1, 0)
-        do_interleave(1, 1, "vector")
-        do_residual(end - 1, 1, 1)
-        do_quant_g(1, 1)
-        for g in range(2):
-            for b in (4, 6, 5):
-                do_out(b, g)
+        do_weigh_turn(1, 0, QUARTER)
+        for f in range(2):
+            do_residual(end - 1, 1, f)
+        do_quant_g(1, 1, 0, QUARTER)
         for i in range(2):
             do_residual(end, i, 0)
+        for b in (4, 6, 5):
+            do_out(b, 0)
+        for b in (4, 5):
+            do_out(b, 1)
+        do_diff(6, "vector", POOL_COLS, 2 * A)
         do_quant_g(last - 1, 0)
         do_interleave(last, 0, "scalar", 0, LAST_SPLIT)
         do_interleave(last, 0, "vector", LAST_SPLIT, HALF)
-        for i in range(2):
-            do_weigh(4, i, 1, "vector")
+        do_diff(7, "vector", POOL_COLS, 2 * A)
+        do_diff(2, "vector", POOL_COLS, 2 * A)
         do_quant_g(last, 0)
-        for i in range(2):
-            do_weigh(5, i, 1, "vector")
         do_weigh_late(3, "scalar")
+        do_interleave(3, 1, "scalar", 0, QUARTER)
         for b in range(3):
             do_out(b, last - 1)
         for b in range(4):
@@ -479,36 +495,42 @@ def tile_clipped_policy_head_grad_s13_kernel(
             do_out(b, last)
         for b in range(4):
             do_store(b, "scalar")
-        do_weigh_late(4, "vector", 0, QUARTER)
-        do_interleave(2, 1, "vector", 0, QUARTER)
+        do_weigh_turn(2, 0, QUARTER)
         for i in range(2):
-            do_residual(end, i, 1, 0, QUARTER)
+            do_residual(end, i, 1)
         do_quant_g(2, 1, 0, QUARTER)
-        for g in range(3, GROUPS):
-            do_interleave(g, 1, "vector", 0, QUARTER)
-            if g > 3:
-                do_quant_g(g - 1, 1, 0, QUARTER)
-        do_weigh_late(4, "vector", QUARTER, HALF)
+        do_weigh_turn(4, 0, QUARTER)
+        do_quant_g(3, 1, 0, QUARTER)
+        do_interleave(last, 1, "vector", 0, QUARTER)
+        do_quant_g(4, 1, 0, QUARTER)
+        do_diff(3, "vector", POOL_COLS, 2 * A)
         do_quant_g(last, 1, 0, QUARTER)
-        for g in (2, 3):
+        do_diff_rest(2)
+        do_weigh_turn(1, QUARTER, HALF)
+        for g in (5, 3):
             do_interleave(g, 1, "scalar", QUARTER, HALF)
-        for i in range(2):
-            do_residual(end, i, 1, QUARTER, HALF)
-        for g in (4, 5):
-            do_interleave(g, 1, "vector", QUARTER, HALF)
-            do_quant_g(g - 2, 1, QUARTER, HALF)
-        for g in (4, 5):
+        do_diff_rest(4)
+        do_quant_g(1, 1, QUARTER, HALF)
+        do_weigh_turn(2, QUARTER, HALF)
+        do_quant_g(last, 1, QUARTER, HALF)
+        do_weigh_turn(4, QUARTER, HALF)
+        for g in (2, 3, 4):
             do_quant_g(g, 1, QUARTER, HALF)
+        do_out(7, 0)
         for g in (2, 3):
             for b in (4, 5):
                 do_out(b, g)
-            do_out(7, g - 2)
+        for b in (8, 9):
+            do_out(b, 0)
         for b in (4, 5):
             for g in (4, 5):
                 do_out(b, g)
         do_store(4, "scalar")
         do_store(5, "scalar")
-        for b in range(6, len(PIECES)):
-            for g in range(2 if b < 8 else 0, GROUPS):
+        for g in (1, 5):
+            for b in range(6, len(PIECES)):
                 do_out(b, g)
-            do_store(b, "vector" if b % 2 == 0 else "scalar")
+        for b in range(6, len(PIECES)):
+            for g in (2, 3, 4):
+                do_out(b, g)
+            do_store(b, "scalar" if b % 2 == 0 else "vector")

@@ -49,8 +49,9 @@ PIECES = (
     (HALF + QUARTER, QUARTER, (0, 1, 2, 3), 2), (HALF + QUARTER, QUARTER, (4, 5), 3),
     (HALF + QUARTER, QUARTER, (6,), 4), (HALF + QUARTER, QUARTER, (7,), 5),
 )
-LAST_SPLIT = 96
+LAST_SPLIT = 160
 HEAD_CASTS = 5
+EXTRA_STEP = 6
 
 
 def tile_clipped_policy_head_grad_s13_kernel(
@@ -281,12 +282,12 @@ def tile_clipped_policy_head_grad_s13_kernel(
                 gi[g, f] = one.tile([P, HALF, 4], BF16, align_bytes=64, name="gi", bufs=GI_BUFS)
             interleave(engine, gi[g, f][:, lo:hi, :], planes[g, f][:, :, lo:hi].rearrange("p t a -> p a t"))
 
-        def do_weigh_turn(g, lo, hi):
-            if (g, 1) not in gi:
-                gi[g, 1] = one.tile([P, HALF, 4], BF16, align_bytes=64, name="gi", bufs=GI_BUFS)
+        def do_weigh_turn(g, f, lo=0, hi=HALF):
+            if (g, f) not in gi:
+                gi[g, f] = one.tile([P, HALF, 4], BF16, align_bytes=64, name="gi", bufs=GI_BUFS)
             nc.vector.tensor_tensor(
-                out=gi[g, 1][:, lo:hi, :],
-                in0=diff_g[g][:].rearrange("p (t a) -> p a t", t=4)[:, HALF + lo : HALF + hi, :],
+                out=gi[g, f][:, lo:hi, :],
+                in0=diff_g[g][:].rearrange("p (t a) -> p a t", t=4)[:, f * HALF + lo : f * HALF + hi, :],
                 in1=wt[:, g, :].unsqueeze(1).to_broadcast([P, hi - lo, 4]),
                 op=MULT,
             )
@@ -402,12 +403,12 @@ def tile_clipped_policy_head_grad_s13_kernel(
             do_turn(2, c, turn_bank(2, c))
         do_cast(3)
         for i in range(2):
-            do_diag(STEPS - 2, i)
-        for i in range(2):
             do_sigmoid(0, i)
         for c in range(X_PASSES):
             do_scale(1, c)
         do_cast(4)
+        for i in range(2):
+            do_diag(STEPS - 2, i)
         do_quant_x(1, 0)
         do_quant_x(1, 1)
 
@@ -416,7 +417,7 @@ def tile_clipped_policy_head_grad_s13_kernel(
             do_diff(h - 2, "gpsimd", 0, POOL_COLS)
             do_z(h - 1, 0, 2)
             do_sigmoid(h - 1, 0)
-            if h < STEADY + 2:
+            if h == STEADY:
                 do_cast_half(halves.pop(0))
             if h < FIRST_OUT:
                 do_turn(h + 1, 0, turn_bank(h + 1, 0))
@@ -439,17 +440,18 @@ def tile_clipped_policy_head_grad_s13_kernel(
                 do_turn(h + 1, 1, turn_bank(h + 1, 1))
             if h == end:
                 do_interleave(0, 1, "scalar")
-            do_weigh(h - 2, 1, 0, "scalar")
-            if h == end:
                 break
-            for k in range(min(1 if h % 2 == 1 else 2, len(halves))):
+            if h < end - 1:
+                do_weigh(h - 2, 1, 0, "scalar")
+            for k in range(min(1 if h % 2 == 1 else 3 if h == EXTRA_STEP else 2, len(halves))):
                 do_cast_half(halves.pop(0))
             if h - 2 < DEFER_FROM:
                 do_diff(h - 2, "vector", POOL_COLS, 2 * A)
             if h % 2 == 0 and h >= 4:
                 do_quant_g((h - 4) // 2, 0)
             do_quant_x(h, 0)
-            do_weigh(h - 2, 0, 0, "vector")
+            if h < end - 1:
+                do_weigh(h - 2, 0, 0, "vector")
             do_quant_x(h, 1)
             if h % 2 == 1:
                 do_interleave((h - 3) // 2, 0, "scalar")
@@ -459,78 +461,88 @@ def tile_clipped_policy_head_grad_s13_kernel(
         do_aw(end - 1, 1, 1)
         for c in range(X_PASSES):
             do_quant_x(end, c)
-        do_weigh(end - 2, 0, 0, "vector")
+        for i in range(2):
+            do_weigh_pair(1, i, "scalar", 0, QUARTER)
         for f in range(2):
             do_z_half(end, f, 2 + f)
-        do_sigmoid_half(end, 0)
-        for f in range(2):
-            do_residual(end - 1, 0, f)
+            do_sigmoid_half(end, f)
+        do_weigh_turn(last - 1, 0)
         do_quant_g(0, 1)
-        do_interleave(last - 1, 0, "scalar")
-        do_sigmoid_half(end, 1)
-        do_weigh_turn(1, 0, QUARTER)
-        for f in range(2):
-            do_residual(end - 1, 1, f)
-        do_quant_g(1, 1, 0, QUARTER)
+        do_quant_g(last - 1, 0)
+        for h in (end - 1, end):
+            for i in range(2):
+                do_residual(h, i, 0)
+        do_interleave(1, 1, "scalar", 0, QUARTER)
         for i in range(2):
-            do_residual(end, i, 0)
-        for b in (4, 6, 5):
+            do_residual(end - 1, i, 1)
+        do_interleave(last, 0, "scalar", 0, LAST_SPLIT)
+        do_interleave(last, 0, "vector", LAST_SPLIT, HALF)
+        do_quant_g(1, 1, 0, QUARTER)
+        do_diff_rest(3)
+        do_quant_g(last, 0)
+        do_out(6, 0)
+        for b in range(4):
+            do_out(b, last - 1)
+        for b in (7, 4, 5):
             do_out(b, 0)
         for b in (4, 5):
             do_out(b, 1)
-        do_diff(6, "vector", POOL_COLS, 2 * A)
-        do_quant_g(last - 1, 0)
-        do_interleave(last, 0, "scalar", 0, LAST_SPLIT)
-        do_interleave(last, 0, "vector", LAST_SPLIT, HALF)
-        do_diff(7, "vector", POOL_COLS, 2 * A)
-        do_diff(2, "vector", POOL_COLS, 2 * A)
-        do_quant_g(last, 0)
-        do_weigh_late(3, "scalar")
-        do_interleave(3, 1, "scalar", 0, QUARTER)
-        for b in range(3):
-            do_out(b, last - 1)
         for b in range(4):
-            if b >= 3:
-                do_out(b, last - 1)
             do_out(b, last)
-        for b in range(4):
-            do_store(b, "scalar")
-        do_weigh_turn(2, 0, QUARTER)
         for i in range(2):
-            do_residual(end, i, 1)
+            do_weigh_pair(3, i, "scalar")
+        do_store(0, "scalar")
+        do_interleave(3, 1, "scalar", 0, QUARTER)
+        for b in range(1, 4):
+            do_store(b, "scalar")
+        do_weigh_turn(2, 1, 0, QUARTER)
+        do_weigh_turn(4, 1, 0, QUARTER)
         do_quant_g(2, 1, 0, QUARTER)
-        do_weigh_turn(4, 0, QUARTER)
-        do_quant_g(3, 1, 0, QUARTER)
-        do_interleave(last, 1, "vector", 0, QUARTER)
+        do_residual(end, 0, 1)
         do_quant_g(4, 1, 0, QUARTER)
-        do_diff(3, "vector", POOL_COLS, 2 * A)
+        do_residual(end, 1, 1)
+        do_diff_rest(1)
+        do_interleave(last, 1, "vector", 0, QUARTER)
+        do_quant_g(3, 1, 0, QUARTER)
+        do_diff(4, "vector", POOL_COLS, 2 * A)
         do_quant_g(last, 1, 0, QUARTER)
-        do_diff_rest(2)
-        do_weigh_turn(1, QUARTER, HALF)
-        for g in (5, 3):
-            do_interleave(g, 1, "scalar", QUARTER, HALF)
-        do_diff_rest(4)
+        do_weigh_turn(1, 1, QUARTER, HALF)
+        for h in (5, 8):
+            do_diff(h, "vector", POOL_COLS, 2 * A)
         do_quant_g(1, 1, QUARTER, HALF)
-        do_weigh_turn(2, QUARTER, HALF)
-        do_quant_g(last, 1, QUARTER, HALF)
-        do_weigh_turn(4, QUARTER, HALF)
-        for g in (2, 3, 4):
+        do_weigh_turn(2, 1, QUARTER, HALF)
+        do_diff(9, "vector", POOL_COLS, 2 * A)
+        for g in (last, 3):
+            do_interleave(g, 1, "scalar", QUARTER, HALF)
+        for g in (last, 2):
             do_quant_g(g, 1, QUARTER, HALF)
-        do_out(7, 0)
-        for g in (2, 3):
+        do_weigh_turn(4, 1, QUARTER, HALF)
+        for g in (3, 4):
+            do_quant_g(g, 1, QUARTER, HALF)
+        for g in (2, 4):
             for b in (4, 5):
                 do_out(b, g)
-        for b in (8, 9):
-            do_out(b, 0)
-        for b in (4, 5):
-            for g in (4, 5):
+        do_out(8, 0)
+        for g in (3, last):
+            for b in (4, 5):
                 do_out(b, g)
         do_store(4, "scalar")
         do_store(5, "scalar")
-        for g in (1, 5):
-            for b in range(6, len(PIECES)):
-                do_out(b, g)
+        do_out(9, 0)
         for b in range(6, len(PIECES)):
-            for g in (2, 3, 4):
+            do_out(b, 1)
+        for g in (5, 2):
+            for b in (6, 9):
                 do_out(b, g)
-            do_store(b, "scalar" if b % 2 == 0 else "vector")
+        do_out(7, 5)
+        for b in (6, 9):
+            for g in (3, 4):
+                do_out(b, g)
+        for g in (2, 3, 4):
+            do_out(7, g)
+        for g in (5, 2, 3, 4):
+            do_out(8, g)
+        do_store(9, "vector")
+        do_store(6, "scalar")
+        do_store(7, "vector")
+        do_store(8, "scalar")

@@ -88,18 +88,9 @@ def tile_clipped_policy_head_grad_s13_kernel(
             src = x_bytes[g * K_PASS : (g + 1) * K_PASS, :].rearrange("(p t) k -> p (t k)", t=4)
             nc.sync.dma_start(out=x_raw[h][:], in_=src[:, lo * D : (lo + 2) * D])
 
-        def load_x_pass(h, c):
-            g, lo = h // 2, 2 * (h % 2)
-            cols = slice(c * K_PASS, (c + 1) * K_PASS)
-            src = x_bytes[g * K_PASS : (g + 1) * K_PASS, :].rearrange("(p t) k -> p t k", t=4)
-            nc.sync.dma_start(
-                out=x_raw[h][:].rearrange("p (i k) -> p i k", i=2)[:, :, cols], in_=src[:, lo : lo + 2, cols]
-            )
-
         def load_w(c):
-            nc.sync.dma_start(
-                out=w_raw[c][:], in_=w[c * K_PASS : (c + 1) * K_PASS, :].rearrange("(p j) n -> p j n", j=4)
-            )
+            rows = w[c * K_PASS : (c + 1) * K_PASS, :].rearrange("(p j) n -> p j n", j=4)
+            nc.sync.dma_start(out=w_raw[c][:], in_=rows)
 
         def load_act(g, lo=0, hi=4):
             rows = action[g * K_PASS : (g + 1) * K_PASS, :].rearrange("(p t) a -> p t a", t=4)
@@ -139,9 +130,10 @@ def tile_clipped_policy_head_grad_s13_kernel(
             else:
                 nc.scalar.copy(out=cast[h][:, lo:hi], in_=x_raw[h][:, lo:hi].bitcast(FP8))
 
-        def do_cast_half(k):
-            if k < 2 * STEPS:
-                do_cast(k // 2, "scalar", (k % 2) * D, (k % 2 + 1) * D)
+        def do_cast_halves(ks):
+            for h in sorted({k // 2 for k in ks}):
+                own = [k % 2 for k in ks if k // 2 == h]
+                do_cast(h, "scalar", own[0] * D, (own[-1] + 1) * D)
 
         def do_turn(h, c, bank):
             turned[h, c] = psum.tile([P, 2, 2 * P], F32, name="turned", tag=f"bank{bank}")
@@ -407,8 +399,6 @@ def tile_clipped_policy_head_grad_s13_kernel(
         for c in range(X_PASSES):
             do_scale(1, c)
         do_cast(4)
-        for i in range(2):
-            do_diag(STEPS - 2, i)
         do_quant_x(1, 0)
         do_quant_x(1, 1)
 
@@ -418,7 +408,10 @@ def tile_clipped_policy_head_grad_s13_kernel(
             do_z(h - 1, 0, 2)
             do_sigmoid(h - 1, 0)
             if h == STEADY:
-                do_cast_half(halves.pop(0))
+                do_cast_halves([halves.pop(0)])
+            if h == STEADY + 1:
+                for i in range(2):
+                    do_diag(STEPS - 2, i)
             if h < FIRST_OUT:
                 do_turn(h + 1, 0, turn_bank(h + 1, 0))
             do_z(h - 1, 1, 3)
@@ -427,7 +420,7 @@ def tile_clipped_policy_head_grad_s13_kernel(
             if h >= FIRST_OUT:
                 pieces = [0, 1] if h % 2 == 1 else [2, 3]
             if h == end:
-                pieces = [0, 1, 2, 3]
+                pieces = [0, 1]
             for b in pieces:
                 do_out(b, (h - FIRST_OUT) // 2)
             do_scale(h, 0)
@@ -441,17 +434,20 @@ def tile_clipped_policy_head_grad_s13_kernel(
             if h == end:
                 do_interleave(0, 1, "scalar")
                 break
-            if h < end - 1:
+            both = h == EXTRA_STEP
+            if h < end - 1 and not both:
                 do_weigh(h - 2, 1, 0, "scalar")
-            for k in range(min(1 if h % 2 == 1 else 3 if h == EXTRA_STEP else 2, len(halves))):
-                do_cast_half(halves.pop(0))
+            count = 1 if h % 2 == 1 else 3 if h == EXTRA_STEP else 2
+            do_cast_halves(halves[:count])
+            halves = halves[count:]
             if h - 2 < DEFER_FROM:
                 do_diff(h - 2, "vector", POOL_COLS, 2 * A)
             if h % 2 == 0 and h >= 4:
                 do_quant_g((h - 4) // 2, 0)
             do_quant_x(h, 0)
             if h < end - 1:
-                do_weigh(h - 2, 0, 0, "vector")
+                for i in range(2 if both else 1):
+                    do_weigh(h - 2, i, 0, "vector")
             do_quant_x(h, 1)
             if h % 2 == 1:
                 do_interleave((h - 3) // 2, 0, "scalar")
@@ -480,6 +476,8 @@ def tile_clipped_policy_head_grad_s13_kernel(
         do_quant_g(1, 1, 0, QUARTER)
         do_diff_rest(3)
         do_quant_g(last, 0)
+        for b in (2, 3):
+            do_out(b, last - 2)
         do_out(6, 0)
         for b in range(4):
             do_out(b, last - 1)

@@ -46,12 +46,11 @@ QUARTER = A // 4
 PIECES = (
     (0, HALF, (0, 1), 4), (0, HALF, (2, 3), 5), (0, HALF, (4, 5), 6), (0, HALF, (6, 7), 7),
     (HALF, QUARTER, (0, 1, 2, 3), 0), (HALF, QUARTER, (4, 5, 6, 7), 1),
-    (HALF + QUARTER, QUARTER, (0, 1, 2, 3), 2), (HALF + QUARTER, QUARTER, (4, 5), 3),
-    (HALF + QUARTER, QUARTER, (6,), 4), (HALF + QUARTER, QUARTER, (7,), 5),
+    (HALF + QUARTER, QUARTER, (0, 1), 2), (HALF + QUARTER, QUARTER, (2, 3), 3),
+    (HALF + QUARTER, QUARTER, (4, 5), 4), (HALF + QUARTER, QUARTER, (6, 7), 5),
 )
 LAST_SPLIT = 160
 HEAD_CASTS = 5
-EXTRA_STEP = 6
 
 
 def tile_clipped_policy_head_grad_s13_kernel(
@@ -399,10 +398,11 @@ def tile_clipped_policy_head_grad_s13_kernel(
         for c in range(X_PASSES):
             do_scale(1, c)
         do_cast(4)
+        do_cast_halves([2 * HEAD_CASTS])
         do_quant_x(1, 0)
         do_quant_x(1, 1)
 
-        halves = list(range(2 * HEAD_CASTS, 2 * STEPS))
+        halves = list(range(2 * HEAD_CASTS + 1, 2 * STEPS))
         for h in range(STEADY, STEPS):
             do_diff(h - 2, "gpsimd", 0, POOL_COLS)
             do_z(h - 1, 0, 2)
@@ -434,10 +434,11 @@ def tile_clipped_policy_head_grad_s13_kernel(
             if h == end:
                 do_interleave(0, 1, "scalar")
                 break
-            both = h == EXTRA_STEP
-            if h < end - 1 and not both:
-                do_weigh(h - 2, 1, 0, "scalar")
-            count = 1 if h % 2 == 1 else 3 if h == EXTRA_STEP else 2
+            both = h % 2 == 0
+            if h < end - 1:
+                for i in (1, 0) if both else (1,):
+                    do_weigh(h - 2, i, 0, "scalar")
+            count = 1 if h % 2 == 1 else 2
             do_cast_halves(halves[:count])
             halves = halves[count:]
             if h - 2 < DEFER_FROM:
@@ -445,9 +446,8 @@ def tile_clipped_policy_head_grad_s13_kernel(
             if h % 2 == 0 and h >= 4:
                 do_quant_g((h - 4) // 2, 0)
             do_quant_x(h, 0)
-            if h < end - 1:
-                for i in range(2 if both else 1):
-                    do_weigh(h - 2, i, 0, "vector")
+            if h < end - 1 and not both:
+                do_weigh(h - 2, 0, 0, "vector")
             do_quant_x(h, 1)
             if h % 2 == 1:
                 do_interleave((h - 3) // 2, 0, "scalar")
@@ -489,9 +489,8 @@ def tile_clipped_policy_head_grad_s13_kernel(
             do_out(b, last)
         for i in range(2):
             do_weigh_pair(3, i, "scalar")
-        do_store(0, "scalar")
         do_interleave(3, 1, "scalar", 0, QUARTER)
-        for b in range(1, 4):
+        for b in range(4):
             do_store(b, "scalar")
         do_weigh_turn(2, 1, 0, QUARTER)
         do_weigh_turn(4, 1, 0, QUARTER)
@@ -499,9 +498,10 @@ def tile_clipped_policy_head_grad_s13_kernel(
         do_residual(end, 0, 1)
         do_quant_g(4, 1, 0, QUARTER)
         do_residual(end, 1, 1)
-        do_diff_rest(1)
-        do_interleave(last, 1, "vector", 0, QUARTER)
         do_quant_g(3, 1, 0, QUARTER)
+        do_diff(2, "vector", POOL_COLS, 2 * A)
+        do_interleave(last, 1, "vector", 0, QUARTER)
+        do_diff(3, "vector", POOL_COLS, 2 * A)
         do_diff(4, "vector", POOL_COLS, 2 * A)
         do_quant_g(last, 1, 0, QUARTER)
         do_weigh_turn(1, 1, QUARTER, HALF)
@@ -509,11 +509,11 @@ def tile_clipped_policy_head_grad_s13_kernel(
             do_diff(h, "vector", POOL_COLS, 2 * A)
         do_quant_g(1, 1, QUARTER, HALF)
         do_weigh_turn(2, 1, QUARTER, HALF)
-        do_diff(9, "vector", POOL_COLS, 2 * A)
         for g in (last, 3):
             do_interleave(g, 1, "scalar", QUARTER, HALF)
-        for g in (last, 2):
-            do_quant_g(g, 1, QUARTER, HALF)
+        do_quant_g(last, 1, QUARTER, HALF)
+        do_diff(9, "vector", POOL_COLS, 2 * A)
+        do_quant_g(2, 1, QUARTER, HALF)
         do_weigh_turn(4, 1, QUARTER, HALF)
         for g in (3, 4):
             do_quant_g(g, 1, QUARTER, HALF)
@@ -527,20 +527,10 @@ def tile_clipped_policy_head_grad_s13_kernel(
         do_store(4, "scalar")
         do_store(5, "scalar")
         do_out(9, 0)
-        for b in range(6, len(PIECES)):
-            do_out(b, 1)
-        for g in (5, 2):
-            for b in (6, 9):
+        for g in (1, 5, 2):
+            for b in range(6, len(PIECES)):
                 do_out(b, g)
-        do_out(7, 5)
-        for b in (6, 9):
+        for b in range(6, len(PIECES)):
             for g in (3, 4):
                 do_out(b, g)
-        for g in (2, 3, 4):
-            do_out(7, g)
-        for g in (5, 2, 3, 4):
-            do_out(8, g)
-        do_store(9, "vector")
-        do_store(6, "scalar")
-        do_store(7, "vector")
-        do_store(8, "scalar")
+            do_store(b, "vector" if b % 2 == 0 else "scalar")

@@ -260,18 +260,19 @@ def tile_clipped_policy_head_grad_s13_kernel(
             for h in (2 * g, 2 * g + 1):
                 do_diff(h, "vector", POOL_COLS, 2 * A)
 
-        def interleave(engine, dst, src):
-            if engine == "vector":
-                nc.vector.tensor_copy(out=dst, in_=src)
-            elif engine == "scalar":
-                nc.scalar.copy(out=dst, in_=src)
-            else:
-                nc.gpsimd.tensor_scalar(out=dst, in0=src, scalar1=1.0, scalar2=0.0, op0=MULT, op1=ADD)
+        def interleave(engine, dst, rows):
+            if engine == "gpsimd":
+                nc.gpsimd.tensor_scalar(
+                    out=dst, in0=rows.rearrange("p t a -> p a t"), scalar1=1.0, scalar2=0.0, op0=MULT, op1=ADD
+                )
+                return
+            copy = nc.vector.tensor_copy if engine == "vector" else nc.scalar.copy
+            copy(out=dst.rearrange("p (c i) t -> p c t i", i=4), in_=rows.rearrange("p t (c i) -> p c t i", i=4))
 
         def do_interleave(g, f, engine, lo=0, hi=HALF):
             if (g, f) not in gi:
                 gi[g, f] = one.tile([P, HALF, 4], BF16, align_bytes=64, name="gi", bufs=GI_BUFS)
-            interleave(engine, gi[g, f][:, lo:hi, :], planes[g, f][:, :, lo:hi].rearrange("p t a -> p a t"))
+            interleave(engine, gi[g, f][:, lo:hi, :], planes[g, f][:, :, lo:hi])
 
         def do_weigh_turn(g, f, lo=0, hi=HALF):
             if (g, f) not in gi:
@@ -321,7 +322,7 @@ def tile_clipped_policy_head_grad_s13_kernel(
             nc.sync.dma_start(out=rows.rearrange("(s p) n -> p s n", p=P), in_=res)
 
         def do_w_interleave(c, engine, lo, hi):
-            interleave(engine, w_int[c][:, lo:hi, :], w_raw[c][:, :, lo:hi].rearrange("p j n -> p n j"))
+            interleave(engine, w_int[c][:, lo:hi, :], w_raw[c][:, :, lo:hi])
 
         def do_quant_w(c):
             nc.vector.quantize_mx(

@@ -36,8 +36,8 @@ SIG_BUFS = 10
 GI_BUFS = 5
 PLANE_BUFS = 4
 WARM = 4
-W_POOL = 192
-W_OWN = 256
+W_POOL = 176
+W_OWN = 224
 STEADY = 2
 EARLY_BANKS = (0, 4, 6)
 EARLY_STEPS = 6
@@ -277,10 +277,11 @@ def tile_clipped_policy_head_grad_s13_kernel(
         def do_weigh_turn(g, f, lo=0, hi=HALF):
             if (g, f) not in gi:
                 gi[g, f] = one.tile([P, HALF, 4], BF16, align_bytes=64, name="gi", bufs=GI_BUFS)
+            rows = diff_g[g][:].rearrange("p (t a) -> p t a", t=4)
             nc.vector.tensor_tensor(
-                out=gi[g, f][:, lo:hi, :],
-                in0=diff_g[g][:].rearrange("p (t a) -> p a t", t=4)[:, f * HALF + lo : f * HALF + hi, :],
-                in1=wt[:, g, :].unsqueeze(1).to_broadcast([P, hi - lo, 4]),
+                out=gi[g, f][:, lo:hi, :].rearrange("p (c i) t -> p c t i", i=4),
+                in0=rows[:, :, f * HALF + lo : f * HALF + hi].rearrange("p t (c i) -> p c t i", i=4),
+                in1=wt[:, g, :].unsqueeze(1).unsqueeze(3).to_broadcast([P, (hi - lo) // 4, 4, 4]),
                 op=MULT,
             )
 
@@ -435,7 +436,7 @@ def tile_clipped_policy_head_grad_s13_kernel(
             if h == end:
                 do_interleave(0, 1, "scalar")
                 break
-            both = h % 2 == 0
+            both = h % 2 == 0 and h > STEADY
             if h < end - 1:
                 for i in (1, 0) if both else (1,):
                     do_weigh(h - 2, i, 0, "scalar")

from contextlib import ExitStack

import concourse.mybir as mybir
from concourse.masks import make_identity

T, D, A = 3072, 1024, 512
FLOPS = 2 * T * D * A * 2

F32 = mybir.dt.float32
BF16 = mybir.dt.bfloat16
I32 = mybir.dt.int32
U32 = mybir.dt.uint32
U8 = mybir.dt.uint8
FP8 = mybir.dt.float8_e4m3fn
FP8X4 = mybir.dt.float8_e4m3fn_x4
FP4X4 = mybir.dt.float4_e2m1fn_x4
MULT = mybir.AluOpType.mult
ADD = mybir.AluOpType.add
SUB = mybir.AluOpType.subtract
SIGMOID = mybir.ActivationFunctionType.Sigmoid
COPY = mybir.ActivationFunctionType.Copy

P = 128
K_PASS = 512
GROUPS = T // K_PASS
STEPS = 2 * GROUPS
X_PASSES = D // K_PASS
HALF = A // 2
POOL_COLS = 896
DEFER_FROM = 2
FIRST_POOL = 0
CAST_BUFS = 5
XG_BUFS = 3
CODE_BUFS = 6
SIG_BUFS = 10
GI_BUFS = 5
PLANE_BUFS = 4
WARM = 4
W_POOL = 176
W_OWN = 224
STEADY = 2
EARLY_BANKS = (0, 4, 6)
EARLY_STEPS = 6
FIRST_OUT = 5
QUARTER = A // 4
PIECES = (
    (0, HALF, (0, 1), 4), (0, HALF, (2, 3), 5), (0, HALF, (4, 5), 6), (0, HALF, (6, 7), 7),
    (HALF, QUARTER, (0, 1, 2, 3), 0), (HALF, QUARTER, (4, 5, 6, 7), 1),
    (HALF + QUARTER, QUARTER, (0, 1), 2), (HALF + QUARTER, QUARTER, (2, 3), 3),
    (HALF + QUARTER, QUARTER, (4, 5), 4), (HALF + QUARTER, QUARTER, (6, 7), 5),
)
LAST_SPLIT = 160
HEAD_CASTS = 5


def tile_clipped_policy_head_grad_s13_kernel(
    tc, x_bytes, x_scale, w, action, weight, h_words, h_scales, out
):
    nc = tc.nc
    with ExitStack() as ctx:
        keep = ctx.enter_context(tc.tile_pool(name="keep", bufs=1))
        one = ctx.enter_context(tc.tile_pool(name="one", bufs=1))
        psum = ctx.enter_context(tc.psum_pool(name="psum", bufs=1))
        ctx.enter_context(tc.manual_schedule())

        x_raw = [keep.tile([P, 2 * D], U8, align_bytes=64, name=f"x_raw{h}") for h in range(STEPS)]
        act = [keep.tile([P, 4, A], BF16, align_bytes=64, name=f"act{g}") for g in range(GROUPS)]
        hw = [keep.tile([P, 2 * D], U8, align_bytes=64, name=f"hw{g}") for g in range(GROUPS)]
        w_raw = [keep.tile([P, 4, A], BF16, align_bytes=64, name=f"w_raw{c}") for c in range(X_PASSES)]
        w_int = [one.tile([P, A, 4], BF16, align_bytes=64, name=f"w_int{c}") for c in range(X_PASSES)]
        w_codes = [keep.tile([P, A], U32, align_bytes=64, name=f"w_codes{c}") for c in range(X_PASSES)]
        w_scales = [keep.tile([P, A], U8, align_bytes=64, name=f"w_scales{c}") for c in range(X_PASSES)]
        g_codes = [keep.tile([P, A], U32, align_bytes=64, name=f"g_codes{g}") for g in range(GROUPS)]
        g_scales = [keep.tile([P, A], U8, align_bytes=64, name=f"g_scales{g}") for g in range(GROUPS)]
        diff_g = [keep.tile([P, 4 * A], F32, align_bytes=64, name=f"diff{g}") for g in range(GROUPS - 1)]
        diff = [diff_g[h // 2][:, (h % 2) * 2 * A : (h % 2 + 1) * 2 * A] for h in range(STEPS - 2)]
        hs = keep.tile([P, GROUPS, D // 4], I32, align_bytes=64, name="hs")
        xs = keep.tile([P, X_PASSES, 2, 2], F32, align_bytes=64, name="xs")
        wt_raw = keep.tile([P, GROUPS, 4], BF16, align_bytes=64, name="wt_raw")
        wt = keep.tile([P, GROUPS, 4], F32, align_bytes=64, name="wt")
        ident = keep.tile([P, P], F32, align_bytes=64, name="ident")
        zeros = keep.tile([P, A], BF16, align_bytes=64, name="zeros")
        warm = keep.tile([P, 1], F32, align_bytes=64, name="warm")

        def load_x(h):
            g, lo = h // 2, 2 * (h % 2)
            src = x_bytes[g * K_PASS : (g + 1) * K_PASS, :].rearrange("(p t) k -> p (t k)", t=4)
            nc.sync.dma_start(out=x_raw[h][:], in_=src[:, lo * D : (lo + 2) * D])

        def load_w(c):
            rows = w[c * K_PASS : (c + 1) * K_PASS, :].rearrange("(p j) n -> p j n", j=4)
            nc.sync.dma_start(out=w_raw[c][:], in_=rows)

        def load_act(g, lo=0, hi=4):
            rows = action[g * K_PASS : (g + 1) * K_PASS, :].rearrange("(p t) a -> p t a", t=4)
            nc.sync.dma_start(out=act[g][:, lo:hi, :], in_=rows[:, lo:hi, :])

        def load_h(g):
            nc.sync.dma_start(out=hw[g][:], in_=h_words[g])

        def load_x_scale():
            nc.sync.dma_start(
                out=xs[:].rearrange("p c u e -> p c (u e)"),
                in_=x_scale.rearrange("o (c p t) -> p (o c) t", p=P, t=4),
            )

        def load_weight():
            nc.sync.dma_start(out=wt_raw[:], in_=weight.rearrange("(g p t) -> p g t", p=P, t=4))

        def load_h_scales():
            scales_src = h_scales.bitcast(I32).rearrange("g (q r) n -> r q g n", r=4)
            for r in range(4):
                nc.sync.dma_start(out=hs[r:P:32, :, :], in_=scales_src[r])

        cast, turned, xg, x_codes, x_scales = {}, {}, {}, {}, {}
        z, sig, planes, gi, accs, diag, aw, pairs = {}, {}, {}, {}, {}, {}, {}, {}

        def token_slot(h, i):
            return h // 2, 2 * (h % 2) + i

        def half_cols(f):
            return slice(f * HALF, (f + 1) * HALF)

        def do_cast(h, engine="scalar", lo=0, hi=2 * D):
            if h not in cast:
                cast[h] = one.tile([P, 2 * D], BF16, align_bytes=64, name="cast", bufs=CAST_BUFS)
            if engine == "vector":
                nc.vector.tensor_copy(out=cast[h][:, lo:hi], in_=x_raw[h][:, lo:hi].bitcast(FP8))
            else:
                nc.scalar.copy(out=cast[h][:, lo:hi], in_=x_raw[h][:, lo:hi].bitcast(FP8))

        def do_cast_halves(ks):
            for h in sorted({k // 2 for k in ks}):
                own = [k % 2 for k in ks if k // 2 == h]
                do_cast(h, "scalar", own[0] * D, (own[-1] + 1) * D)

        def do_turn(h, c, bank):
            turned[h, c] = psum.tile([P, 2, 2 * P], F32, name="turned", tag=f"bank{bank}")
            for i in range(2):
                words = cast[h][:, i * D : (i + 1) * D].bitcast(F32)
                for u in range(2):
                    nc.tensor.transpose(
                        turned[h, c][:, u, i * P : (i + 1) * P], words[:, 256 * c + u : 256 * (c + 1) : 2], ident[:]
                    )

        def do_scale(h, c):
            if c == 0 and FIRST_POOL <= h - 1 < STEPS - 2:
                xg[h, c] = diff[h - 1][:, :A].bitcast(BF16).rearrange("p (r u e) -> p r u e", u=2, e=2)
            else:
                tile = one.tile([P, 2 * P, 2, 2], BF16, align_bytes=64, name="xg", bufs=XG_BUFS)
                xg[h, c] = tile[:]
            nc.vector.tensor_tensor(
                out=xg[h, c],
                in0=turned[h, c][:].bitcast(BF16).rearrange("p u (r e) -> p r u e", e=2),
                in1=xs[:, c].unsqueeze(1).to_broadcast([P, 2 * P, 2, 2]),
                op=MULT,
            )

        def do_quant_x(h, c):
            x_codes[h, c] = one.tile([P, 2 * P], U32, align_bytes=64, name="x_codes", bufs=CODE_BUFS)
            x_scales[h, c] = one.tile([P, 2 * P], U8, align_bytes=64, name="x_scales", bufs=CODE_BUFS)
            nc.vector.quantize_mx(
                out=x_codes[h, c][:].bitcast(FP8X4),
                scales=x_scales[h, c][:],
                in_=xg[h, c].rearrange("p r u e -> p (r u e)"),
            )

        def logits_pass(dst, h, i, c, cols):
            nc.tensor.matmul_mx(
                out=dst,
                lhsT=x_codes[h, c][:, i * P : (i + 1) * P].bitcast(FP8X4),
                lhsT_scale=x_scales[h, c][:, i * P : (i + 1) * P],
                rhs=w_codes[c][:, cols].bitcast(FP8X4),
                rhs_scale=w_scales[c][:, cols],
                start=(c == 0),
                stop=(c == X_PASSES - 1),
            )

        def do_z(h, i, bank, passes=range(X_PASSES)):
            if (h, i) not in z:
                z[h, i] = psum.tile([P, A], F32, name="zt", tag=f"bank{bank}")
            for c in passes:
                logits_pass(z[h, i][:], h, i, c, slice(0, A))

        def sig_tile(h):
            if h not in sig:
                sig[h] = one.tile([P, 2 * A], F32, align_bytes=64, name="sig", bufs=SIG_BUFS)
            return sig[h]

        def do_sigmoid(h, i):
            nc.scalar.activation(out=sig_tile(h)[:, i * A : (i + 1) * A], in_=z[h, i][:], func=SIGMOID)

        def do_z_half(h, f, bank):
            z[h, "half", f] = psum.tile([P, 2, HALF], F32, name="zh", tag=f"bank{bank}")
            for i in range(2):
                for c in range(X_PASSES):
                    logits_pass(z[h, "half", f][:, i, :], h, i, c, half_cols(f))

        def do_sigmoid_half(h, f):
            both = sig_tile(h)[:].rearrange("p (i a) -> p i a", i=2)
            nc.scalar.activation(out=both[:, :, half_cols(f)], in_=z[h, "half", f][:], func=SIGMOID)

        def do_diff(h, engine, lo, hi):
            g, t = token_slot(h, 0)
            taken = act[g][:, t : t + 2, :].rearrange("p i a -> p (i a)")
            op = nc.gpsimd.tensor_tensor if engine == "gpsimd" else nc.vector.tensor_tensor
            op(out=diff[h][:, lo:hi], in0=sig[h][:, lo:hi], in1=taken[:, lo:hi], op=SUB)

        def plane_tile(g, f):
            if (g, f) not in planes:
                planes[g, f] = one.tile([P, 4, HALF], BF16, align_bytes=64, name="planes", bufs=PLANE_BUFS)
            return planes[g, f]

        def do_weigh(h, i, f, engine, lo=0, hi=HALF):
            g, t = token_slot(h, i)
            src = diff[h][:, i * A + f * HALF + lo : i * A + f * HALF + hi]
            dst = plane_tile(g, f)[:, t, lo:hi]
            if engine == "scalar":
                nc.scalar.activation(out=dst, in_=src, func=COPY, scale=wt[:, g, t : t + 1])
            else:
                nc.vector.tensor_scalar(out=dst, in0=src, scalar1=wt[:, g, t : t + 1], scalar2=None, op0=MULT)

        def do_diag(h, i):
            g, t = token_slot(h, i)
            diag[h, i] = keep.tile([P, P], BF16, align_bytes=64, name=f"diag{h}_{i}")
            nc.scalar.activation(out=diag[h, i][:], in_=ident[:], func=COPY, scale=wt[:, g, t : t + 1])

        def do_aw(h, i, bank):
            g, t = token_slot(h, i)
            aw[h, i] = psum.tile([P, A], F32, name="aw", tag=f"bank{bank}")
            nc.tensor.matmul(aw[h, i][:], lhsT=diag[h, i][:], rhs=act[g][:, t, :], start=True, stop=True)

        def do_aw_pool(h, slot):
            tile = one.tile([P, 2, A], F32, align_bytes=64, name="aw_pool", tag=slot)
            for i in range(2):
                g, t = token_slot(h, i)
                nc.gpsimd.tensor_scalar(
                    out=tile[:, i, :], in0=act[g][:, t, :], scalar1=wt[:, g, t : t + 1], scalar2=0.0,
                    op0=MULT, op1=ADD,
                )
                aw[h, i] = tile[:, i, :]

        def do_residual(h, i, f, lo=0, hi=HALF):
            g, t = token_slot(h, i)
            nc.vector.scalar_tensor_tensor(
                out=plane_tile(g, f)[:, t, lo:hi], in0=sig[h][:, i * A + f * HALF + lo : i * A + f * HALF + hi],
                scalar=wt[:, g, t : t + 1], in1=aw[h, i][:, f * HALF + lo : f * HALF + hi], op0=MULT, op1=SUB,
            )

        def do_weigh_late(g, engine):
            for h in (2 * g, 2 * g + 1):
                for i in range(2):
                    do_weigh(h, i, 1, engine)

        def do_weigh_pair(g, i, engine, lo=0, hi=HALF):
            for h in (2 * g, 2 * g + 1):
                do_weigh(h, i, 1, engine, lo, hi)

        def do_diff_rest(g):
            for h in (2 * g, 2 * g + 1):
                do_diff(h, "vector", POOL_COLS, 2 * A)

        def interleave(engine, dst, rows):
            if engine == "gpsimd":
                nc.gpsimd.tensor_scalar(
                    out=dst, in0=rows.rearrange("p t a -> p a t"), scalar1=1.0, scalar2=0.0, op0=MULT, op1=ADD
                )
                return
            copy = nc.vector.tensor_copy if engine == "vector" else nc.scalar.copy
            copy(out=dst.rearrange("p (c i) t -> p c t i", i=4), in_=rows.rearrange("p t (c i) -> p c t i", i=4))

        def do_interleave(g, f, engine, lo=0, hi=HALF):
            if (g, f) not in gi:
                gi[g, f] = one.tile([P, HALF, 4], BF16, align_bytes=64, name="gi", bufs=GI_BUFS)
            interleave(engine, gi[g, f][:, lo:hi, :], planes[g, f][:, :, lo:hi])

        def do_weigh_turn(g, f, lo=0, hi=HALF):
            if (g, f) not in gi:
                gi[g, f] = one.tile([P, HALF, 4], BF16, align_bytes=64, name="gi", bufs=GI_BUFS)
            rows = diff_g[g][:].rearrange("p (t a) -> p t a", t=4)
            nc.vector.tensor_tensor(
                out=gi[g, f][:, lo:hi, :].rearrange("p (c i) t -> p c t i", i=4),
                in0=rows[:, :, f * HALF + lo : f * HALF + hi].rearrange("p t (c i) -> p c t i", i=4),
                in1=wt[:, g, :].unsqueeze(1).unsqueeze(3).to_broadcast([P, (hi - lo) // 4, 4, 4]),
                op=MULT,
            )

        def do_quant_g(g, f, lo=0, hi=HALF):
            cols = slice(f * HALF + lo, f * HALF + hi)
            nc.vector.quantize_mx(
                out=g_codes[g][:, cols].bitcast(FP8X4), scales=g_scales[g][:, cols],
                in_=gi[g, f][:, lo:hi, :].rearrange("p a t -> p (a t)"),
            )

        def do_out(b, g):
            lo, width, tiles, bank = PIECES[b]
            cols = slice(lo, lo + width)
            closing = GROUPS - 1 if lo < HALF + QUARTER else GROUPS - 2
            if g == 0:
                accs[b] = psum.tile([P, len(tiles), width], F32, name="acc", tag=f"bank{bank}")
            for s, m in enumerate(tiles):
                nc.tensor.matmul_mx(
                    out=accs[b][:, s, :],
                    lhsT=hw[g][:, 2 * P * m : 2 * P * (m + 1)].bitcast(FP4X4),
                    lhsT_scale=hs[:, g, 32 * m : 32 * (m + 1)].bitcast(U8),
                    rhs=g_codes[g][:, cols].bitcast(FP8X4),
                    rhs_scale=g_scales[g][:, cols],
                    start=(g == 0 and s == 0),
                    stop=(g == closing and s == len(tiles) - 1),
                )

        def do_store(b, engine):
            lo, width, tiles, bank = PIECES[b]
            if b // 2 not in pairs:
                pairs[b // 2] = one.tile([P, 2 * A], F32, align_bytes=64, name="res", tag="cast", bufs=CAST_BUFS)
            at = (b % 2) * A
            res = pairs[b // 2][:, at : at + len(tiles) * width].rearrange("p (s n) -> p s n", n=width)
            if engine == "scalar":
                nc.scalar.copy(out=res, in_=accs[b][:])
            else:
                nc.vector.tensor_copy(out=res, in_=accs[b][:])
            rows = out[tiles[0] * P : (tiles[-1] + 1) * P, lo : lo + width]
            nc.sync.dma_start(out=rows.rearrange("(s p) n -> p s n", p=P), in_=res)

        def do_w_interleave(c, engine, lo, hi):
            interleave(engine, w_int[c][:, lo:hi, :], w_raw[c][:, :, lo:hi])

        def do_quant_w(c):
            nc.vector.quantize_mx(
                out=w_codes[c][:].bitcast(FP8X4), scales=w_scales[c][:],
                in_=w_int[c][:].rearrange("p n j -> p (n j)"),
            )

        last = GROUPS - 1
        end = STEPS - 1

        nc.vector.memset(ident[:], 0.0)
        nc.vector.memset(zeros[:], 0.0)
        nc.vector.memset(hs[:], 0)
        make_identity(nc, ident[:], nomemset=True)
        nc.scalar.activation(out=warm[:], in_=zeros[:, :1], func=SIGMOID)
        idle = psum.tile([P, A], F32, name="idle", tag="bank7")
        for k in range(WARM):
            nc.tensor.matmul(idle[:], lhsT=zeros[:, :P], rhs=zeros[:], start=True, stop=True)

        load_x(0)
        load_x_scale()
        load_x(1)
        load_w(0)
        load_weight()
        load_w(1)
        load_x(2)
        load_act(GROUPS - 1, 2, 4)
        load_x(3)
        load_act(0, 0, 2)
        load_x(4)
        load_x(5)
        load_act(0, 2, 4)
        load_x(6)
        load_act(1)
        load_h_scales()
        for g in range(GROUPS):
            load_h(g)
            for h in range(2 * g + 7, min(2 * g + 9, STEPS)):
                load_x(h)
            if g + 2 < GROUPS:
                load_act(g + 2, 0, 4 if g + 2 < GROUPS - 1 else 2)

        def turn_bank(h, c):
            return c + (EARLY_BANKS[h % 3] if h < EARLY_STEPS else 0)

        for c in range(X_PASSES):
            do_cast(0, "vector", c * K_PASS, (c + 1) * K_PASS)
            do_cast(0, "scalar", D + c * K_PASS, D + (c + 1) * K_PASS)
        for c in range(X_PASSES):
            do_turn(0, c, turn_bank(0, c))
        do_cast(1)
        do_w_interleave(0, "gpsimd", 0, W_POOL)
        do_w_interleave(0, "scalar", W_POOL, A)
        do_w_interleave(1, "scalar", W_OWN, A)
        nc.scalar.copy(out=wt[:], in_=wt_raw[:])
        for c in range(X_PASSES):
            do_scale(0, c)
            do_turn(1, c, turn_bank(1, c))
        do_cast(2)
        do_quant_x(0, 0)
        do_quant_w(0)
        do_w_interleave(1, "vector", 0, W_OWN)
        do_quant_x(0, 1)
        do_quant_w(1)
        do_aw_pool(STEPS - 1, "w_int1")
        for c in range(X_PASSES):
            for i in range(2):
                do_z(0, i, 2 + i, (c,))
        for c in range(X_PASSES):
            do_turn(2, c, turn_bank(2, c))
        do_cast(3)
        for i in range(2):
            do_sigmoid(0, i)
        for c in range(X_PASSES):
            do_scale(1, c)
        do_cast(4)
        do_cast_halves([2 * HEAD_CASTS])
        do_quant_x(1, 0)
        do_quant_x(1, 1)

        halves = list(range(2 * HEAD_CASTS + 1, 2 * STEPS))
        for h in range(STEADY, STEPS):
            do_diff(h - 2, "gpsimd", 0, POOL_COLS)
            do_z(h - 1, 0, 2)
            do_sigmoid(h - 1, 0)
            if h == STEADY:
                do_cast_halves([halves.pop(0)])
            if h == STEADY + 1:
                for i in range(2):
                    do_diag(STEPS - 2, i)
            if h < FIRST_OUT:
                do_turn(h + 1, 0, turn_bank(h + 1, 0))
            do_z(h - 1, 1, 3)
            do_sigmoid(h - 1, 1)
            pieces = []
            if h >= FIRST_OUT:
                pieces = [0, 1] if h % 2 == 1 else [2, 3]
            if h == end:
                pieces = [0, 1]
            for b in pieces:
                do_out(b, (h - FIRST_OUT) // 2)
            do_scale(h, 0)
            if FIRST_OUT <= h < end:
                do_turn(h + 1, 0, turn_bank(h + 1, 0))
            if h == end:
                do_aw(end - 1, 0, 0)
            do_scale(h, 1)
            if h < end:
                do_turn(h + 1, 1, turn_bank(h + 1, 1))
            if h == end:
                do_interleave(0, 1, "scalar")
                break
            both = h % 2 == 0 and h > STEADY
            if h < end - 1:
                for i in (1, 0) if both else (1,):
                    do_weigh(h - 2, i, 0, "scalar")
            count = 1 if h % 2 == 1 else 2
            do_cast_halves(halves[:count])
            halves = halves[count:]
            if h - 2 < DEFER_FROM:
                do_diff(h - 2, "vector", POOL_COLS, 2 * A)
            if h % 2 == 0 and h >= 4:
                do_quant_g((h - 4) // 2, 0)
            do_quant_x(h, 0)
            if h < end - 1 and not both:
                do_weigh(h - 2, 0, 0, "vector")
            do_quant_x(h, 1)
            if h % 2 == 1:
                do_interleave((h - 3) // 2, 0, "scalar")
            if h == end - 1:
                do_weigh_late(0, "scalar")

        do_aw(end - 1, 1, 1)
        for c in range(X_PASSES):
            do_quant_x(end, c)
        for i in range(2):
            do_weigh_pair(1, i, "scalar", 0, QUARTER)
        for f in range(2):
            do_z_half(end, f, 2 + f)
            do_sigmoid_half(end, f)
        do_weigh_turn(last - 1, 0)
        do_quant_g(0, 1)
        do_quant_g(last - 1, 0)
        for h in (end - 1, end):
            for i in range(2):
                do_residual(h, i, 0)
        do_interleave(1, 1, "scalar", 0, QUARTER)
        for i in range(2):
            do_residual(end - 1, i, 1)
        do_interleave(last, 0, "scalar", 0, LAST_SPLIT)
        do_interleave(last, 0, "vector", LAST_SPLIT, HALF)
        do_quant_g(1, 1, 0, QUARTER)
        do_diff_rest(3)
        do_quant_g(last, 0)
        for b in (2, 3):
            do_out(b, last - 2)
        do_out(6, 0)
        for b in range(4):
            do_out(b, last - 1)
        for b in (7, 4, 5):
            do_out(b, 0)
        for b in (4, 5):
            do_out(b, 1)
        for b in range(4):
            do_out(b, last)
        for i in range(2):
            do_weigh_pair(3, i, "scalar")
        do_interleave(3, 1, "scalar", 0, QUARTER)
        for b in range(4):
            do_store(b, "scalar")
        do_weigh_turn(2, 1, 0, QUARTER)
        do_weigh_turn(4, 1, 0, QUARTER)
        do_quant_g(2, 1, 0, QUARTER)
        do_residual(end, 0, 1)
        do_quant_g(4, 1, 0, QUARTER)
        do_residual(end, 1, 1)
        do_quant_g(3, 1, 0, QUARTER)
        do_diff(2, "vector", POOL_COLS, 2 * A)
        do_interleave(last, 1, "vector", 0, QUARTER)
        do_diff(3, "vector", POOL_COLS, 2 * A)
        do_diff(4, "vector", POOL_COLS, 2 * A)
        do_quant_g(last, 1, 0, QUARTER)
        do_weigh_turn(1, 1, QUARTER, HALF)
        for h in (5, 8):
            do_diff(h, "vector", POOL_COLS, 2 * A)
        do_quant_g(1, 1, QUARTER, HALF)
        do_weigh_turn(2, 1, QUARTER, HALF)
        for g in (last, 3):
            do_interleave(g, 1, "scalar", QUARTER, HALF)
        do_quant_g(last, 1, QUARTER, HALF)
        do_diff(9, "vector", POOL_COLS, 2 * A)
        do_quant_g(2, 1, QUARTER, HALF)
        do_weigh_turn(4, 1, QUARTER, HALF)
        for g in (3, 4):
            do_quant_g(g, 1, QUARTER, HALF)
        for g in (2, 4):
            for b in (4, 5):
                do_out(b, g)
        do_out(8, 0)
        for g in (3, last):
            for b in (4, 5):
                do_out(b, g)
        do_store(4, "scalar")
        do_store(5, "scalar")
        do_out(9, 0)
        for g in (1, 5, 2):
            for b in range(6, len(PIECES)):
                do_out(b, g)
        for b in range(6, len(PIECES)):
            for g in (3, 4):
                do_out(b, g)
            do_store(b, "vector" if b % 2 == 0 else "scalar")
